import numpy as np
import ml_dtypes


def mxq(x, axis, fmt="e4m3"):
    dtype, down = {"e4m3": (ml_dtypes.float8_e4m3fn, 7), "e5m2": (ml_dtypes.float8_e5m2, 14)}[fmt]
    v = np.moveaxis(np.asarray(x, np.float32).astype(ml_dtypes.bfloat16).astype(np.float64), axis, -1)
    blocks = v.reshape(v.shape[:-1] + (-1, 32))
    amax = np.abs(blocks).max(-1, keepdims=True)
    byte = np.maximum(np.where(amax > 0, np.frexp(amax)[1] - 1 + 127, 0) - down, 1)
    scale = np.exp2(byte - 127.0)
    codes = (blocks / scale).astype(np.float32).astype(dtype).astype(np.float64)
    return np.moveaxis((codes * scale).reshape(v.shape), -1, axis)


WIDE = False


def mx_kscale(k):
    if not WIDE:
        return np.ones(k)
    levels = np.array([10, -10, 5, -5, 0])
    if k % 512:
        return np.exp2(np.random.permutation(np.resize(levels, k // 32))).repeat(32)
    a = np.empty((k // 512, 16))
    for p in range(k // 512):
        a[p, :8] = np.random.permutation(np.resize(levels, 8))
        for g in range(8):
            far = levels[np.abs(levels - a[p, g]) >= 10]
            a[p, g + 8] = far[np.random.randint(len(far))]
    return np.exp2(a.ravel()).repeat(32)


def f64(x):
    return np.asarray(x).astype(np.float64)


def striped(idx):
    return np.tile(idx.reshape(-1, 16).T, (8, 1)).astype(np.uint16)


def unstriped(offs):
    return offs[:16].T.reshape(-1).astype(np.int64)


E2M1 = np.array([0.0, 0.5, 1.0, 1.5, 2.0, 3.0, 4.0, 6.0, -0.0, -0.5, -1.0, -1.5, -2.0, -3.0, -4.0, -6.0])


def pack_weight(w, fmt):
    k, n = w.shape
    w = f64(np.asarray(w, np.float32).astype(ml_dtypes.bfloat16)).reshape(k // 32, 32, n)
    amax = np.abs(w).max(1)
    if fmt == "e4m3":
        byte = np.frexp(amax)[1] - 1 + 127 - 7
    else:
        mant, ex = np.frexp(amax / 6.0)
        byte = np.where(mant > 0.5, ex, ex - 1) + 127
    byte = np.clip(np.where(amax > 0, byte, 1), 1, 254)
    scaled = (w * np.exp2(127.0 - byte)[:, None, :]).reshape(k, n).astype(np.float32)
    by_word = np.ascontiguousarray(scaled.reshape(k // 512, 128, 4, n).transpose(0, 1, 3, 2))
    if fmt == "e4m3":
        words = by_word.astype(ml_dtypes.float8_e4m3fn).view(np.uint8)
    else:
        c = by_word.astype(ml_dtypes.float4_e2m1fn).view(np.uint8) & 0xF
        words = (c[..., 0::2] | (c[..., 1::2] << 4)).reshape(k // 512, 128, 2 * n)
    return np.ascontiguousarray(words), np.ascontiguousarray(byte.astype(np.uint8).reshape(k // 512, 16, n))


def unpack_weight(words, scales, fmt):
    g, _, n = scales.shape
    words = np.ascontiguousarray(words).reshape(g, 128, n, -1)
    if fmt == "e4m3":
        vals = words.view(ml_dtypes.float8_e4m3fn).astype(np.float64)
    else:
        nib = np.empty((g, 128, n, 4), np.uint8)
        nib[..., 0::2] = words & 0xF
        nib[..., 1::2] = words >> 4
        vals = E2M1[nib]
    vals = vals * np.repeat(np.exp2(scales.astype(np.float64) - 127.0), 8, axis=1)[..., None]
    return vals.transpose(0, 1, 3, 2).reshape(g * 512, n)


def gelu(v):
    return 0.5 * v * (1.0 + np.tanh(np.sqrt(2.0 / np.pi) * (v + 0.044715 * v**3)))


K, H, T, S, T2, S2 = 1536, 512, 2048, 1024, 4096, 1024

def setup_inputs():
    n = np.random.standard_normal
    s = mx_kscale(K)[:, None]
    u = mx_kscale(H)[:, None]
    tab_words, tab_scales = pack_weight(n((K, T)) * s, "e4m3")
    tab2_words, tab2_scales = pack_weight(n((H, T2)) * H ** -0.5 / u, "e4m3")
    w1 = n((K, H)) * K ** -0.5 / s * u.T
    w4_words, w4_scales = pack_weight(n((K, H)) * K ** -0.5 / s, "e2m1")
    return {
        "tab_words": tab_words, "tab_scales": tab_scales,
        "offs": striped(np.random.permutation(T)[:S]),
        "tab2_words": tab2_words, "tab2_scales": tab2_scales,
        "offs2": striped(np.random.permutation(T2)[:S2]),
        "w1": w1.astype(np.float32),
        "w4_words": w4_words, "w4_scales": w4_scales,
        "alpha": n(S2).astype(np.float32),
    }

def reference(tab_words, tab_scales, offs, tab2_words, tab2_scales, offs2, w1, w4_words, w4_scales, alpha):
    v = unpack_weight(tab_words, tab_scales, "e4m3")[:, unstriped(offs)]
    v2 = unpack_weight(tab2_words, tab2_scales, "e4m3")[:, unstriped(offs2)]
    w4 = unpack_weight(w4_words, w4_scales, "e2m1")
    a = mxq(f64(w1), 0, "e4m3").T @ v
    g = w4.T @ v
    h = a / (1.0 + np.exp(-g))
    y = v2.T @ mxq(h, 0, "e4m3")
    return f64(alpha)[:, None] * np.square(y + 1.0)

@@ -1,0 +1,276 @@
+from contextlib import ExitStack
+
+import concourse.mybir as mybir
+from concourse.masks import make_identity
+
+K, H, T, S, T2, S2 = 1536, 512, 2048, 1024, 4096, 1024
+FLOPS = 2 * (2 * K * H * S + H * S * S2)
+
+F32 = mybir.dt.float32
+BF16 = mybir.dt.bfloat16
+I32 = mybir.dt.int32
+U32 = mybir.dt.uint32
+U16 = mybir.dt.uint16
+U8 = mybir.dt.uint8
+FP8X4 = mybir.dt.float8_e4m3fn_x4
+FP4X4 = mybir.dt.float4_e2m1fn_x4
+ACT = mybir.ActivationFunctionType
+MULT = mybir.AluOpType.mult
+
+P = 128
+PASSES = K // 512
+HALF = 512
+CHUNKS = S // P
+SHIFT_ROWS = 112
+
+
+def tile_list_poly_kernel_contributions_kernel(
+    tc, tab_words, tab_scales, offs, tab2_words, tab2_scales, offs2, w1, w4_words, w4_scales, alpha, out
+):
+    nc = tc.nc
+    with ExitStack() as ctx:
+        keep = ctx.enter_context(tc.tile_pool(name="keep", bufs=1))
+        psum = ctx.enter_context(tc.psum_pool(name="psum", bufs=1))
+
+        def sb(name, shape, dtype, tag=None):
+            return keep.tile(shape, dtype, name=name, tag=tag or name, align_bytes=64)
+
+        idx = keep.tile([P, S // 16], U16, name="idx")
+        idx2 = keep.tile([P, S2 // 16], U16, name="idx2")
+        tabw = [sb("tabw%d" % a, [P, T], U32) for a in range(PASSES)]
+        tabs = sb("tabs", [P, T], U8)
+        tab2w = sb("tab2w", [P, T2], U32)
+        tab2s = sb("tab2s", [P, T2], U8)
+        w1raw = [sb("w1raw%d" % a, [P, 4, H], F32) for a in range(PASSES)]
+        w1bf = [sb("w1bf%d" % a, [P, H, 4], BF16) for a in range(PASSES)]
+        w1c = [sb("w1c%d" % a, [P, H], U32) for a in range(PASSES)]
+        w1s = [sb("w1s%d" % a, [P, H], U8) for a in range(PASSES)]
+        w4w = sb("w4w", [P, PASSES, 2 * H], U8)
+        w4s = sb("w4s", [P, PASSES, H], U8)
+        vw = {}
+        vs = [sb("vs%d" % a, [P, S], U8) for a in range(PASSES)]
+        v2w = {}
+        v2s = [sb("v2s%d" % b, [P, HALF], U8) for b in range(2)]
+        arow = sb("arow", [P, P], F32)
+        acol = sb("acol", [P, S2 // P], F32)
+        ident = sb("ident", [P, P], F32)
+        warm = sb("warm", [P, 1], F32)
+        sig = [sb("sig%d" % c, [P, H], F32) for c in range(CHUNKS)]
+        hT = [sb("hT%d" % c, [P, H], BF16) for c in range(CHUNKS)]
+        hin = [sb("hin%d" % b, [P, HALF, 4], BF16) for b in range(2)]
+        hc = [sb("hc%d" % b, [P, HALF], U32) for b in range(2)]
+        hs = [sb("hs%d" % b, [P, HALF], U8) for b in range(2)]
+        sq = [sb("sq%d" % n, [P, HALF], F32) for n in range(16)]
+        res = [sb("res%d" % n, [P, HALF], F32) for n in range(16)]
+        banks = [psum.tile([P, 512], F32, name="bank%d" % b) for b in range(8)]
+
+        nc.vector.memset(tabs[:].bitcast(I32), 0)
+        nc.vector.memset(w4s[:].rearrange("p a c -> p (a c)").bitcast(I32), 0)
+        nc.vector.memset(tab2s[:].bitcast(I32), 0)
+        nc.vector.memset(arow[:], 0.0)
+        for a in (1, 2):
+            nc.vector.memset(vs[a][:].bitcast(I32), 0)
+        nc.scalar.activation(out=warm[:], in_=arow[:, 0:1], func=ACT.Sigmoid)
+
+        def load_tab(a):
+            nc.sync.dma_start(
+                out=tabw[a][:].bitcast(I32), in_=tab_words[a].rearrange("p t i -> p (t i)").bitcast(I32)
+            )
+
+        def load_w1(a):
+            nc.sync.dma_start(
+                out=w1raw[a][:], in_=w1[512 * a : 512 * (a + 1), :].rearrange("(p j) c -> p j c", j=4)
+            )
+
+        nc.sync.dma_start(idx[:], offs)
+        load_tab(0)
+        nc.sync.dma_start(out=w4w[:].bitcast(I32), in_=w4_words.bitcast(I32).rearrange("a p c -> p a c"))
+        nc.sync.dma_start(idx2[:], offs2)
+        load_w1(0)
+        load_tab(1)
+        load_w1(1)
+        load_tab(2)
+        load_w1(2)
+        nc.sync.dma_start(
+            out=tab2w[:].bitcast(I32), in_=tab2_words[0].rearrange("p t i -> p (t i)").bitcast(I32)
+        )
+
+        for q in range(4):
+            nc.gpsimd.dma_start(
+                out=tabs[32 * q : 32 * q + 4 * PASSES, :].bitcast(I32),
+                in_=tab_scales[:, 4 * q : 4 * q + 4, :].bitcast(I32),
+            )
+        for q in range(4):
+            nc.gpsimd.dma_start(
+                out=w4s[32 * q : 32 * q + 4, :, :].bitcast(I32),
+                in_=w4_scales[:, 4 * q : 4 * q + 4, :].bitcast(I32).rearrange("a r c -> r a c"),
+            )
+        for q in range(4):
+            nc.gpsimd.dma_start(
+                out=tab2s[32 * q + 12 : 32 * q + 16, :].bitcast(I32),
+                in_=tab2_scales[0, 4 * q : 4 * q + 4, :].bitcast(I32),
+            )
+        nc.gpsimd.dma_start(out=arow[0 : S2 // P, :], in_=alpha.rearrange("(n p) -> n p", p=P))
+        make_identity(nc, ident[:])
+
+        def half_list(lst, b):
+            return lst[:, 32 * b : 32 * (b + 1)]
+
+        def gather_tab(a, b):
+            vw[a, b] = sb("vw%d_%d" % (a, b), [P, HALF], U32, "tabs" if (a, b) == (1, 0) else None)
+            nc.vector.tensor_copy(out=vw[a, b][:], in_=tabw[a][:].indirect(half_list(idx, b)))
+
+        def gather_tab_scales():
+            nc.vector.tensor_copy(out=vs[0][:], in_=tabs[:].indirect(idx[:]))
+            for a in (1, 2):
+                nc.scalar.dma_start(
+                    out=vs[a][0:SHIFT_ROWS, :].bitcast(I32),
+                    in_=vs[0][4 * a : 4 * a + SHIFT_ROWS, :].bitcast(I32),
+                )
+
+        def interleave_w1(a, on_vector):
+            dst = w1bf[a][:].rearrange("p (c i) t -> p c t i", i=4)
+            src = w1raw[a][:].rearrange("p t (c i) -> p c t i", i=4)
+            if on_vector:
+                nc.vector.tensor_copy(out=dst, in_=src)
+            else:
+                nc.scalar.copy(out=dst, in_=src)
+
+        def quant_w1(a):
+            nc.vector.quantize_mx(
+                out=w1c[a][:].bitcast(FP8X4), scales=w1s[a][:], in_=w1bf[a][:].rearrange("p c t -> p (c t)")
+            )
+
+        def stationary(a, c):
+            b, o = divmod(c, 4)
+            return vw[a, b][:, o * P : (o + 1) * P].bitcast(FP8X4), vs[a][:, c * P : (c + 1) * P]
+
+        def mm_g(c, a):
+            codes, scales = stationary(a, c)
+            nc.tensor.matmul_mx(
+                out=banks[c % 4][:], lhsT=codes, lhsT_scale=scales,
+                rhs=w4w[:, a, :].bitcast(FP4X4), rhs_scale=w4s[:, a, :],
+                start=(a == 0), stop=(a == PASSES - 1),
+            )
+
+        def mm_a(c, a):
+            codes, scales = stationary(a, c)
+            nc.tensor.matmul_mx(
+                out=banks[4 + c % 4][:], lhsT=codes, lhsT_scale=scales,
+                rhs=w1c[a][:].bitcast(FP8X4), rhs_scale=w1s[a][:],
+                start=(a == 0), stop=(a == PASSES - 1),
+            )
+
+        def sigmoid(c):
+            nc.scalar.activation(
+                out=sig[c][:].rearrange("j (u p e) -> j u p e", u=2, e=2),
+                in_=banks[c % 4][:].rearrange("j (p u e) -> j u p e", u=2, e=2),
+                func=ACT.Sigmoid,
+            )
+
+        def gate(c):
+            nc.vector.tensor_tensor(
+                out=hT[c][:].rearrange("j (u p e) -> j u p e", u=2, e=2),
+                in0=banks[4 + c % 4][:].rearrange("j (p u e) -> j u p e", u=2, e=2),
+                in1=sig[c][:].rearrange("j (u p e) -> j u p e", u=2, e=2),
+                op=MULT,
+            )
+
+        def turn(pair):
+            bank = banks[pair % 2]
+            for cc in range(2):
+                words = hT[2 * pair + cc][:].bitcast(F32)
+                for u in range(2):
+                    o = u * 256 + cc * P
+                    nc.tensor.transpose(bank[:, o : o + P], words[:, u * P : (u + 1) * P], ident[:])
+            b, o = divmod(pair, 2)
+            dst = hin[b][:, o * 256 : (o + 1) * 256, :].rearrange("p n t -> p (n t)").bitcast(F32)
+            nc.scalar.copy(
+                out=dst.rearrange("p (n u) -> p n u", u=2),
+                in_=bank[:].rearrange("p (u n) -> p n u", u=2),
+            )
+
+        def quant_h(b):
+            nc.vector.quantize_mx(
+                out=hc[b][:].bitcast(FP8X4), scales=hs[b][:], in_=hin[b][:].rearrange("p n t -> p (n t)")
+            )
+
+        def gather_tab2_scales(b):
+            nc.vector.tensor_copy(out=v2s[b][:], in_=tab2s[:].indirect(half_list(idx2, b)))
+
+        def gather_tab2(b):
+            v2w[b] = sb("v2w%d" % b, [P, HALF], U32, "sig%d" % (3, 5)[b])
+            nc.vector.tensor_copy(out=v2w[b][:], in_=tab2w[:].indirect(half_list(idx2, b)))
+
+        y_banks = [2, 3, 2, 3, 4, 5, 6, 7, 2, 3, 0, 1, 4, 5, 6, 7]
+
+        def result(n):
+            jb, i = divmod(n, 8)
+            b, o = divmod(i, 4)
+            bank = banks[y_banks[n]]
+            nc.tensor.matmul_mx(
+                out=bank[:], lhsT=v2w[b][:, o * P : (o + 1) * P].bitcast(FP8X4),
+                lhsT_scale=v2s[b][12:P, o * P : (o + 1) * P],
+                rhs=hc[jb][:].bitcast(FP8X4), rhs_scale=hs[jb][:], start=True, stop=True,
+            )
+            nc.scalar.activation(out=sq[n][:], in_=bank[:], func=ACT.Square, bias=1.0)
+            nc.vector.tensor_scalar(
+                out=res[n][:], in0=sq[n][:], scalar1=acol[:, i : i + 1], scalar2=None, op0=MULT
+            )
+            nc.sync.dma_start(out=out[i * P : (i + 1) * P, jb * HALF : (jb + 1) * HALF], in_=res[n][:])
+
+        nc.tensor.transpose(banks[7][:, 0:P], arow[:], ident[:])
+        nc.scalar.copy(out=acol[:], in_=banks[7][:, 0 : S2 // P])
+
+        gather_tab(0, 0)
+        gather_tab_scales()
+        interleave_w1(0, False)
+        for c in range(4):
+            mm_g(c, 0)
+        gather_tab(0, 1)
+        gather_tab(1, 0)
+        quant_w1(0)
+        interleave_w1(1, False)
+        for c in range(4):
+            mm_g(c, 1)
+        for c in range(4):
+            mm_a(c, 0)
+        gather_tab(1, 1)
+        quant_w1(1)
+        for c in range(4):
+            mm_a(c, 1)
+        gather_tab2_scales(0)
+        gather_tab(2, 0)
+        gather_tab(2, 1)
+        for c in range(4):
+            mm_g(c, 2)
+            sigmoid(c)
+        interleave_w1(2, True)
+        quant_w1(2)
+        gather_tab2_scales(1)
+        for c in range(4, 6):
+            for a in range(PASSES):
+                mm_g(c, a)
+            sigmoid(c)
+        for c in range(4):
+            mm_a(c, 2)
+            gate(c)
+        for c in range(6, 8):
+            for a in range(PASSES):
+                mm_g(c, a)
+            sigmoid(c)
+        turn(0)
+        turn(1)
+        quant_h(0)
+        gather_tab2(0)
+        for c in range(4, 8):
+            for a in range(PASSES):
+                mm_a(c, a)
+            gate(c)
+            result(c - 4)
+        gather_tab2(1)
+        turn(2)
+        turn(3)
+        quant_h(1)
+        for n in range(4, 16):
+            result(n)

@@ -18,10 +18,25 @@ ACT = mybir.ActivationFunctionType
 MULT = mybir.AluOpType.mult
 
 P = 128
-PASSES = K // 512
+PACK = 4
+K_PASS = P * PACK
+PASSES = K // K_PASS
 HALF = 512
 CHUNKS = S // P
+PER_HALF = HALF // P
+ROW_TILES = S2 // P
+QUADRANT = 32
 SHIFT_ROWS = 112
+TAB2_PLANE = 12
+
+A_BANK = [0, 1, 2, 3, 0, 1, 2, 3]
+TURN_BANK = [4, 5, 4, 5]
+ALPHA_BANK = 6
+Y_BANK = [6, 7, 6, 7, 0, 1, 6, 7, 2, 3, 0, 1, 6, 7, 4, 5]
+
+W1_LAST_AT = 0
+W1_FIRST_AT = 4096
+TAB2_AT = 8192
 
 
 def tile_list_poly_kernel_contributions_kernel(
@@ -30,247 +45,240 @@ def tile_list_poly_kernel_contributions_kernel(
     nc = tc.nc
     with ExitStack() as ctx:
         keep = ctx.enter_context(tc.tile_pool(name="keep", bufs=1))
+        shared = ctx.enter_context(tc.tile_pool(name="shared", bufs=1))
         psum = ctx.enter_context(tc.psum_pool(name="psum", bufs=1))
 
-        def sb(name, shape, dtype, tag=None):
-            return keep.tile(shape, dtype, name=name, tag=tag or name, align_bytes=64)
+        def sbuf(name, shape, dtype, on=None):
+            return keep.tile(shape, dtype, name=name, tag=on or name, align_bytes=64)
+
+        def placed(name, shape, dtype, offset):
+            return shared.tile(shape, dtype, name=name, align_bytes=64, offset=offset)
 
         idx = keep.tile([P, S // 16], U16, name="idx")
         idx2 = keep.tile([P, S2 // 16], U16, name="idx2")
-        tabw = [sb("tabw%d" % a, [P, T], U32) for a in range(PASSES)]
-        tabs = sb("tabs", [P, T], U8)
-        tab2w = sb("tab2w", [P, T2], U32)
-        tab2s = sb("tab2s", [P, T2], U8)
-        w1raw = [sb("w1raw%d" % a, [P, 4, H], F32) for a in range(PASSES)]
-        w1bf = [sb("w1bf%d" % a, [P, H, 4], BF16) for a in range(PASSES)]
-        w1c = [sb("w1c%d" % a, [P, H], U32) for a in range(PASSES)]
-        w1s = [sb("w1s%d" % a, [P, H], U8) for a in range(PASSES)]
-        w4w = sb("w4w", [P, PASSES, 2 * H], U8)
-        w4s = sb("w4s", [P, PASSES, H], U8)
-        vw = {}
-        vs = [sb("vs%d" % a, [P, S], U8) for a in range(PASSES)]
-        v2w = {}
-        v2s = [sb("v2s%d" % b, [P, HALF], U8) for b in range(2)]
-        arow = sb("arow", [P, P], F32)
-        acol = sb("acol", [P, S2 // P], F32)
-        ident = sb("ident", [P, P], F32)
-        warm = sb("warm", [P, 1], F32)
-        sig = [sb("sig%d" % c, [P, H], F32) for c in range(CHUNKS)]
-        hT = [sb("hT%d" % c, [P, H], BF16) for c in range(CHUNKS)]
-        hin = [sb("hin%d" % b, [P, HALF, 4], BF16) for b in range(2)]
-        hc = [sb("hc%d" % b, [P, HALF], U32) for b in range(2)]
-        hs = [sb("hs%d" % b, [P, HALF], U8) for b in range(2)]
-        sq = [sb("sq%d" % n, [P, HALF], F32) for n in range(16)]
-        res = [sb("res%d" % n, [P, HALF], F32) for n in range(16)]
-        banks = [psum.tile([P, 512], F32, name="bank%d" % b) for b in range(8)]
+        tab_scale_window = sbuf("tab_scale_window", [P, T], U8)
+        tab2_scale_window = sbuf("tab2_scale_window", [P, T2], U8)
+        w1_bf16 = [sbuf("w1_bf16_%d" % a, [P, H, PACK], BF16) for a in range(PASSES)]
+        w1_plane = [sbuf("w1_plane%d" % a, [P, H], U8) for a in range(PASSES)]
+        w4_codes = sbuf("w4_codes", [P, PASSES, 2 * H], U8)
+        w4_plane = sbuf("w4_plane", [P, PASSES, H], U8)
+        v_plane = [sbuf("v_plane%d" % a, [P, S], U8) for a in range(PASSES)]
+        alpha_rows = sbuf("alpha_rows", [P, P], F32)
+        alpha_cols = sbuf("alpha_cols", [P, ROW_TILES], F32)
+        ident = sbuf("ident", [P, P], F32)
+        sig = [sbuf("sig%d" % c, [P, H], F32) for c in range(CHUNKS)]
+        h_turned = [sbuf("h_turned%d" % b, [P, HALF, PACK], BF16) for b in range(2)]
+        h_plane = [sbuf("h_plane%d" % b, [P, HALF], U8) for b in range(2)]
+        squared = [sbuf("squared%d" % n, [P, HALF], F32) for n in range(2 * ROW_TILES)]
+        result = [sbuf("result%d" % n, [P, HALF], F32) for n in range(2 * ROW_TILES)]
+        banks = [psum.tile([P, HALF], F32, name="bank%d" % b) for b in range(8)]
+        tab_window, tab2_window, w1_raw, w1_codes = {}, {}, {}, {}
+        v_codes, v2_codes, v2_plane, h_chunk, h_codes = {}, {}, {}, {}, {}
 
-        nc.vector.memset(tabs[:].bitcast(I32), 0)
-        nc.vector.memset(w4s[:].rearrange("p a c -> p (a c)").bitcast(I32), 0)
-        nc.vector.memset(tab2s[:].bitcast(I32), 0)
-        nc.vector.memset(arow[:], 0.0)
-        for a in (1, 2):
-            nc.vector.memset(vs[a][:].bitcast(I32), 0)
-        nc.scalar.activation(out=warm[:], in_=arow[:, 0:1], func=ACT.Sigmoid)
+        nc.vector.memset(tab_scale_window[:].bitcast(I32), 0)
+        nc.vector.memset(tab2_scale_window[:].bitcast(I32), 0)
+        nc.vector.memset(w4_plane[:].rearrange("p a c -> p (a c)").bitcast(I32), 0)
+        nc.vector.memset(alpha_rows[:], 0.0)
+        for a in range(1, PASSES):
+            nc.vector.memset(v_plane[a][:].bitcast(I32), 0)
 
-        def load_tab(a):
-            nc.sync.dma_start(
-                out=tabw[a][:].bitcast(I32), in_=tab_words[a].rearrange("p t i -> p (t i)").bitcast(I32)
-            )
+        def load_tab(a, on=None):
+            tab_window[a] = sbuf("tab_window%d" % a, [P, T], U32, on)
+            words = tab_words[a].rearrange("p t i -> p (t i)")
+            nc.sync.dma_start(out=tab_window[a][:].bitcast(I32), in_=words.bitcast(I32))
 
-        def load_w1(a):
-            nc.sync.dma_start(
-                out=w1raw[a][:], in_=w1[512 * a : 512 * (a + 1), :].rearrange("(p j) c -> p j c", j=4)
-            )
+        def load_w1(a, tile):
+            w1_raw[a] = tile
+            rows = w1[K_PASS * a : K_PASS * (a + 1), :]
+            nc.sync.dma_start(out=tile[:], in_=rows.rearrange("(p t) c -> p t c", t=PACK))
+
+        def load_tab2():
+            tab2_window[0] = placed("tab2_window", [P, T2], U32, TAB2_AT)
+            words = tab2_words[0].rearrange("p t i -> p (t i)")
+            nc.sync.dma_start(out=tab2_window[0][:].bitcast(I32), in_=words.bitcast(I32))
 
         nc.sync.dma_start(idx[:], offs)
         load_tab(0)
-        nc.sync.dma_start(out=w4w[:].bitcast(I32), in_=w4_words.bitcast(I32).rearrange("a p c -> p a c"))
-        nc.sync.dma_start(idx2[:], offs2)
-        load_w1(0)
-        load_tab(1)
-        load_w1(1)
-        load_tab(2)
-        load_w1(2)
-        nc.sync.dma_start(
-            out=tab2w[:].bitcast(I32), in_=tab2_words[0].rearrange("p t i -> p (t i)").bitcast(I32)
-        )
-
         for q in range(4):
-            nc.gpsimd.dma_start(
-                out=tabs[32 * q : 32 * q + 4 * PASSES, :].bitcast(I32),
+            nc.sync.dma_start(
+                out=tab_scale_window[QUADRANT * q : QUADRANT * q + 4 * PASSES, :].bitcast(I32),
                 in_=tab_scales[:, 4 * q : 4 * q + 4, :].bitcast(I32),
             )
-        for q in range(4):
-            nc.gpsimd.dma_start(
-                out=w4s[32 * q : 32 * q + 4, :, :].bitcast(I32),
-                in_=w4_scales[:, 4 * q : 4 * q + 4, :].bitcast(I32).rearrange("a r c -> r a c"),
+        nc.sync.dma_start(out=w4_codes[:].bitcast(I32), in_=w4_words.bitcast(I32).rearrange("a p c -> p a c"))
+        load_tab(1)
+        nc.sync.dma_start(idx2[:], offs2)
+        for s in range(4):
+            nc.sync.dma_start(
+                out=tab2_scale_window[TAB2_PLANE + s : P : QUADRANT, :].bitcast(I32),
+                in_=tab2_scales[0, s:16:4, :].bitcast(I32),
             )
-        for q in range(4):
-            nc.gpsimd.dma_start(
-                out=tab2s[32 * q + 12 : 32 * q + 16, :].bitcast(I32),
-                in_=tab2_scales[0, 4 * q : 4 * q + 4, :].bitcast(I32),
+        for s in range(4):
+            nc.sync.dma_start(
+                out=w4_plane[s:P:QUADRANT, :, :].bitcast(I32),
+                in_=w4_scales[:, s:16:4, :].bitcast(I32).rearrange("a q c -> q a c"),
             )
-        nc.gpsimd.dma_start(out=arow[0 : S2 // P, :], in_=alpha.rearrange("(n p) -> n p", p=P))
+        load_w1(0, placed("w1_raw0", [P, PACK, H], F32, W1_FIRST_AT))
+        nc.gpsimd.dma_start(out=alpha_rows[0:ROW_TILES, :], in_=alpha.rearrange("(n p) -> n p", p=P))
         make_identity(nc, ident[:])
 
-        def half_list(lst, b):
-            return lst[:, 32 * b : 32 * (b + 1)]
+        def half_of(offsets, b):
+            columns = HALF // 16
+            return offsets[:, columns * b : columns * (b + 1)]
 
         def gather_tab(a, b):
-            vw[a, b] = sb("vw%d_%d" % (a, b), [P, HALF], U32, "tabs" if (a, b) == (1, 0) else None)
-            nc.vector.tensor_copy(out=vw[a, b][:], in_=tabw[a][:].indirect(half_list(idx, b)))
+            v_codes[a, b] = sbuf("v_codes%d_%d" % (a, b), [P, HALF], U32)
+            nc.vector.tensor_copy(out=v_codes[a, b][:], in_=tab_window[a][:].indirect(half_of(idx, b)))
 
         def gather_tab_scales():
-            nc.vector.tensor_copy(out=vs[0][:], in_=tabs[:].indirect(idx[:]))
-            for a in (1, 2):
-                nc.scalar.dma_start(
-                    out=vs[a][0:SHIFT_ROWS, :].bitcast(I32),
-                    in_=vs[0][4 * a : 4 * a + SHIFT_ROWS, :].bitcast(I32),
+            nc.vector.tensor_copy(out=v_plane[0][:], in_=tab_scale_window[:].indirect(idx[:]))
+            for a in range(1, PASSES):
+                nc.sync.dma_start(
+                    out=v_plane[a][0:SHIFT_ROWS, :].bitcast(I32),
+                    in_=v_plane[0][4 * a : 4 * a + SHIFT_ROWS, :].bitcast(I32),
                 )
 
-        def interleave_w1(a, on_vector):
-            dst = w1bf[a][:].rearrange("p (c i) t -> p c t i", i=4)
-            src = w1raw[a][:].rearrange("p t (c i) -> p c t i", i=4)
-            if on_vector:
-                nc.vector.tensor_copy(out=dst, in_=src)
-            else:
-                nc.scalar.copy(out=dst, in_=src)
+        def gather_tab2_scales(b):
+            v2_plane[b] = sbuf("v2_plane%d" % b, [P, HALF], U8)
+            nc.vector.tensor_copy(out=v2_plane[b][:], in_=tab2_scale_window[:].indirect(half_of(idx2, b)))
 
-        def quant_w1(a):
+        def gather_tab2(b, on=None):
+            v2_codes[b] = sbuf("v2_codes%d" % b, [P, HALF], U32, on)
+            nc.vector.tensor_copy(out=v2_codes[b][:], in_=tab2_window[0][:].indirect(half_of(idx2, b)))
+
+        def interleave_w1_scalar(a):
+            nc.scalar.copy(
+                out=w1_bf16[a][:].rearrange("p (c i) t -> p c t i", i=4),
+                in_=w1_raw[a][:].rearrange("p t (c i) -> p c t i", i=4),
+            )
+
+        def interleave_w1_vector(a):
+            nc.vector.tensor_copy(out=w1_bf16[a][:], in_=w1_raw[a][:].rearrange("p t c -> p c t"))
+
+        def quantise_w1(a, on=None):
+            w1_codes[a] = sbuf("w1_codes%d" % a, [P, H], U32, on)
             nc.vector.quantize_mx(
-                out=w1c[a][:].bitcast(FP8X4), scales=w1s[a][:], in_=w1bf[a][:].rearrange("p c t -> p (c t)")
+                out=w1_codes[a][:].bitcast(FP8X4),
+                scales=w1_plane[a][:],
+                in_=w1_bf16[a][:].rearrange("p c t -> p (c t)"),
             )
 
-        def stationary(a, c):
-            b, o = divmod(c, 4)
-            return vw[a, b][:, o * P : (o + 1) * P].bitcast(FP8X4), vs[a][:, c * P : (c + 1) * P]
-
-        def mm_g(c, a):
-            codes, scales = stationary(a, c)
+        def project(bank, c, a, codes, plane):
+            b, o = divmod(c, PER_HALF)
             nc.tensor.matmul_mx(
-                out=banks[c % 4][:], lhsT=codes, lhsT_scale=scales,
-                rhs=w4w[:, a, :].bitcast(FP4X4), rhs_scale=w4s[:, a, :],
-                start=(a == 0), stop=(a == PASSES - 1),
+                out=bank[:],
+                lhsT=v_codes[a, b][:, o * P : (o + 1) * P].bitcast(FP8X4),
+                lhsT_scale=v_plane[a][:, c * P : (c + 1) * P],
+                rhs=codes,
+                rhs_scale=plane,
+                start=(a == 0),
+                stop=(a == PASSES - 1),
             )
 
-        def mm_a(c, a):
-            codes, scales = stationary(a, c)
-            nc.tensor.matmul_mx(
-                out=banks[4 + c % 4][:], lhsT=codes, lhsT_scale=scales,
-                rhs=w1c[a][:].bitcast(FP8X4), rhs_scale=w1s[a][:],
-                start=(a == 0), stop=(a == PASSES - 1),
-            )
+        def gate_pass(a):
+            for c in range(CHUNKS):
+                project(banks[c], c, a, w4_codes[:, a, :].bitcast(FP4X4), w4_plane[:, a, :])
+
+        def in_word_order(bank):
+            return bank[:].rearrange("j (p u e) -> j u p e", u=2, e=2)
+
+        def as_stored(tile):
+            return tile[:].rearrange("j (u p e) -> j u p e", u=2, e=2)
 
         def sigmoid(c):
-            nc.scalar.activation(
-                out=sig[c][:].rearrange("j (u p e) -> j u p e", u=2, e=2),
-                in_=banks[c % 4][:].rearrange("j (p u e) -> j u p e", u=2, e=2),
-                func=ACT.Sigmoid,
-            )
+            nc.scalar.activation(out=as_stored(sig[c]), in_=in_word_order(banks[c]), func=ACT.Sigmoid)
 
-        def gate(c):
-            nc.vector.tensor_tensor(
-                out=hT[c][:].rearrange("j (u p e) -> j u p e", u=2, e=2),
-                in0=banks[4 + c % 4][:].rearrange("j (p u e) -> j u p e", u=2, e=2),
-                in1=sig[c][:].rearrange("j (u p e) -> j u p e", u=2, e=2),
-                op=MULT,
-            )
+        def gated_chunk(c):
+            bank = banks[A_BANK[c]]
+            for a in range(PASSES):
+                project(bank, c, a, w1_codes[a][:].bitcast(FP8X4), w1_plane[a][:])
+            if c == PER_HALF:
+                h_chunk[c] = placed("h_chunk%d" % c, [P, H], BF16, TAB2_AT)
+            else:
+                h_chunk[c] = sbuf("h_chunk%d" % c, [P, H], BF16)
+            nc.vector.tensor_tensor(out=as_stored(h_chunk[c]), in0=in_word_order(bank), in1=as_stored(sig[c]), op=MULT)
 
-        def turn(pair):
-            bank = banks[pair % 2]
-            for cc in range(2):
-                words = hT[2 * pair + cc][:].bitcast(F32)
+        def turn(pair, copy):
+            bank = banks[TURN_BANK[pair]]
+            for second in range(2):
+                words = h_chunk[2 * pair + second][:].bitcast(F32)
                 for u in range(2):
-                    o = u * 256 + cc * P
+                    o = (2 * u + second) * P
                     nc.tensor.transpose(bank[:, o : o + P], words[:, u * P : (u + 1) * P], ident[:])
             b, o = divmod(pair, 2)
-            dst = hin[b][:, o * 256 : (o + 1) * 256, :].rearrange("p n t -> p (n t)").bitcast(F32)
-            nc.scalar.copy(
-                out=dst.rearrange("p (n u) -> p n u", u=2),
-                in_=bank[:].rearrange("p (u n) -> p n u", u=2),
-            )
+            samples = h_turned[b][:, o * 2 * P : (o + 1) * 2 * P, :].rearrange("p j t -> p (j t)").bitcast(F32)
+            copy(out=samples.rearrange("p (j u) -> p j u", u=2), in_=bank[:].rearrange("p (u j) -> p j u", u=2))
 
-        def quant_h(b):
+        def quantise_h(b):
+            h_codes[b] = sbuf("h_codes%d" % b, [P, HALF], U32)
             nc.vector.quantize_mx(
-                out=hc[b][:].bitcast(FP8X4), scales=hs[b][:], in_=hin[b][:].rearrange("p n t -> p (n t)")
+                out=h_codes[b][:].bitcast(FP8X4),
+                scales=h_plane[b][:],
+                in_=h_turned[b][:].rearrange("p j t -> p (j t)"),
             )
 
-        def gather_tab2_scales(b):
-            nc.vector.tensor_copy(out=v2s[b][:], in_=tab2s[:].indirect(half_list(idx2, b)))
-
-        def gather_tab2(b):
-            v2w[b] = sb("v2w%d" % b, [P, HALF], U32, "sig%d" % (3, 5)[b])
-            nc.vector.tensor_copy(out=v2w[b][:], in_=tab2w[:].indirect(half_list(idx2, b)))
-
-        y_banks = [2, 3, 2, 3, 4, 5, 6, 7, 2, 3, 0, 1, 4, 5, 6, 7]
-
-        def result(n):
-            jb, i = divmod(n, 8)
-            b, o = divmod(i, 4)
-            bank = banks[y_banks[n]]
+        def out_tile(n):
+            half, i = divmod(n, ROW_TILES)
+            b, o = divmod(i, PER_HALF)
+            bank = banks[Y_BANK[n]]
             nc.tensor.matmul_mx(
-                out=bank[:], lhsT=v2w[b][:, o * P : (o + 1) * P].bitcast(FP8X4),
-                lhsT_scale=v2s[b][12:P, o * P : (o + 1) * P],
-                rhs=hc[jb][:].bitcast(FP8X4), rhs_scale=hs[jb][:], start=True, stop=True,
+                out=bank[:],
+                lhsT=v2_codes[b][:, o * P : (o + 1) * P].bitcast(FP8X4),
+                lhsT_scale=v2_plane[b][TAB2_PLANE:P, o * P : (o + 1) * P],
+                rhs=h_codes[half][:].bitcast(FP8X4),
+                rhs_scale=h_plane[half][:],
+                start=True,
+                stop=True,
             )
-            nc.scalar.activation(out=sq[n][:], in_=bank[:], func=ACT.Square, bias=1.0)
+            nc.scalar.activation(out=squared[n][:], in_=bank[:], func=ACT.Square, bias=1.0)
             nc.vector.tensor_scalar(
-                out=res[n][:], in0=sq[n][:], scalar1=acol[:, i : i + 1], scalar2=None, op0=MULT
+                out=result[n][:], in0=squared[n][:], scalar1=alpha_cols[:, i : i + 1], scalar2=None, op0=MULT
             )
-            nc.sync.dma_start(out=out[i * P : (i + 1) * P, jb * HALF : (jb + 1) * HALF], in_=res[n][:])
-
-        nc.tensor.transpose(banks[7][:, 0:P], arow[:], ident[:])
-        nc.scalar.copy(out=acol[:], in_=banks[7][:, 0 : S2 // P])
+            nc.sync.dma_start(out=out[i * P : (i + 1) * P, half * HALF : (half + 1) * HALF], in_=result[n][:])
 
         gather_tab(0, 0)
         gather_tab_scales()
-        interleave_w1(0, False)
-        for c in range(4):
-            mm_g(c, 0)
+        load_tab(2, on="tab_scale_window")
         gather_tab(0, 1)
+        interleave_w1_scalar(0)
+        gate_pass(0)
         gather_tab(1, 0)
-        quant_w1(0)
-        interleave_w1(1, False)
-        for c in range(4):
-            mm_g(c, 1)
-        for c in range(4):
-            mm_a(c, 0)
         gather_tab(1, 1)
-        quant_w1(1)
-        for c in range(4):
-            mm_a(c, 1)
-        gather_tab2_scales(0)
+        load_w1(1, sbuf("w1_raw1", [P, PACK, H], F32, on="tab_window1"))
+        load_w1(2, placed("w1_raw2", [P, PACK, H], F32, W1_LAST_AT))
+        load_tab2()
+        gate_pass(1)
         gather_tab(2, 0)
         gather_tab(2, 1)
-        for c in range(4):
-            mm_g(c, 2)
+        quantise_w1(0, on="tab_scale_window")
+        interleave_w1_vector(1)
+        quantise_w1(1)
+        gate_pass(2)
+        for c in range(PER_HALF):
             sigmoid(c)
-        interleave_w1(2, True)
-        quant_w1(2)
+        interleave_w1_vector(2)
+        quantise_w1(2)
+        for c in range(PER_HALF, CHUNKS):
+            sigmoid(c)
+        gather_tab2_scales(0)
         gather_tab2_scales(1)
-        for c in range(4, 6):
-            for a in range(PASSES):
-                mm_g(c, a)
-            sigmoid(c)
-        for c in range(4):
-            mm_a(c, 2)
-            gate(c)
-        for c in range(6, 8):
-            for a in range(PASSES):
-                mm_g(c, a)
-            sigmoid(c)
-        turn(0)
-        turn(1)
-        quant_h(0)
-        gather_tab2(0)
-        for c in range(4, 8):
-            for a in range(PASSES):
-                mm_a(c, a)
-            gate(c)
-            result(c - 4)
+
+        for c in range(PER_HALF):
+            gated_chunk(c)
+        nc.tensor.transpose(banks[ALPHA_BANK][:, 0:P], alpha_rows[:], ident[:])
+        nc.scalar.copy(out=alpha_cols[:], in_=banks[ALPHA_BANK][:, 0:ROW_TILES])
+        turn(0, nc.scalar.copy)
+        turn(1, nc.scalar.copy)
+        gather_tab2(0, on="sig%d" % (PER_HALF - 1))
         gather_tab2(1)
-        turn(2)
-        turn(3)
-        quant_h(1)
-        for n in range(4, 16):
-            result(n)
+        quantise_h(0)
+
+        for pair in (2, 3):
+            out_tile(2 * pair - 4)
+            out_tile(2 * pair - 3)
+            gated_chunk(2 * pair)
+            gated_chunk(2 * pair + 1)
+        turn(2, nc.scalar.copy)
+        turn(3, nc.vector.tensor_copy)
+        quantise_h(1)
+        for n in range(4, 2 * ROW_TILES):
+            out_tile(n)

@@ -29,14 +29,19 @@ QUADRANT = 32
 SHIFT_ROWS = 112
 TAB2_PLANE = 12
 
-A_BANK = [0, 1, 2, 3, 0, 1, 2, 3]
-TURN_BANK = [4, 5, 4, 5]
-ALPHA_BANK = 6
-Y_BANK = [6, 7, 6, 7, 0, 1, 6, 7, 2, 3, 0, 1, 6, 7, 4, 5]
+TURN_BANK = [0, 2, 4, 6]
+ALPHA_BANK = 1
+Y_BANK = [3, 1, 0, 2, 3, 1, 0, 2, 5, 7, 3, 1, 0, 2, 4, 6]
 
-W1_LAST_AT = 0
-W1_FIRST_AT = 4096
-TAB2_AT = 8192
+LAP = 64
+WINDOW = 4 * T
+TAB_LAST_AT = 0
+TAB_SCALES_AT = TAB_LAST_AT + WINDOW - LAP
+V_CODES_AT = TAB_SCALES_AT + T - LAP
+W1_LAST_AT = V_CODES_AT + 4 * HALF
+TAB_MID_AT = W1_LAST_AT + WINDOW - LAP
+TAB2_AT = TAB_MID_AT + WINDOW - LAP
+H_TURNED_AT = TAB2_AT + 4 * T2
 
 
 def tile_list_poly_kernel_contributions_kernel(
@@ -56,7 +61,7 @@ def tile_list_poly_kernel_contributions_kernel(
 
         idx = keep.tile([P, S // 16], U16, name="idx")
         idx2 = keep.tile([P, S2 // 16], U16, name="idx2")
-        tab_scale_window = sbuf("tab_scale_window", [P, T], U8)
+        tab_scale_window = placed("tab_scale_window", [P, T], U8, TAB_SCALES_AT)
         tab2_scale_window = sbuf("tab2_scale_window", [P, T2], U8)
         w1_bf16 = [sbuf("w1_bf16_%d" % a, [P, H, PACK], BF16) for a in range(PASSES)]
         w1_plane = [sbuf("w1_plane%d" % a, [P, H], U8) for a in range(PASSES)]
@@ -67,7 +72,7 @@ def tile_list_poly_kernel_contributions_kernel(
         alpha_cols = sbuf("alpha_cols", [P, ROW_TILES], F32)
         ident = sbuf("ident", [P, P], F32)
         sig = [sbuf("sig%d" % c, [P, H], F32) for c in range(CHUNKS)]
-        h_turned = [sbuf("h_turned%d" % b, [P, HALF, PACK], BF16) for b in range(2)]
+        h_turned = [placed("h_turned0", [P, HALF, PACK], BF16, H_TURNED_AT), sbuf("h_turned1", [P, HALF, PACK], BF16)]
         h_plane = [sbuf("h_plane%d" % b, [P, HALF], U8) for b in range(2)]
         squared = [sbuf("squared%d" % n, [P, HALF], F32) for n in range(2 * ROW_TILES)]
         result = [sbuf("result%d" % n, [P, HALF], F32) for n in range(2 * ROW_TILES)]
@@ -76,16 +81,16 @@ def tile_list_poly_kernel_contributions_kernel(
         v_codes, v2_codes, v2_plane, h_chunk, h_codes = {}, {}, {}, {}, {}
 
         nc.vector.memset(tab_scale_window[:].bitcast(I32), 0)
-        nc.vector.memset(tab2_scale_window[:].bitcast(I32), 0)
         nc.vector.memset(w4_plane[:].rearrange("p a c -> p (a c)").bitcast(I32), 0)
+        nc.vector.memset(tab2_scale_window[:].bitcast(I32), 0)
         nc.vector.memset(alpha_rows[:], 0.0)
         for a in range(1, PASSES):
             nc.vector.memset(v_plane[a][:].bitcast(I32), 0)
 
-        def load_tab(a, on=None):
-            tab_window[a] = sbuf("tab_window%d" % a, [P, T], U32, on)
+        def load_tab(a, tile):
+            tab_window[a] = tile
             words = tab_words[a].rearrange("p t i -> p (t i)")
-            nc.sync.dma_start(out=tab_window[a][:].bitcast(I32), in_=words.bitcast(I32))
+            nc.sync.dma_start(out=tile[:].bitcast(I32), in_=words.bitcast(I32))
 
         def load_w1(a, tile):
             w1_raw[a] = tile
@@ -98,26 +103,27 @@ def tile_list_poly_kernel_contributions_kernel(
             nc.sync.dma_start(out=tab2_window[0][:].bitcast(I32), in_=words.bitcast(I32))
 
         nc.sync.dma_start(idx[:], offs)
-        load_tab(0)
+        load_tab(0, sbuf("tab_window0", [P, T], U32))
+        load_w1(0, sbuf("w1_raw0", [P, PACK, H], F32))
         for q in range(4):
             nc.sync.dma_start(
                 out=tab_scale_window[QUADRANT * q : QUADRANT * q + 4 * PASSES, :].bitcast(I32),
                 in_=tab_scales[:, 4 * q : 4 * q + 4, :].bitcast(I32),
             )
-        nc.sync.dma_start(out=w4_codes[:].bitcast(I32), in_=w4_words.bitcast(I32).rearrange("a p c -> p a c"))
-        load_tab(1)
+        load_tab(1, placed("tab_window1", [P, T], U32, TAB_MID_AT))
         nc.sync.dma_start(idx2[:], offs2)
-        for s in range(4):
-            nc.sync.dma_start(
-                out=tab2_scale_window[TAB2_PLANE + s : P : QUADRANT, :].bitcast(I32),
-                in_=tab2_scales[0, s:16:4, :].bitcast(I32),
-            )
+        nc.sync.dma_start(out=w4_codes[:].bitcast(I32), in_=w4_words.bitcast(I32).rearrange("a p c -> p a c"))
         for s in range(4):
             nc.sync.dma_start(
                 out=w4_plane[s:P:QUADRANT, :, :].bitcast(I32),
                 in_=w4_scales[:, s:16:4, :].bitcast(I32).rearrange("a q c -> q a c"),
             )
-        load_w1(0, placed("w1_raw0", [P, PACK, H], F32, W1_FIRST_AT))
+        load_w1(1, sbuf("w1_raw1", [P, PACK, H], F32))
+        for s in range(4):
+            nc.sync.dma_start(
+                out=tab2_scale_window[TAB2_PLANE + s : P : QUADRANT, :].bitcast(I32),
+                in_=tab2_scales[0, s:16:4, :].bitcast(I32),
+            )
         nc.gpsimd.dma_start(out=alpha_rows[0:ROW_TILES, :], in_=alpha.rearrange("(n p) -> n p", p=P))
         make_identity(nc, ident[:])
 
@@ -126,7 +132,10 @@ def tile_list_poly_kernel_contributions_kernel(
             return offsets[:, columns * b : columns * (b + 1)]
 
         def gather_tab(a, b):
-            v_codes[a, b] = sbuf("v_codes%d_%d" % (a, b), [P, HALF], U32)
+            if (a, b) == (1, 0):
+                v_codes[a, b] = placed("v_codes%d_%d" % (a, b), [P, HALF], U32, V_CODES_AT)
+            else:
+                v_codes[a, b] = sbuf("v_codes%d_%d" % (a, b), [P, HALF], U32)
             nc.vector.tensor_copy(out=v_codes[a, b][:], in_=tab_window[a][:].indirect(half_of(idx, b)))
 
         def gather_tab_scales():
@@ -138,7 +147,7 @@ def tile_list_poly_kernel_contributions_kernel(
                 )
 
         def gather_tab2_scales(b):
-            v2_plane[b] = sbuf("v2_plane%d" % b, [P, HALF], U8)
+            v2_plane[b] = placed("v2_plane%d" % b, [P, HALF], U8, TAB_MID_AT + (b + 1) * 2 * HALF)
             nc.vector.tensor_copy(out=v2_plane[b][:], in_=tab2_scale_window[:].indirect(half_of(idx2, b)))
 
         def gather_tab2(b, on=None):
@@ -154,15 +163,18 @@ def tile_list_poly_kernel_contributions_kernel(
         def interleave_w1_vector(a):
             nc.vector.tensor_copy(out=w1_bf16[a][:], in_=w1_raw[a][:].rearrange("p t c -> p c t"))
 
-        def quantise_w1(a, on=None):
-            w1_codes[a] = sbuf("w1_codes%d" % a, [P, H], U32, on)
+        def quantise_w1(a):
+            if a == 1:
+                w1_codes[a] = placed("w1_codes%d" % a, [P, H], U32, TAB_LAST_AT)
+            else:
+                w1_codes[a] = sbuf("w1_codes%d" % a, [P, H], U32)
             nc.vector.quantize_mx(
                 out=w1_codes[a][:].bitcast(FP8X4),
                 scales=w1_plane[a][:],
                 in_=w1_bf16[a][:].rearrange("p c t -> p (c t)"),
             )
 
-        def project(bank, c, a, codes, plane):
+        def project(bank, c, a, codes, plane, order=tuple(range(PASSES))):
             b, o = divmod(c, PER_HALF)
             nc.tensor.matmul_mx(
                 out=bank[:],
@@ -170,8 +182,8 @@ def tile_list_poly_kernel_contributions_kernel(
                 lhsT_scale=v_plane[a][:, c * P : (c + 1) * P],
                 rhs=codes,
                 rhs_scale=plane,
-                start=(a == 0),
-                stop=(a == PASSES - 1),
+                start=(a == order[0]),
+                stop=(a == order[-1]),
             )
 
         def gate_pass(a):
@@ -187,15 +199,18 @@ def tile_list_poly_kernel_contributions_kernel(
         def sigmoid(c):
             nc.scalar.activation(out=as_stored(sig[c]), in_=in_word_order(banks[c]), func=ACT.Sigmoid)
 
-        def gated_chunk(c):
-            bank = banks[A_BANK[c]]
-            for a in range(PASSES):
-                project(bank, c, a, w1_codes[a][:].bitcast(FP8X4), w1_plane[a][:])
-            if c == PER_HALF:
-                h_chunk[c] = placed("h_chunk%d" % c, [P, H], BF16, TAB2_AT)
-            else:
+        def value_pass(c, a):
+            order = (0, 1, 2) if c < PER_HALF else (2, 1, 0)
+            project(banks[c], c, a, w1_codes[a][:].bitcast(FP8X4), w1_plane[a][:], order)
+
+        def gate(c):
+            if c < PER_HALF:
                 h_chunk[c] = sbuf("h_chunk%d" % c, [P, H], BF16)
-            nc.vector.tensor_tensor(out=as_stored(h_chunk[c]), in0=in_word_order(bank), in1=as_stored(sig[c]), op=MULT)
+            else:
+                h_chunk[c] = placed("h_chunk%d" % c, [P, H], BF16, H_TURNED_AT + (c - PER_HALF) * 2 * H)
+            nc.vector.tensor_tensor(
+                out=as_stored(h_chunk[c]), in0=in_word_order(banks[c]), in1=as_stored(sig[c]), op=MULT
+            )
 
         def turn(pair, copy):
             bank = banks[TURN_BANK[pair]]
@@ -236,48 +251,54 @@ def tile_list_poly_kernel_contributions_kernel(
             nc.sync.dma_start(out=out[i * P : (i + 1) * P, half * HALF : (half + 1) * HALF], in_=result[n][:])
 
         gather_tab(0, 0)
-        gather_tab_scales()
-        load_tab(2, on="tab_scale_window")
         gather_tab(0, 1)
+        gather_tab_scales()
+        load_tab(2, placed("tab_window2", [P, T], U32, TAB_LAST_AT))
         interleave_w1_scalar(0)
         gate_pass(0)
         gather_tab(1, 0)
         gather_tab(1, 1)
-        load_w1(1, sbuf("w1_raw1", [P, PACK, H], F32, on="tab_window1"))
         load_w1(2, placed("w1_raw2", [P, PACK, H], F32, W1_LAST_AT))
         load_tab2()
+        quantise_w1(0)
+        gather_tab2_scales(0)
+        gather_tab2_scales(1)
+        interleave_w1_scalar(1)
         gate_pass(1)
         gather_tab(2, 0)
         gather_tab(2, 1)
-        quantise_w1(0, on="tab_scale_window")
-        interleave_w1_vector(1)
-        quantise_w1(1)
         gate_pass(2)
-        for c in range(PER_HALF):
+        quantise_w1(1)
+        for c in range(CHUNKS):
             sigmoid(c)
         interleave_w1_vector(2)
         quantise_w1(2)
-        for c in range(PER_HALF, CHUNKS):
-            sigmoid(c)
-        gather_tab2_scales(0)
-        gather_tab2_scales(1)
 
         for c in range(PER_HALF):
-            gated_chunk(c)
+            value_pass(c, 0)
+            value_pass(c, 1)
+        for c in range(PER_HALF):
+            value_pass(c, 2)
+            gate(c)
+        for c in range(PER_HALF, CHUNKS):
+            for a in reversed(range(PASSES)):
+                value_pass(c, a)
+        turn(0, nc.scalar.copy)
         nc.tensor.transpose(banks[ALPHA_BANK][:, 0:P], alpha_rows[:], ident[:])
         nc.scalar.copy(out=alpha_cols[:], in_=banks[ALPHA_BANK][:, 0:ROW_TILES])
-        turn(0, nc.scalar.copy)
         turn(1, nc.scalar.copy)
         gather_tab2(0, on="sig%d" % (PER_HALF - 1))
-        gather_tab2(1)
         quantise_h(0)
-
-        for pair in (2, 3):
-            out_tile(2 * pair - 4)
-            out_tile(2 * pair - 3)
-            gated_chunk(2 * pair)
-            gated_chunk(2 * pair + 1)
+        gate(4)
+        gate(5)
+        out_tile(0)
+        out_tile(1)
+        gather_tab2(1, on="sig5")
         turn(2, nc.scalar.copy)
+        gate(6)
+        gate(7)
+        out_tile(2)
+        out_tile(3)
         turn(3, nc.vector.tensor_copy)
         quantise_h(1)
         for n in range(4, 2 * ROW_TILES):

@@ -16,6 +16,7 @@ FP8X4 = mybir.dt.float8_e4m3fn_x4
 FP4X4 = mybir.dt.float4_e2m1fn_x4
 ACT = mybir.ActivationFunctionType
 MULT = mybir.AluOpType.mult
+ADD = mybir.AluOpType.add
 
 P = 128
 PACK = 4
@@ -27,18 +28,21 @@ PER_HALF = HALF // P
 ROW_TILES = S2 // P
 QUADRANT = 32
 SHIFT_ROWS = 112
+GPSIMD_TILES = 0
+TAB2_ROWS_AT, TAB2_ROWS_STEP = 4, 8
 TAB2_PLANE = 12
 
-TURN_BANK = [0, 2, 4, 6]
-ALPHA_BANK = 1
-Y_BANK = [3, 1, 0, 2, 3, 1, 0, 2, 5, 7, 3, 1, 0, 2, 4, 6]
+A_BANK = [0, 1, 2, 3, 4, 5, 0, 2]
+TURN_BANK = [0, 2, 4, 0]
+ALPHA_BANK = 7
+Y_BANK = [6, 7, 1, 3, 6, 7, 1, 3, 5, 6, 7, 1, 3, 2, 4, 0]
 
 LAP = 64
 WINDOW = 4 * T
 TAB_LAST_AT = 0
 TAB_SCALES_AT = TAB_LAST_AT + WINDOW - LAP
 V_CODES_AT = TAB_SCALES_AT + T - LAP
-W1_LAST_AT = V_CODES_AT + 4 * HALF
+W1_LAST_AT = V_CODES_AT + 4 * S
 TAB_MID_AT = W1_LAST_AT + WINDOW - LAP
 TAB2_AT = TAB_MID_AT + WINDOW - LAP
 H_TURNED_AT = TAB2_AT + 4 * T2
@@ -68,9 +72,9 @@ def tile_list_poly_kernel_contributions_kernel(
         w4_codes = sbuf("w4_codes", [P, PASSES, 2 * H], U8)
         w4_plane = sbuf("w4_plane", [P, PASSES, H], U8)
         v_plane = [sbuf("v_plane%d" % a, [P, S], U8) for a in range(PASSES)]
+        v2_plane = sbuf("v2_plane", [P, S2], U8)
         alpha_rows = sbuf("alpha_rows", [P, P], F32)
         alpha_cols = sbuf("alpha_cols", [P, ROW_TILES], F32)
-        ident = sbuf("ident", [P, P], F32)
         sig = [sbuf("sig%d" % c, [P, H], F32) for c in range(CHUNKS)]
         h_turned = [placed("h_turned0", [P, HALF, PACK], BF16, H_TURNED_AT), sbuf("h_turned1", [P, HALF, PACK], BF16)]
         h_plane = [sbuf("h_plane%d" % b, [P, HALF], U8) for b in range(2)]
@@ -78,7 +82,7 @@ def tile_list_poly_kernel_contributions_kernel(
         result = [sbuf("result%d" % n, [P, HALF], F32) for n in range(2 * ROW_TILES)]
         banks = [psum.tile([P, HALF], F32, name="bank%d" % b) for b in range(8)]
         tab_window, tab2_window, w1_raw, w1_codes = {}, {}, {}, {}
-        v_codes, v2_codes, v2_plane, h_chunk, h_codes = {}, {}, {}, {}, {}
+        v_codes, v2_codes, h_chunk, h_codes = {}, {}, {}, {}
 
         nc.vector.memset(tab_scale_window[:].bitcast(I32), 0)
         nc.vector.memset(w4_plane[:].rearrange("p a c -> p (a c)").bitcast(I32), 0)
@@ -86,6 +90,7 @@ def tile_list_poly_kernel_contributions_kernel(
         nc.vector.memset(alpha_rows[:], 0.0)
         for a in range(1, PASSES):
             nc.vector.memset(v_plane[a][:].bitcast(I32), 0)
+        nc.vector.memset(v2_plane[:].bitcast(I32), 0)
 
         def load_tab(a, tile):
             tab_window[a] = tile
@@ -118,25 +123,25 @@ def tile_list_poly_kernel_contributions_kernel(
                 out=w4_plane[s:P:QUADRANT, :, :].bitcast(I32),
                 in_=w4_scales[:, s:16:4, :].bitcast(I32).rearrange("a q c -> q a c"),
             )
+        nc.sync.dma_start(
+            out=tab2_scale_window[TAB2_ROWS_AT:P:TAB2_ROWS_STEP, :].bitcast(I32), in_=tab2_scales[0].bitcast(I32)
+        )
         load_w1(1, sbuf("w1_raw1", [P, PACK, H], F32))
-        for s in range(4):
-            nc.sync.dma_start(
-                out=tab2_scale_window[TAB2_PLANE + s : P : QUADRANT, :].bitcast(I32),
-                in_=tab2_scales[0, s:16:4, :].bitcast(I32),
-            )
         nc.gpsimd.dma_start(out=alpha_rows[0:ROW_TILES, :], in_=alpha.rearrange("(n p) -> n p", p=P))
-        make_identity(nc, ident[:])
 
         def half_of(offsets, b):
             columns = HALF // 16
             return offsets[:, columns * b : columns * (b + 1)]
 
         def gather_tab(a, b):
-            if (a, b) == (1, 0):
-                v_codes[a, b] = placed("v_codes%d_%d" % (a, b), [P, HALF], U32, V_CODES_AT)
-            else:
-                v_codes[a, b] = sbuf("v_codes%d_%d" % (a, b), [P, HALF], U32)
-            nc.vector.tensor_copy(out=v_codes[a, b][:], in_=tab_window[a][:].indirect(half_of(idx, b)))
+            tile = sbuf("v_codes%d_%d" % (a, b), [P, HALF], U32)
+            nc.vector.tensor_copy(out=tile[:], in_=tab_window[a][:].indirect(half_of(idx, b)))
+            v_codes[a, b] = tile[:]
+
+        def gather_tab_whole(a, tile):
+            nc.vector.tensor_copy(out=tile[:], in_=tab_window[a][:].indirect(idx[:]))
+            for b in range(2):
+                v_codes[a, b] = tile[:, b * HALF : (b + 1) * HALF]
 
         def gather_tab_scales():
             nc.vector.tensor_copy(out=v_plane[0][:], in_=tab_scale_window[:].indirect(idx[:]))
@@ -146,26 +151,35 @@ def tile_list_poly_kernel_contributions_kernel(
                     in_=v_plane[0][4 * a : 4 * a + SHIFT_ROWS, :].bitcast(I32),
                 )
 
-        def gather_tab2_scales(b):
-            v2_plane[b] = placed("v2_plane%d" % b, [P, HALF], U8, TAB_MID_AT + (b + 1) * 2 * HALF)
-            nc.vector.tensor_copy(out=v2_plane[b][:], in_=tab2_scale_window[:].indirect(half_of(idx2, b)))
+        def gather_tab2_scales():
+            rows = placed("v2_scale_rows", [P, S2], U8, TAB_MID_AT + S2)
+            nc.vector.tensor_copy(out=rows[:], in_=tab2_scale_window[:].indirect(idx2[:]))
+            for s in range(4):
+                nc.gpsimd.dma_start(
+                    out=v2_plane[TAB2_PLANE + s : P : QUADRANT, :].bitcast(I32),
+                    in_=rows[TAB2_ROWS_AT + TAB2_ROWS_STEP * s : P : QUADRANT, :].bitcast(I32),
+                )
 
         def gather_tab2(b, on=None):
             v2_codes[b] = sbuf("v2_codes%d" % b, [P, HALF], U32, on)
             nc.vector.tensor_copy(out=v2_codes[b][:], in_=tab2_window[0][:].indirect(half_of(idx2, b)))
 
-        def interleave_w1_scalar(a):
+        def interleave_w1_scalar(a, columns=slice(0, H)):
             nc.scalar.copy(
-                out=w1_bf16[a][:].rearrange("p (c i) t -> p c t i", i=4),
-                in_=w1_raw[a][:].rearrange("p t (c i) -> p c t i", i=4),
+                out=w1_bf16[a][:, columns, :].rearrange("p (c i) t -> p c t i", i=4),
+                in_=w1_raw[a][:, :, columns].rearrange("p t (c i) -> p c t i", i=4),
             )
 
-        def interleave_w1_vector(a):
-            nc.vector.tensor_copy(out=w1_bf16[a][:], in_=w1_raw[a][:].rearrange("p t c -> p c t"))
+        def interleave_w1_vector(a, columns):
+            nc.vector.tensor_copy(
+                out=w1_bf16[a][:, columns, :], in_=w1_raw[a][:, :, columns].rearrange("p t c -> p c t")
+            )
 
         def quantise_w1(a):
             if a == 1:
                 w1_codes[a] = placed("w1_codes%d" % a, [P, H], U32, TAB_LAST_AT)
+            elif a == 0:
+                w1_codes[a] = placed("w1_codes%d" % a, [P, H], U32, TAB_MID_AT + WINDOW // 2)
             else:
                 w1_codes[a] = sbuf("w1_codes%d" % a, [P, H], U32)
             nc.vector.quantize_mx(
@@ -201,7 +215,7 @@ def tile_list_poly_kernel_contributions_kernel(
 
         def value_pass(c, a):
             order = (0, 1, 2) if c < PER_HALF else (2, 1, 0)
-            project(banks[c], c, a, w1_codes[a][:].bitcast(FP8X4), w1_plane[a][:], order)
+            project(banks[A_BANK[c]], c, a, w1_codes[a][:].bitcast(FP8X4), w1_plane[a][:], order)
 
         def gate(c):
             if c < PER_HALF:
@@ -209,7 +223,7 @@ def tile_list_poly_kernel_contributions_kernel(
             else:
                 h_chunk[c] = placed("h_chunk%d" % c, [P, H], BF16, H_TURNED_AT + (c - PER_HALF) * 2 * H)
             nc.vector.tensor_tensor(
-                out=as_stored(h_chunk[c]), in0=in_word_order(banks[c]), in1=as_stored(sig[c]), op=MULT
+                out=as_stored(h_chunk[c]), in0=in_word_order(banks[A_BANK[c]]), in1=as_stored(sig[c]), op=MULT
             )
 
         def turn(pair, copy):
@@ -238,41 +252,47 @@ def tile_list_poly_kernel_contributions_kernel(
             nc.tensor.matmul_mx(
                 out=bank[:],
                 lhsT=v2_codes[b][:, o * P : (o + 1) * P].bitcast(FP8X4),
-                lhsT_scale=v2_plane[b][TAB2_PLANE:P, o * P : (o + 1) * P],
+                lhsT_scale=v2_plane[TAB2_PLANE:P, i * P : (i + 1) * P],
                 rhs=h_codes[half][:].bitcast(FP8X4),
                 rhs_scale=h_plane[half][:],
                 start=True,
                 stop=True,
             )
             nc.scalar.activation(out=squared[n][:], in_=bank[:], func=ACT.Square, bias=1.0)
-            nc.vector.tensor_scalar(
-                out=result[n][:], in0=squared[n][:], scalar1=alpha_cols[:, i : i + 1], scalar2=None, op0=MULT
-            )
+            if n < GPSIMD_TILES:
+                nc.gpsimd.tensor_scalar(
+                    out=result[n][:], in0=squared[n][:], scalar1=alpha_cols[:, i : i + 1], scalar2=0.0, op0=MULT, op1=ADD
+                )
+            else:
+                nc.vector.tensor_scalar(
+                    out=result[n][:], in0=squared[n][:], scalar1=alpha_cols[:, i : i + 1], scalar2=None, op0=MULT
+                )
             nc.sync.dma_start(out=out[i * P : (i + 1) * P, half * HALF : (half + 1) * HALF], in_=result[n][:])
 
-        gather_tab(0, 0)
-        gather_tab(0, 1)
+        gather_tab_whole(0, sbuf("v_codes0", [P, S], U32))
+        ident = sbuf("ident", [P, P], F32, on="tab_window0")
+        make_identity(nc, ident[:])
         gather_tab_scales()
         load_tab(2, placed("tab_window2", [P, T], U32, TAB_LAST_AT))
         interleave_w1_scalar(0)
         gate_pass(0)
-        gather_tab(1, 0)
-        gather_tab(1, 1)
+        gather_tab_whole(1, placed("v_codes1", [P, S], U32, V_CODES_AT))
         load_w1(2, placed("w1_raw2", [P, PACK, H], F32, W1_LAST_AT))
         load_tab2()
         quantise_w1(0)
-        gather_tab2_scales(0)
-        gather_tab2_scales(1)
+        gather_tab2_scales()
         interleave_w1_scalar(1)
         gate_pass(1)
         gather_tab(2, 0)
         gather_tab(2, 1)
         gate_pass(2)
+        interleave_w1_vector(2, slice(0, H))
         quantise_w1(1)
         for c in range(CHUNKS):
             sigmoid(c)
-        interleave_w1_vector(2)
         quantise_w1(2)
+        nc.tensor.transpose(banks[ALPHA_BANK][:, 0:P], alpha_rows[:], ident[:])
+        nc.scalar.copy(out=alpha_cols[:], in_=banks[ALPHA_BANK][:, 0:ROW_TILES])
 
         for c in range(PER_HALF):
             value_pass(c, 0)
@@ -280,25 +300,23 @@ def tile_list_poly_kernel_contributions_kernel(
         for c in range(PER_HALF):
             value_pass(c, 2)
             gate(c)
+        turn(0, nc.scalar.copy)
+        turn(1, nc.scalar.copy)
         for c in range(PER_HALF, CHUNKS):
             for a in reversed(range(PASSES)):
                 value_pass(c, a)
-        turn(0, nc.scalar.copy)
-        nc.tensor.transpose(banks[ALPHA_BANK][:, 0:P], alpha_rows[:], ident[:])
-        nc.scalar.copy(out=alpha_cols[:], in_=banks[ALPHA_BANK][:, 0:ROW_TILES])
-        turn(1, nc.scalar.copy)
         gather_tab2(0, on="sig%d" % (PER_HALF - 1))
         quantise_h(0)
-        gate(4)
-        gate(5)
         out_tile(0)
         out_tile(1)
-        gather_tab2(1, on="sig5")
+        gate(4)
+        gate(5)
         turn(2, nc.scalar.copy)
-        gate(6)
-        gate(7)
         out_tile(2)
         out_tile(3)
+        gate(6)
+        gate(7)
+        gather_tab2(1, on="sig7")
         turn(3, nc.vector.tensor_copy)
         quantise_h(1)
         for n in range(4, 2 * ROW_TILES):

@@ -16,7 +16,6 @@ FP8X4 = mybir.dt.float8_e4m3fn_x4
 FP4X4 = mybir.dt.float4_e2m1fn_x4
 ACT = mybir.ActivationFunctionType
 MULT = mybir.AluOpType.mult
-ADD = mybir.AluOpType.add
 
 P = 128
 PACK = 4
@@ -28,22 +27,25 @@ PER_HALF = HALF // P
 ROW_TILES = S2 // P
 QUADRANT = 32
 SHIFT_ROWS = 112
-GPSIMD_TILES = 0
+SIG_EARLY = 0
+VECTOR_COLUMNS = 256
 TAB2_ROWS_AT, TAB2_ROWS_STEP = 4, 8
 TAB2_PLANE = 12
 
-A_BANK = [0, 1, 2, 3, 4, 5, 0, 2]
-TURN_BANK = [0, 2, 4, 0]
+G_BANK = [0, 1, 2, 3, 0, 1, 2, 3]
+A_BANK = [4, 5, 6, 7, 6, 7, 0, 1]
+TURN_BANK = [4, 5, 6, 7]
 ALPHA_BANK = 7
-Y_BANK = [6, 7, 1, 3, 6, 7, 1, 3, 5, 6, 7, 1, 3, 2, 4, 0]
+Y_BANK = [4, 5, 2, 3, 4, 5, 2, 3, 6, 4, 5, 2, 0, 1, 3, 7]
 
 LAP = 64
 WINDOW = 4 * T
-TAB_LAST_AT = 0
-TAB_SCALES_AT = TAB_LAST_AT + WINDOW - LAP
+W1_LAST_AT = 0
+TAB_SCALES_AT = W1_LAST_AT + WINDOW - LAP
 V_CODES_AT = TAB_SCALES_AT + T - LAP
-W1_LAST_AT = V_CODES_AT + 4 * S
-TAB_MID_AT = W1_LAST_AT + WINDOW - LAP
+SIG_AT = W1_LAST_AT
+W1_FIRST_AT = V_CODES_AT + 4 * S - LAP
+TAB_MID_AT = W1_FIRST_AT + 2 * PACK * H
 TAB2_AT = TAB_MID_AT + WINDOW - LAP
 H_TURNED_AT = TAB2_AT + 4 * T2
 
@@ -67,27 +69,32 @@ def tile_list_poly_kernel_contributions_kernel(
         idx2 = keep.tile([P, S2 // 16], U16, name="idx2")
         tab_scale_window = placed("tab_scale_window", [P, T], U8, TAB_SCALES_AT)
         tab2_scale_window = sbuf("tab2_scale_window", [P, T2], U8)
-        w1_bf16 = [sbuf("w1_bf16_%d" % a, [P, H, PACK], BF16) for a in range(PASSES)]
-        w1_plane = [sbuf("w1_plane%d" % a, [P, H], U8) for a in range(PASSES)]
+        w1_bf16 = [placed("w1_bf16_0", [P, H, PACK], BF16, W1_FIRST_AT)]
+        w1_bf16 = w1_bf16 + [sbuf("w1_bf16_%d" % a, [P, H, PACK], BF16) for a in range(1, PASSES)]
         w4_codes = sbuf("w4_codes", [P, PASSES, 2 * H], U8)
         w4_plane = sbuf("w4_plane", [P, PASSES, H], U8)
         v_plane = [sbuf("v_plane%d" % a, [P, S], U8) for a in range(PASSES)]
         v2_plane = sbuf("v2_plane", [P, S2], U8)
         alpha_rows = sbuf("alpha_rows", [P, P], F32)
         alpha_cols = sbuf("alpha_cols", [P, ROW_TILES], F32)
-        sig = [sbuf("sig%d" % c, [P, H], F32) for c in range(CHUNKS)]
-        h_turned = [placed("h_turned0", [P, HALF, PACK], BF16, H_TURNED_AT), sbuf("h_turned1", [P, HALF, PACK], BF16)]
-        h_plane = [sbuf("h_plane%d" % b, [P, HALF], U8) for b in range(2)]
+        sig = {}
+        h_turned = [placed("h_turned0", [P, HALF, PACK], BF16, H_TURNED_AT)]
+        h_turned = h_turned + [sbuf("h_turned%d" % b, [P, HALF // 2, PACK], BF16) for b in (1, 2)]
+        h_plane = [sbuf("h_plane%d" % b, [P, HALF // min(b + 1, 2)], U8) for b in range(3)]
         squared = [sbuf("squared%d" % n, [P, HALF], F32) for n in range(2 * ROW_TILES)]
         result = [sbuf("result%d" % n, [P, HALF], F32) for n in range(2 * ROW_TILES)]
         banks = [psum.tile([P, HALF], F32, name="bank%d" % b) for b in range(8)]
-        tab_window, tab2_window, w1_raw, w1_codes = {}, {}, {}, {}
+        tab_window, tab2_window, w1_raw, w1_codes, w1_plane = {}, {}, {}, {}, {}
         v_codes, v2_codes, h_chunk, h_codes = {}, {}, {}, {}
 
+        nc.gpsimd.memset(tab2_scale_window[:, 0 : T2 // 2].bitcast(I32), 0)
+        nc.vector.memset(tab2_scale_window[:, T2 // 2 : T2].bitcast(I32), 0)
         nc.vector.memset(tab_scale_window[:].bitcast(I32), 0)
         nc.vector.memset(w4_plane[:].rearrange("p a c -> p (a c)").bitcast(I32), 0)
-        nc.vector.memset(tab2_scale_window[:].bitcast(I32), 0)
         nc.vector.memset(alpha_rows[:], 0.0)
+        warm = sbuf("warm", [P, 16], F32)
+        nc.gpsimd.memset(warm[:, 0:8], 0.0)
+        nc.scalar.activation(out=warm[:, 8:16], in_=warm[:, 0:8], func=ACT.Sigmoid)
         for a in range(1, PASSES):
             nc.vector.memset(v_plane[a][:].bitcast(I32), 0)
         nc.vector.memset(v2_plane[:].bitcast(I32), 0)
@@ -107,7 +114,12 @@ def tile_list_poly_kernel_contributions_kernel(
             words = tab2_words[0].rearrange("p t i -> p (t i)")
             nc.sync.dma_start(out=tab2_window[0][:].bitcast(I32), in_=words.bitcast(I32))
 
+        nc.sync.dma_start(idx2[:], offs2)
         nc.sync.dma_start(idx[:], offs)
+        nc.sync.dma_start(out=w4_codes[:].bitcast(I32), in_=w4_words.bitcast(I32).rearrange("a p c -> p a c"))
+        nc.sync.dma_start(
+            out=tab2_scale_window[TAB2_ROWS_AT:P:TAB2_ROWS_STEP, :].bitcast(I32), in_=tab2_scales[0].bitcast(I32)
+        )
         load_tab(0, sbuf("tab_window0", [P, T], U32))
         load_w1(0, sbuf("w1_raw0", [P, PACK, H], F32))
         for q in range(4):
@@ -116,32 +128,26 @@ def tile_list_poly_kernel_contributions_kernel(
                 in_=tab_scales[:, 4 * q : 4 * q + 4, :].bitcast(I32),
             )
         load_tab(1, placed("tab_window1", [P, T], U32, TAB_MID_AT))
-        nc.sync.dma_start(idx2[:], offs2)
-        nc.sync.dma_start(out=w4_codes[:].bitcast(I32), in_=w4_words.bitcast(I32).rearrange("a p c -> p a c"))
-        for s in range(4):
+        for q in range(4):
             nc.sync.dma_start(
-                out=w4_plane[s:P:QUADRANT, :, :].bitcast(I32),
-                in_=w4_scales[:, s:16:4, :].bitcast(I32).rearrange("a q c -> q a c"),
+                out=w4_plane[QUADRANT * q : QUADRANT * q + 4, :, :].bitcast(I32),
+                in_=w4_scales[:, 4 * q : 4 * q + 4, :].bitcast(I32).rearrange("a s c -> s a c"),
             )
-        nc.sync.dma_start(
-            out=tab2_scale_window[TAB2_ROWS_AT:P:TAB2_ROWS_STEP, :].bitcast(I32), in_=tab2_scales[0].bitcast(I32)
-        )
         load_w1(1, sbuf("w1_raw1", [P, PACK, H], F32))
+        load_tab(2, sbuf("tab_window2", [P, T], U32))
         nc.gpsimd.dma_start(out=alpha_rows[0:ROW_TILES, :], in_=alpha.rearrange("(n p) -> n p", p=P))
 
         def half_of(offsets, b):
             columns = HALF // 16
             return offsets[:, columns * b : columns * (b + 1)]
 
-        def gather_tab(a, b):
-            tile = sbuf("v_codes%d_%d" % (a, b), [P, HALF], U32)
-            nc.vector.tensor_copy(out=tile[:], in_=tab_window[a][:].indirect(half_of(idx, b)))
-            v_codes[a, b] = tile[:]
-
-        def gather_tab_whole(a, tile):
-            nc.vector.tensor_copy(out=tile[:], in_=tab_window[a][:].indirect(idx[:]))
-            for b in range(2):
-                v_codes[a, b] = tile[:, b * HALF : (b + 1) * HALF]
+        def gather_tab(a, first, tile):
+            count = tile[:].shape[1] // P
+            columns = P // 16
+            offsets = idx[:, columns * first : columns * (first + count)]
+            nc.vector.tensor_copy(out=tile[:], in_=tab_window[a][:].indirect(offsets))
+            for o in range(count):
+                v_codes[a, first + o] = tile[:, o * P : (o + 1) * P]
 
         def gather_tab_scales():
             nc.vector.tensor_copy(out=v_plane[0][:], in_=tab_scale_window[:].indirect(idx[:]))
@@ -152,16 +158,17 @@ def tile_list_poly_kernel_contributions_kernel(
                 )
 
         def gather_tab2_scales():
-            rows = placed("v2_scale_rows", [P, S2], U8, TAB_MID_AT + S2)
+            rows = sbuf("v2_scale_rows", [P, S2], U8)
             nc.vector.tensor_copy(out=rows[:], in_=tab2_scale_window[:].indirect(idx2[:]))
-            for s in range(4):
-                nc.gpsimd.dma_start(
-                    out=v2_plane[TAB2_PLANE + s : P : QUADRANT, :].bitcast(I32),
-                    in_=rows[TAB2_ROWS_AT + TAB2_ROWS_STEP * s : P : QUADRANT, :].bitcast(I32),
+            for q in range(4):
+                first = QUADRANT * q
+                nc.sync.dma_start(
+                    out=v2_plane[first + TAB2_PLANE : first + TAB2_PLANE + 4, :].bitcast(I32),
+                    in_=rows[first + TAB2_ROWS_AT : first + QUADRANT : TAB2_ROWS_STEP, :].bitcast(I32),
                 )
 
-        def gather_tab2(b, on=None):
-            v2_codes[b] = sbuf("v2_codes%d" % b, [P, HALF], U32, on)
+        def gather_tab2(b, tile):
+            v2_codes[b] = tile
             nc.vector.tensor_copy(out=v2_codes[b][:], in_=tab2_window[0][:].indirect(half_of(idx2, b)))
 
         def interleave_w1_scalar(a, columns=slice(0, H)):
@@ -176,12 +183,11 @@ def tile_list_poly_kernel_contributions_kernel(
             )
 
         def quantise_w1(a):
-            if a == 1:
-                w1_codes[a] = placed("w1_codes%d" % a, [P, H], U32, TAB_LAST_AT)
-            elif a == 0:
-                w1_codes[a] = placed("w1_codes%d" % a, [P, H], U32, TAB_MID_AT + WINDOW // 2)
+            if a == 0:
+                w1_codes[a] = sbuf("w1_codes%d" % a, [P, H], U32, on="alpha_rows")
             else:
                 w1_codes[a] = sbuf("w1_codes%d" % a, [P, H], U32)
+            w1_plane[a] = sbuf("w1_plane%d" % a, [P, H], U8)
             nc.vector.quantize_mx(
                 out=w1_codes[a][:].bitcast(FP8X4),
                 scales=w1_plane[a][:],
@@ -189,10 +195,9 @@ def tile_list_poly_kernel_contributions_kernel(
             )
 
         def project(bank, c, a, codes, plane, order=tuple(range(PASSES))):
-            b, o = divmod(c, PER_HALF)
             nc.tensor.matmul_mx(
                 out=bank[:],
-                lhsT=v_codes[a, b][:, o * P : (o + 1) * P].bitcast(FP8X4),
+                lhsT=v_codes[a, c].bitcast(FP8X4),
                 lhsT_scale=v_plane[a][:, c * P : (c + 1) * P],
                 rhs=codes,
                 rhs_scale=plane,
@@ -200,9 +205,8 @@ def tile_list_poly_kernel_contributions_kernel(
                 stop=(a == order[-1]),
             )
 
-        def gate_pass(a):
-            for c in range(CHUNKS):
-                project(banks[c], c, a, w4_codes[:, a, :].bitcast(FP4X4), w4_plane[:, a, :])
+        def gate_pass(c, a):
+            project(banks[G_BANK[c]], c, a, w4_codes[:, a, :].bitcast(FP4X4), w4_plane[:, a, :])
 
         def in_word_order(bank):
             return bank[:].rearrange("j (p u e) -> j u p e", u=2, e=2)
@@ -211,17 +215,17 @@ def tile_list_poly_kernel_contributions_kernel(
             return tile[:].rearrange("j (u p e) -> j u p e", u=2, e=2)
 
         def sigmoid(c):
-            nc.scalar.activation(out=as_stored(sig[c]), in_=in_word_order(banks[c]), func=ACT.Sigmoid)
+            if SIG_EARLY <= c < PER_HALF:
+                sig[c] = placed("sig%d" % c, [P, H], F32, SIG_AT + (c - SIG_EARLY) * 4 * H)
+            else:
+                sig[c] = sbuf("sig%d" % c, [P, H], F32)
+            nc.scalar.activation(out=as_stored(sig[c]), in_=in_word_order(banks[G_BANK[c]]), func=ACT.Sigmoid)
 
         def value_pass(c, a):
-            order = (0, 1, 2) if c < PER_HALF else (2, 1, 0)
-            project(banks[A_BANK[c]], c, a, w1_codes[a][:].bitcast(FP8X4), w1_plane[a][:], order)
+            project(banks[A_BANK[c]], c, a, w1_codes[a][:].bitcast(FP8X4), w1_plane[a][:])
 
         def gate(c):
-            if c < PER_HALF:
-                h_chunk[c] = sbuf("h_chunk%d" % c, [P, H], BF16)
-            else:
-                h_chunk[c] = placed("h_chunk%d" % c, [P, H], BF16, H_TURNED_AT + (c - PER_HALF) * 2 * H)
+            h_chunk[c] = sbuf("h_chunk%d" % c, [P, H], BF16)
             nc.vector.tensor_tensor(
                 out=as_stored(h_chunk[c]), in0=in_word_order(banks[A_BANK[c]]), in1=as_stored(sig[c]), op=MULT
             )
@@ -233,91 +237,143 @@ def tile_list_poly_kernel_contributions_kernel(
                 for u in range(2):
                     o = (2 * u + second) * P
                     nc.tensor.transpose(bank[:, o : o + P], words[:, u * P : (u + 1) * P], ident[:])
-            b, o = divmod(pair, 2)
+            b, o = (0, pair) if pair < 2 else (pair - 1, 0)
             samples = h_turned[b][:, o * 2 * P : (o + 1) * 2 * P, :].rearrange("p j t -> p (j t)").bitcast(F32)
             copy(out=samples.rearrange("p (j u) -> p j u", u=2), in_=bank[:].rearrange("p (u j) -> p j u", u=2))
 
         def quantise_h(b):
-            h_codes[b] = sbuf("h_codes%d" % b, [P, HALF], U32)
+            h_codes[b] = sbuf("h_codes%d" % b, [P, HALF // min(b + 1, 2)], U32)
             nc.vector.quantize_mx(
                 out=h_codes[b][:].bitcast(FP8X4),
                 scales=h_plane[b][:],
                 in_=h_turned[b][:].rearrange("p j t -> p (j t)"),
             )
 
-        def out_tile(n):
-            half, i = divmod(n, ROW_TILES)
-            b, o = divmod(i, PER_HALF)
+        def out_block(n, piece, tiles):
             bank = banks[Y_BANK[n]]
-            nc.tensor.matmul_mx(
-                out=bank[:],
-                lhsT=v2_codes[b][:, o * P : (o + 1) * P].bitcast(FP8X4),
-                lhsT_scale=v2_plane[TAB2_PLANE:P, i * P : (i + 1) * P],
-                rhs=h_codes[half][:].bitcast(FP8X4),
-                rhs_scale=h_plane[half][:],
-                start=True,
-                stop=True,
-            )
+            width = HALF // len(tiles)
+            first = (0, HALF, HALF + HALF // 2)[piece]
+            for m, i in enumerate(tiles):
+                b, o = divmod(i, PER_HALF)
+                nc.tensor.matmul_mx(
+                    out=bank[:, m * width : (m + 1) * width],
+                    lhsT=v2_codes[b][:, o * P : (o + 1) * P].bitcast(FP8X4),
+                    lhsT_scale=v2_plane[TAB2_PLANE:P, i * P : (i + 1) * P],
+                    rhs=h_codes[piece][:].bitcast(FP8X4),
+                    rhs_scale=h_plane[piece][:],
+                    start=True,
+                    stop=True,
+                )
             nc.scalar.activation(out=squared[n][:], in_=bank[:], func=ACT.Square, bias=1.0)
-            if n < GPSIMD_TILES:
-                nc.gpsimd.tensor_scalar(
-                    out=result[n][:], in0=squared[n][:], scalar1=alpha_cols[:, i : i + 1], scalar2=0.0, op0=MULT, op1=ADD
-                )
-            else:
-                nc.vector.tensor_scalar(
-                    out=result[n][:], in0=squared[n][:], scalar1=alpha_cols[:, i : i + 1], scalar2=None, op0=MULT
-                )
-            nc.sync.dma_start(out=out[i * P : (i + 1) * P, half * HALF : (half + 1) * HALF], in_=result[n][:])
 
-        gather_tab_whole(0, sbuf("v_codes0", [P, S], U32))
+        def finish(n, piece, tiles):
+            width = HALF // len(tiles)
+            first = (0, HALF, HALF + HALF // 2)[piece]
+            for m, i in enumerate(tiles):
+                columns = slice(m * width, (m + 1) * width)
+                nc.vector.tensor_scalar(
+                    out=result[n][:, columns],
+                    in0=squared[n][:, columns],
+                    scalar1=alpha_cols[:, i : i + 1],
+                    scalar2=None,
+                    op0=MULT,
+                )
+            rows = out[tiles[0] * P : (tiles[-1] + 1) * P, first : first + width]
+            nc.sync.dma_start(
+                out=rows.rearrange("(m p) c -> p m c", p=P),
+                in_=result[n][:].rearrange("p (m c) -> p m c", c=width),
+            )
+
+        def gate_product(c):
+            for a in range(PASSES):
+                gate_pass(c, a)
+            sigmoid(c)
+
+        def value_product(c):
+            for a in range(PASSES):
+                value_pass(c, a)
+
+        gather_tab2_scales()
+        gather_tab(0, 0, sbuf("v_codes0", [P, S], U32))
         ident = sbuf("ident", [P, P], F32, on="tab_window0")
         make_identity(nc, ident[:])
         gather_tab_scales()
-        load_tab(2, placed("tab_window2", [P, T], U32, TAB_LAST_AT))
-        interleave_w1_scalar(0)
-        gate_pass(0)
-        gather_tab_whole(1, placed("v_codes1", [P, S], U32, V_CODES_AT))
         load_w1(2, placed("w1_raw2", [P, PACK, H], F32, W1_LAST_AT))
-        load_tab2()
-        quantise_w1(0)
-        gather_tab2_scales()
-        interleave_w1_scalar(1)
-        gate_pass(1)
-        gather_tab(2, 0)
-        gather_tab(2, 1)
-        gate_pass(2)
-        interleave_w1_vector(2, slice(0, H))
-        quantise_w1(1)
-        for c in range(CHUNKS):
-            sigmoid(c)
-        quantise_w1(2)
+        interleave_w1_scalar(0)
         nc.tensor.transpose(banks[ALPHA_BANK][:, 0:P], alpha_rows[:], ident[:])
         nc.scalar.copy(out=alpha_cols[:], in_=banks[ALPHA_BANK][:, 0:ROW_TILES])
-
+        quantise_w1(0)
+        gather_tab(1, 0, placed("v_codes1", [P, S], U32, V_CODES_AT))
+        load_tab2()
+        interleave_w1_scalar(1)
+        quantise_w1(1)
+        gather_tab(2, 0, sbuf("v_codes2_0", [P, 4 * P], U32))
+        for a in range(PASSES):
+            for c in range(PER_HALF):
+                gate_pass(c, a)
+        for a in range(PASSES - 1):
+            for c in range(PER_HALF):
+                value_pass(c, a)
+        interleave_w1_vector(2, slice(0, VECTOR_COLUMNS))
+        interleave_w1_scalar(2, slice(VECTOR_COLUMNS, H))
+        gather_tab(2, 4, sbuf("v_codes2_4", [P, 2 * P], U32))
+        quantise_w1(2)
+        gather_tab(2, 6, sbuf("v_codes2_6", [P, 2 * P], U32, on="w1_bf16_2"))
         for c in range(PER_HALF):
-            value_pass(c, 0)
-            value_pass(c, 1)
+            sigmoid(c)
         for c in range(PER_HALF):
             value_pass(c, 2)
             gate(c)
-        turn(0, nc.scalar.copy)
-        turn(1, nc.scalar.copy)
-        for c in range(PER_HALF, CHUNKS):
-            for a in reversed(range(PASSES)):
-                value_pass(c, a)
-        gather_tab2(0, on="sig%d" % (PER_HALF - 1))
+            if c % 2:
+                turn(c // 2, nc.scalar.copy)
+        gather_tab2(0, placed("v2_codes0", [P, HALF], U32, SIG_AT + (PER_HALF - 1 - SIG_EARLY) * 4 * H))
         quantise_h(0)
-        out_tile(0)
-        out_tile(1)
+        gather_tab2(1, placed("v2_codes1", [P, HALF], U32, H_TURNED_AT))
+        gate_product(4)
+        gate_product(5)
+        gate_product(6)
+        gate_product(7)
+        out_block(0, 0, [0])
+        finish(0, 0, [0])
+        out_block(1, 0, [1])
+        finish(1, 0, [1])
+        value_product(4)
         gate(4)
+        value_product(5)
         gate(5)
         turn(2, nc.scalar.copy)
-        out_tile(2)
-        out_tile(3)
-        gate(6)
-        gate(7)
-        gather_tab2(1, on="sig7")
-        turn(3, nc.vector.tensor_copy)
         quantise_h(1)
-        for n in range(4, 2 * ROW_TILES):
-            out_tile(n)
+        out_block(2, 0, [2])
+        finish(2, 0, [2])
+        out_block(3, 0, [3])
+        finish(3, 0, [3])
+        out_block(4, 0, [4])
+        finish(4, 0, [4])
+        out_block(5, 0, [5])
+        finish(5, 0, [5])
+        value_product(6)
+        gate(6)
+        value_product(7)
+        gate(7)
+        turn(3, nc.vector.tensor_copy)
+        quantise_h(2)
+        out_block(6, 0, [6])
+        finish(6, 0, [6])
+        out_block(7, 0, [7])
+        finish(7, 0, [7])
+        out_block(8, 1, [0, 1])
+        finish(8, 1, [0, 1])
+        out_block(9, 1, [2, 3])
+        finish(9, 1, [2, 3])
+        out_block(10, 1, [4, 5])
+        finish(10, 1, [4, 5])
+        out_block(11, 1, [6, 7])
+        finish(11, 1, [6, 7])
+        out_block(12, 2, [0, 1])
+        finish(12, 2, [0, 1])
+        out_block(13, 2, [2, 3])
+        finish(13, 2, [2, 3])
+        out_block(14, 2, [4, 5])
+        finish(14, 2, [4, 5])
+        out_block(15, 2, [6, 7])
+        finish(15, 2, [6, 7])

@@ -87,10 +87,9 @@ def tile_list_poly_kernel_contributions_kernel(
         tab_window, tab2_window, w1_raw, w1_codes, w1_plane = {}, {}, {}, {}, {}
         v_codes, v2_codes, h_chunk, h_codes = {}, {}, {}, {}
 
-        nc.gpsimd.memset(tab2_scale_window[:, 0 : T2 // 2].bitcast(I32), 0)
-        nc.vector.memset(tab2_scale_window[:, T2 // 2 : T2].bitcast(I32), 0)
         nc.vector.memset(tab_scale_window[:].bitcast(I32), 0)
         nc.vector.memset(w4_plane[:].rearrange("p a c -> p (a c)").bitcast(I32), 0)
+        nc.vector.memset(tab2_scale_window[:].bitcast(I32), 0)
         nc.vector.memset(alpha_rows[:], 0.0)
         warm = sbuf("warm", [P, 16], F32)
         nc.gpsimd.memset(warm[:, 0:8], 0.0)
@@ -114,12 +113,8 @@ def tile_list_poly_kernel_contributions_kernel(
             words = tab2_words[0].rearrange("p t i -> p (t i)")
             nc.sync.dma_start(out=tab2_window[0][:].bitcast(I32), in_=words.bitcast(I32))
 
-        nc.sync.dma_start(idx2[:], offs2)
         nc.sync.dma_start(idx[:], offs)
-        nc.sync.dma_start(out=w4_codes[:].bitcast(I32), in_=w4_words.bitcast(I32).rearrange("a p c -> p a c"))
-        nc.sync.dma_start(
-            out=tab2_scale_window[TAB2_ROWS_AT:P:TAB2_ROWS_STEP, :].bitcast(I32), in_=tab2_scales[0].bitcast(I32)
-        )
+        nc.sync.dma_start(idx2[:], offs2)
         load_tab(0, sbuf("tab_window0", [P, T], U32))
         load_w1(0, sbuf("w1_raw0", [P, PACK, H], F32))
         for q in range(4):
@@ -128,11 +123,15 @@ def tile_list_poly_kernel_contributions_kernel(
                 in_=tab_scales[:, 4 * q : 4 * q + 4, :].bitcast(I32),
             )
         load_tab(1, placed("tab_window1", [P, T], U32, TAB_MID_AT))
+        nc.sync.dma_start(out=w4_codes[:].bitcast(I32), in_=w4_words.bitcast(I32).rearrange("a p c -> p a c"))
         for q in range(4):
             nc.sync.dma_start(
                 out=w4_plane[QUADRANT * q : QUADRANT * q + 4, :, :].bitcast(I32),
                 in_=w4_scales[:, 4 * q : 4 * q + 4, :].bitcast(I32).rearrange("a s c -> s a c"),
             )
+        nc.sync.dma_start(
+            out=tab2_scale_window[TAB2_ROWS_AT:P:TAB2_ROWS_STEP, :].bitcast(I32), in_=tab2_scales[0].bitcast(I32)
+        )
         load_w1(1, sbuf("w1_raw1", [P, PACK, H], F32))
         load_tab(2, sbuf("tab_window2", [P, T], U32))
         nc.gpsimd.dma_start(out=alpha_rows[0:ROW_TILES, :], in_=alpha.rearrange("(n p) -> n p", p=P))
@@ -158,11 +157,11 @@ def tile_list_poly_kernel_contributions_kernel(
                 )
 
         def gather_tab2_scales():
-            rows = sbuf("v2_scale_rows", [P, S2], U8)
+            rows = placed("v2_scale_rows", [P, S2], U8, TAB_MID_AT + S2)
             nc.vector.tensor_copy(out=rows[:], in_=tab2_scale_window[:].indirect(idx2[:]))
             for q in range(4):
                 first = QUADRANT * q
-                nc.sync.dma_start(
+                nc.gpsimd.dma_start(
                     out=v2_plane[first + TAB2_PLANE : first + TAB2_PLANE + 4, :].bitcast(I32),
                     in_=rows[first + TAB2_ROWS_AT : first + QUADRANT : TAB2_ROWS_STEP, :].bitcast(I32),
                 )
@@ -293,7 +292,6 @@ def tile_list_poly_kernel_contributions_kernel(
             for a in range(PASSES):
                 value_pass(c, a)
 
-        gather_tab2_scales()
         gather_tab(0, 0, sbuf("v_codes0", [P, S], U32))
         ident = sbuf("ident", [P, P], F32, on="tab_window0")
         make_identity(nc, ident[:])
@@ -305,6 +303,7 @@ def tile_list_poly_kernel_contributions_kernel(
         quantise_w1(0)
         gather_tab(1, 0, placed("v_codes1", [P, S], U32, V_CODES_AT))
         load_tab2()
+        gather_tab2_scales()
         interleave_w1_scalar(1)
         quantise_w1(1)
         gather_tab(2, 0, sbuf("v_codes2_0", [P, 4 * P], U32))

@@ -21,16 +21,21 @@ P = 128
 PACK = 4
 K_PASS = P * PACK
 PASSES = K // K_PASS
+LAST = PASSES - 1
+BANK = 512
 HALF = 512
 CHUNKS = S // P
 PER_HALF = HALF // P
 ROW_TILES = S2 // P
+LIST_ROWS = 16
 QUADRANT = 32
 SHIFT_ROWS = 112
-SIG_EARLY = 0
-VECTOR_COLUMNS = 256
 TAB2_ROWS_AT, TAB2_ROWS_STEP = 4, 8
 TAB2_PLANE = 12
+VECTOR_COLUMNS = 320
+PIECES = [(0, HALF), (HALF, HALF // 2), (HALF + HALF // 2, HALF // 2)]
+BLOCKS = [(0, [i]) for i in range(ROW_TILES)]
+BLOCKS = BLOCKS + [(piece, [i, i + 1]) for piece in (1, 2) for i in range(0, ROW_TILES, 2)]
 
 G_BANK = [0, 1, 2, 3, 0, 1, 2, 3]
 A_BANK = [4, 5, 6, 7, 6, 7, 0, 1]
@@ -40,14 +45,15 @@ Y_BANK = [4, 5, 2, 3, 4, 5, 2, 3, 6, 4, 5, 2, 0, 1, 3, 7]
 
 LAP = 64
 WINDOW = 4 * T
+SIG_BYTES = 4 * H
 W1_LAST_AT = 0
 TAB_SCALES_AT = W1_LAST_AT + WINDOW - LAP
-V_CODES_AT = TAB_SCALES_AT + T - LAP
-SIG_AT = W1_LAST_AT
-W1_FIRST_AT = V_CODES_AT + 4 * S - LAP
+V_MID_AT = TAB_SCALES_AT + T - LAP
+W1_FIRST_AT = V_MID_AT + 4 * S - LAP
 TAB_MID_AT = W1_FIRST_AT + 2 * PACK * H
+TAB2_ROWS_TILE_AT = TAB_MID_AT + S2
 TAB2_AT = TAB_MID_AT + WINDOW - LAP
-H_TURNED_AT = TAB2_AT + 4 * T2
+H_FIRST_AT = TAB2_AT + 4 * T2
 
 
 def tile_list_poly_kernel_contributions_kernel(
@@ -65,8 +71,8 @@ def tile_list_poly_kernel_contributions_kernel(
         def placed(name, shape, dtype, offset):
             return shared.tile(shape, dtype, name=name, align_bytes=64, offset=offset)
 
-        idx = keep.tile([P, S // 16], U16, name="idx")
-        idx2 = keep.tile([P, S2 // 16], U16, name="idx2")
+        idx = keep.tile([P, S // LIST_ROWS], U16, name="idx")
+        idx2 = keep.tile([P, S2 // LIST_ROWS], U16, name="idx2")
         tab_scale_window = placed("tab_scale_window", [P, T], U8, TAB_SCALES_AT)
         tab2_scale_window = sbuf("tab2_scale_window", [P, T2], U8)
         w1_bf16 = [placed("w1_bf16_0", [P, H, PACK], BF16, W1_FIRST_AT)]
@@ -77,41 +83,34 @@ def tile_list_poly_kernel_contributions_kernel(
         v2_plane = sbuf("v2_plane", [P, S2], U8)
         alpha_rows = sbuf("alpha_rows", [P, P], F32)
         alpha_cols = sbuf("alpha_cols", [P, ROW_TILES], F32)
-        sig = {}
-        h_turned = [placed("h_turned0", [P, HALF, PACK], BF16, H_TURNED_AT)]
-        h_turned = h_turned + [sbuf("h_turned%d" % b, [P, HALF // 2, PACK], BF16) for b in (1, 2)]
-        h_plane = [sbuf("h_plane%d" % b, [P, HALF // min(b + 1, 2)], U8) for b in range(3)]
-        squared = [sbuf("squared%d" % n, [P, HALF], F32) for n in range(2 * ROW_TILES)]
-        result = [sbuf("result%d" % n, [P, HALF], F32) for n in range(2 * ROW_TILES)]
-        banks = [psum.tile([P, HALF], F32, name="bank%d" % b) for b in range(8)]
-        tab_window, tab2_window, w1_raw, w1_codes, w1_plane = {}, {}, {}, {}, {}
-        v_codes, v2_codes, h_chunk, h_codes = {}, {}, {}, {}
+        h_turned = [placed("h_turned0", [P, HALF, PACK], BF16, H_FIRST_AT)]
+        h_turned = h_turned + [sbuf("h_turned%d" % b, [P, PIECES[b][1], PACK], BF16) for b in (1, 2)]
+        h_plane = [sbuf("h_plane%d" % b, [P, width], U8) for b, (first, width) in enumerate(PIECES)]
+        squared = [sbuf("squared%d" % n, [P, BANK], F32) for n in range(len(BLOCKS))]
+        result = [sbuf("result%d" % n, [P, BANK], F32) for n in range(len(BLOCKS))]
+        banks = [psum.tile([P, BANK], F32, name="bank%d" % b) for b in range(8)]
+        tab_window, w1_raw, w1_codes, w1_plane = {}, {}, {}, {}
+        v_codes, v2_codes, sig, h_chunk, h_codes = {}, {}, {}, {}, {}
 
         nc.vector.memset(tab_scale_window[:].bitcast(I32), 0)
         nc.vector.memset(w4_plane[:].rearrange("p a c -> p (a c)").bitcast(I32), 0)
         nc.vector.memset(tab2_scale_window[:].bitcast(I32), 0)
         nc.vector.memset(alpha_rows[:], 0.0)
-        warm = sbuf("warm", [P, 16], F32)
-        nc.gpsimd.memset(warm[:, 0:8], 0.0)
-        nc.scalar.activation(out=warm[:, 8:16], in_=warm[:, 0:8], func=ACT.Sigmoid)
         for a in range(1, PASSES):
             nc.vector.memset(v_plane[a][:].bitcast(I32), 0)
         nc.vector.memset(v2_plane[:].bitcast(I32), 0)
 
+        def load_words(words, tile):
+            nc.sync.dma_start(out=tile[:].bitcast(I32), in_=words.rearrange("p t i -> p (t i)").bitcast(I32))
+
         def load_tab(a, tile):
             tab_window[a] = tile
-            words = tab_words[a].rearrange("p t i -> p (t i)")
-            nc.sync.dma_start(out=tile[:].bitcast(I32), in_=words.bitcast(I32))
+            load_words(tab_words[a], tile)
 
         def load_w1(a, tile):
             w1_raw[a] = tile
             rows = w1[K_PASS * a : K_PASS * (a + 1), :]
             nc.sync.dma_start(out=tile[:], in_=rows.rearrange("(p t) c -> p t c", t=PACK))
-
-        def load_tab2():
-            tab2_window[0] = placed("tab2_window", [P, T2], U32, TAB2_AT)
-            words = tab2_words[0].rearrange("p t i -> p (t i)")
-            nc.sync.dma_start(out=tab2_window[0][:].bitcast(I32), in_=words.bitcast(I32))
 
         nc.sync.dma_start(idx[:], offs)
         nc.sync.dma_start(idx2[:], offs2)
@@ -133,19 +132,16 @@ def tile_list_poly_kernel_contributions_kernel(
             out=tab2_scale_window[TAB2_ROWS_AT:P:TAB2_ROWS_STEP, :].bitcast(I32), in_=tab2_scales[0].bitcast(I32)
         )
         load_w1(1, sbuf("w1_raw1", [P, PACK, H], F32))
-        load_tab(2, sbuf("tab_window2", [P, T], U32))
+        load_tab(LAST, sbuf("tab_window2", [P, T], U32))
         nc.gpsimd.dma_start(out=alpha_rows[0:ROW_TILES, :], in_=alpha.rearrange("(n p) -> n p", p=P))
 
-        def half_of(offsets, b):
-            columns = HALF // 16
-            return offsets[:, columns * b : columns * (b + 1)]
+        def entries(offsets, first, count):
+            return offsets[:, first // LIST_ROWS : (first + count) // LIST_ROWS]
 
         def gather_tab(a, first, tile):
-            count = tile[:].shape[1] // P
-            columns = P // 16
-            offsets = idx[:, columns * first : columns * (first + count)]
-            nc.vector.tensor_copy(out=tile[:], in_=tab_window[a][:].indirect(offsets))
-            for o in range(count):
+            count = tile[:].shape[1]
+            nc.vector.tensor_copy(out=tile[:], in_=tab_window[a][:].indirect(entries(idx, first * P, count)))
+            for o in range(count // P):
                 v_codes[a, first + o] = tile[:, o * P : (o + 1) * P]
 
         def gather_tab_scales():
@@ -157,7 +153,7 @@ def tile_list_poly_kernel_contributions_kernel(
                 )
 
         def gather_tab2_scales():
-            rows = placed("v2_scale_rows", [P, S2], U8, TAB_MID_AT + S2)
+            rows = placed("v2_scale_rows", [P, S2], U8, TAB2_ROWS_TILE_AT)
             nc.vector.tensor_copy(out=rows[:], in_=tab2_scale_window[:].indirect(idx2[:]))
             for q in range(4):
                 first = QUADRANT * q
@@ -166,26 +162,18 @@ def tile_list_poly_kernel_contributions_kernel(
                     in_=rows[first + TAB2_ROWS_AT : first + QUADRANT : TAB2_ROWS_STEP, :].bitcast(I32),
                 )
 
-        def gather_tab2(b, tile):
-            v2_codes[b] = tile
-            nc.vector.tensor_copy(out=v2_codes[b][:], in_=tab2_window[0][:].indirect(half_of(idx2, b)))
+        def gather_tab2(b, offset):
+            v2_codes[b] = placed("v2_codes%d" % b, [P, HALF], U32, offset)
+            nc.vector.tensor_copy(out=v2_codes[b][:], in_=tab2_window[:].indirect(entries(idx2, b * HALF, HALF)))
 
-        def interleave_w1_scalar(a, columns=slice(0, H)):
-            nc.scalar.copy(
+        def interleave_w1(a, copy, columns=slice(0, H)):
+            copy(
                 out=w1_bf16[a][:, columns, :].rearrange("p (c i) t -> p c t i", i=4),
                 in_=w1_raw[a][:, :, columns].rearrange("p t (c i) -> p c t i", i=4),
             )
 
-        def interleave_w1_vector(a, columns):
-            nc.vector.tensor_copy(
-                out=w1_bf16[a][:, columns, :], in_=w1_raw[a][:, :, columns].rearrange("p t c -> p c t")
-            )
-
-        def quantise_w1(a):
-            if a == 0:
-                w1_codes[a] = sbuf("w1_codes%d" % a, [P, H], U32, on="alpha_rows")
-            else:
-                w1_codes[a] = sbuf("w1_codes%d" % a, [P, H], U32)
+        def quantise_w1(a, on=None):
+            w1_codes[a] = sbuf("w1_codes%d" % a, [P, H], U32, on)
             w1_plane[a] = sbuf("w1_plane%d" % a, [P, H], U8)
             nc.vector.quantize_mx(
                 out=w1_codes[a][:].bitcast(FP8X4),
@@ -193,19 +181,22 @@ def tile_list_poly_kernel_contributions_kernel(
                 in_=w1_bf16[a][:].rearrange("p c t -> p (c t)"),
             )
 
-        def project(bank, c, a, codes, plane, order=tuple(range(PASSES))):
+        def project(bank, c, a, codes, plane):
             nc.tensor.matmul_mx(
                 out=bank[:],
                 lhsT=v_codes[a, c].bitcast(FP8X4),
                 lhsT_scale=v_plane[a][:, c * P : (c + 1) * P],
                 rhs=codes,
                 rhs_scale=plane,
-                start=(a == order[0]),
-                stop=(a == order[-1]),
+                start=(a == 0),
+                stop=(a == LAST),
             )
 
-        def gate_pass(c, a):
+        def g_pass(c, a):
             project(banks[G_BANK[c]], c, a, w4_codes[:, a, :].bitcast(FP4X4), w4_plane[:, a, :])
+
+        def a_pass(c, a):
+            project(banks[A_BANK[c]], c, a, w1_codes[a][:].bitcast(FP8X4), w1_plane[a][:])
 
         def in_word_order(bank):
             return bank[:].rearrange("j (p u e) -> j u p e", u=2, e=2)
@@ -213,15 +204,15 @@ def tile_list_poly_kernel_contributions_kernel(
         def as_stored(tile):
             return tile[:].rearrange("j (u p e) -> j u p e", u=2, e=2)
 
+        def sig_at(c):
+            return W1_LAST_AT + (c - 1) * SIG_BYTES
+
         def sigmoid(c):
-            if SIG_EARLY <= c < PER_HALF:
-                sig[c] = placed("sig%d" % c, [P, H], F32, SIG_AT + (c - SIG_EARLY) * 4 * H)
+            if 1 <= c < PER_HALF:
+                sig[c] = placed("sig%d" % c, [P, H], F32, sig_at(c))
             else:
                 sig[c] = sbuf("sig%d" % c, [P, H], F32)
             nc.scalar.activation(out=as_stored(sig[c]), in_=in_word_order(banks[G_BANK[c]]), func=ACT.Sigmoid)
-
-        def value_pass(c, a):
-            project(banks[A_BANK[c]], c, a, w1_codes[a][:].bitcast(FP8X4), w1_plane[a][:])
 
         def gate(c):
             h_chunk[c] = sbuf("h_chunk%d" % c, [P, H], BF16)
@@ -229,29 +220,37 @@ def tile_list_poly_kernel_contributions_kernel(
                 out=as_stored(h_chunk[c]), in0=in_word_order(banks[A_BANK[c]]), in1=as_stored(sig[c]), op=MULT
             )
 
-        def turn(pair, copy):
+        def turn(pair, piece, first, copy):
             bank = banks[TURN_BANK[pair]]
-            for second in range(2):
+            for second in (1, 0):
                 words = h_chunk[2 * pair + second][:].bitcast(F32)
                 for u in range(2):
                     o = (2 * u + second) * P
                     nc.tensor.transpose(bank[:, o : o + P], words[:, u * P : (u + 1) * P], ident[:])
-            b, o = (0, pair) if pair < 2 else (pair - 1, 0)
-            samples = h_turned[b][:, o * 2 * P : (o + 1) * 2 * P, :].rearrange("p j t -> p (j t)").bitcast(F32)
+            samples = h_turned[piece][:, first : first + 2 * P, :].rearrange("p j t -> p (j t)").bitcast(F32)
             copy(out=samples.rearrange("p (j u) -> p j u", u=2), in_=bank[:].rearrange("p (u j) -> p j u", u=2))
 
-        def quantise_h(b):
-            h_codes[b] = sbuf("h_codes%d" % b, [P, HALF // min(b + 1, 2)], U32)
+        def quantise_h(piece):
+            h_codes[piece] = sbuf("h_codes%d" % piece, [P, PIECES[piece][1]], U32)
             nc.vector.quantize_mx(
-                out=h_codes[b][:].bitcast(FP8X4),
-                scales=h_plane[b][:],
-                in_=h_turned[b][:].rearrange("p j t -> p (j t)"),
+                out=h_codes[piece][:].bitcast(FP8X4),
+                scales=h_plane[piece][:],
+                in_=h_turned[piece][:].rearrange("p j t -> p (j t)"),
             )
 
-        def out_block(n, piece, tiles):
+        def quarter(piece, copy):
+            pair = piece + 1
+            for c in (2 * pair, 2 * pair + 1):
+                for a in range(PASSES):
+                    a_pass(c, a)
+                gate(c)
+            turn(pair, piece, 0, copy)
+            quantise_h(piece)
+
+        def out_block(n):
+            piece, tiles = BLOCKS[n]
+            first, width = PIECES[piece]
             bank = banks[Y_BANK[n]]
-            width = HALF // len(tiles)
-            first = (0, HALF, HALF + HALF // 2)[piece]
             for m, i in enumerate(tiles):
                 b, o = divmod(i, PER_HALF)
                 nc.tensor.matmul_mx(
@@ -264,10 +263,6 @@ def tile_list_poly_kernel_contributions_kernel(
                     stop=True,
                 )
             nc.scalar.activation(out=squared[n][:], in_=bank[:], func=ACT.Square, bias=1.0)
-
-        def finish(n, piece, tiles):
-            width = HALF // len(tiles)
-            first = (0, HALF, HALF + HALF // 2)[piece]
             for m, i in enumerate(tiles):
                 columns = slice(m * width, (m + 1) * width)
                 nc.vector.tensor_scalar(
@@ -283,96 +278,54 @@ def tile_list_poly_kernel_contributions_kernel(
                 in_=result[n][:].rearrange("p (m c) -> p m c", c=width),
             )
 
-        def gate_product(c):
-            for a in range(PASSES):
-                gate_pass(c, a)
-            sigmoid(c)
-
-        def value_product(c):
-            for a in range(PASSES):
-                value_pass(c, a)
-
         gather_tab(0, 0, sbuf("v_codes0", [P, S], U32))
         ident = sbuf("ident", [P, P], F32, on="tab_window0")
         make_identity(nc, ident[:])
         gather_tab_scales()
-        load_w1(2, placed("w1_raw2", [P, PACK, H], F32, W1_LAST_AT))
-        interleave_w1_scalar(0)
+        load_w1(LAST, placed("w1_raw2", [P, PACK, H], F32, W1_LAST_AT))
+        interleave_w1(0, nc.scalar.copy)
         nc.tensor.transpose(banks[ALPHA_BANK][:, 0:P], alpha_rows[:], ident[:])
         nc.scalar.copy(out=alpha_cols[:], in_=banks[ALPHA_BANK][:, 0:ROW_TILES])
-        quantise_w1(0)
-        gather_tab(1, 0, placed("v_codes1", [P, S], U32, V_CODES_AT))
-        load_tab2()
+        quantise_w1(0, on="alpha_rows")
+        gather_tab(1, 0, placed("v_codes1", [P, S], U32, V_MID_AT))
+        tab2_window = placed("tab2_window", [P, T2], U32, TAB2_AT)
+        load_words(tab2_words[0], tab2_window)
         gather_tab2_scales()
-        interleave_w1_scalar(1)
+        interleave_w1(1, nc.scalar.copy)
         quantise_w1(1)
-        gather_tab(2, 0, sbuf("v_codes2_0", [P, 4 * P], U32))
+
+        gather_tab(LAST, 0, sbuf("v_codes2_0", [P, HALF], U32))
         for a in range(PASSES):
             for c in range(PER_HALF):
-                gate_pass(c, a)
-        for a in range(PASSES - 1):
+                g_pass(c, a)
+        for a in range(LAST):
             for c in range(PER_HALF):
-                value_pass(c, a)
-        interleave_w1_vector(2, slice(0, VECTOR_COLUMNS))
-        interleave_w1_scalar(2, slice(VECTOR_COLUMNS, H))
-        gather_tab(2, 4, sbuf("v_codes2_4", [P, 2 * P], U32))
-        quantise_w1(2)
-        gather_tab(2, 6, sbuf("v_codes2_6", [P, 2 * P], U32, on="w1_bf16_2"))
+                a_pass(c, a)
+        interleave_w1(LAST, nc.vector.tensor_copy, slice(0, VECTOR_COLUMNS))
+        interleave_w1(LAST, nc.scalar.copy, slice(VECTOR_COLUMNS, H))
+        gather_tab(LAST, PER_HALF, sbuf("v_codes2_4", [P, 2 * P], U32))
+        quantise_w1(LAST)
+        gather_tab(LAST, PER_HALF + 2, sbuf("v_codes2_6", [P, 2 * P], U32, on="w1_bf16_2"))
         for c in range(PER_HALF):
             sigmoid(c)
-        for c in range(PER_HALF):
-            value_pass(c, 2)
-            gate(c)
-            if c % 2:
-                turn(c // 2, nc.scalar.copy)
-        gather_tab2(0, placed("v2_codes0", [P, HALF], U32, SIG_AT + (PER_HALF - 1 - SIG_EARLY) * 4 * H))
+        for pair in range(PER_HALF // 2):
+            for c in (2 * pair, 2 * pair + 1):
+                a_pass(c, LAST)
+                gate(c)
+            turn(pair, 0, pair * 2 * P, nc.scalar.copy)
+        gather_tab2(0, sig_at(PER_HALF - 1))
         quantise_h(0)
-        gather_tab2(1, placed("v2_codes1", [P, HALF], U32, H_TURNED_AT))
-        gate_product(4)
-        gate_product(5)
-        gate_product(6)
-        gate_product(7)
-        out_block(0, 0, [0])
-        finish(0, 0, [0])
-        out_block(1, 0, [1])
-        finish(1, 0, [1])
-        value_product(4)
-        gate(4)
-        value_product(5)
-        gate(5)
-        turn(2, nc.scalar.copy)
-        quantise_h(1)
-        out_block(2, 0, [2])
-        finish(2, 0, [2])
-        out_block(3, 0, [3])
-        finish(3, 0, [3])
-        out_block(4, 0, [4])
-        finish(4, 0, [4])
-        out_block(5, 0, [5])
-        finish(5, 0, [5])
-        value_product(6)
-        gate(6)
-        value_product(7)
-        gate(7)
-        turn(3, nc.vector.tensor_copy)
-        quantise_h(2)
-        out_block(6, 0, [6])
-        finish(6, 0, [6])
-        out_block(7, 0, [7])
-        finish(7, 0, [7])
-        out_block(8, 1, [0, 1])
-        finish(8, 1, [0, 1])
-        out_block(9, 1, [2, 3])
-        finish(9, 1, [2, 3])
-        out_block(10, 1, [4, 5])
-        finish(10, 1, [4, 5])
-        out_block(11, 1, [6, 7])
-        finish(11, 1, [6, 7])
-        out_block(12, 2, [0, 1])
-        finish(12, 2, [0, 1])
-        out_block(13, 2, [2, 3])
-        finish(13, 2, [2, 3])
-        out_block(14, 2, [4, 5])
-        finish(14, 2, [4, 5])
-        out_block(15, 2, [6, 7])
-        finish(15, 2, [6, 7])
+        gather_tab2(1, H_FIRST_AT)
+
+        for c in range(PER_HALF, CHUNKS):
+            for a in range(PASSES):
+                g_pass(c, a)
+            sigmoid(c)
+        for n in range(0, 2):
+            out_block(n)
+        quarter(1, nc.scalar.copy)
+        for n in range(2, 6):
+            out_block(n)
+        quarter(2, nc.vector.tensor_copy)
+        for n in range(6, len(BLOCKS)):
+            out_block(n)

@@ -32,28 +32,26 @@ QUADRANT = 32
 SHIFT_ROWS = 112
 TAB2_ROWS_AT, TAB2_ROWS_STEP = 4, 8
 TAB2_PLANE = 12
-VECTOR_COLUMNS = 320
-PIECES = [(0, HALF), (HALF, HALF // 2), (HALF + HALF // 2, HALF // 2)]
-BLOCKS = [(0, [i]) for i in range(ROW_TILES)]
-BLOCKS = BLOCKS + [(piece, [i, i + 1]) for piece in (1, 2) for i in range(0, ROW_TILES, 2)]
-
-G_BANK = [0, 1, 2, 3, 0, 1, 2, 3]
-A_BANK = [4, 5, 6, 7, 6, 7, 0, 1]
-TURN_BANK = [4, 5, 6, 7]
-ALPHA_BANK = 7
-Y_BANK = [4, 5, 2, 3, 4, 5, 2, 3, 6, 4, 5, 2, 0, 1, 3, 7]
+VECTOR_COLUMNS = [128, 320, 320]
+PAIRS = CHUNKS // 2
+TURN_BANK = [0, 2, 4, 6]
+BLOCKS = [(i, [half]) for half in range(2) for i in range(ROW_TILES)]
+Y_BANK = [1, 3, 0, 2, 1, 3, 5, 0, 2, 7, 4, 1, 3, 6, 5, 0]
 
 LAP = 64
 WINDOW = 4 * T
 SIG_BYTES = 4 * H
-W1_LAST_AT = 0
-TAB_SCALES_AT = W1_LAST_AT + WINDOW - LAP
+TAB2_SCALES_AT = 0
+V_FIRST_AT = TAB2_SCALES_AT + T2 - LAP
+TAB_LAST_AT = V_FIRST_AT + 4 * HALF
+TAB_SCALES_AT = TAB_LAST_AT + WINDOW
 V_MID_AT = TAB_SCALES_AT + T - LAP
-W1_FIRST_AT = V_MID_AT + 4 * S - LAP
-TAB_MID_AT = W1_FIRST_AT + 2 * PACK * H
-TAB2_ROWS_TILE_AT = TAB_MID_AT + S2
+W1_MID_AT = V_MID_AT + 4 * HALF
+TAB_FIRST_AT = W1_MID_AT + WINDOW - LAP
+W1_LAST_AT = TAB_FIRST_AT + WINDOW - LAP
+TAB_MID_AT = W1_LAST_AT + WINDOW
 TAB2_AT = TAB_MID_AT + WINDOW - LAP
-H_FIRST_AT = TAB2_AT + 4 * T2
+TURNED_AT = TAB2_AT + 4 * T2
 
 
 def tile_list_poly_kernel_contributions_kernel(
@@ -65,37 +63,42 @@ def tile_list_poly_kernel_contributions_kernel(
         shared = ctx.enter_context(tc.tile_pool(name="shared", bufs=1))
         psum = ctx.enter_context(tc.psum_pool(name="psum", bufs=1))
 
-        def sbuf(name, shape, dtype, on=None):
-            return keep.tile(shape, dtype, name=name, tag=on or name, align_bytes=64)
+        def sbuf(name, shape, dtype):
+            return keep.tile(shape, dtype, name=name, align_bytes=64)
 
         def placed(name, shape, dtype, offset):
             return shared.tile(shape, dtype, name=name, align_bytes=64, offset=offset)
 
         idx = keep.tile([P, S // LIST_ROWS], U16, name="idx")
         idx2 = keep.tile([P, S2 // LIST_ROWS], U16, name="idx2")
+        tab2_scale_window = placed("tab2_scale_window", [P, T2], U8, TAB2_SCALES_AT)
         tab_scale_window = placed("tab_scale_window", [P, T], U8, TAB_SCALES_AT)
-        tab2_scale_window = sbuf("tab2_scale_window", [P, T2], U8)
-        w1_bf16 = [placed("w1_bf16_0", [P, H, PACK], BF16, W1_FIRST_AT)]
-        w1_bf16 = w1_bf16 + [sbuf("w1_bf16_%d" % a, [P, H, PACK], BF16) for a in range(1, PASSES)]
+        tab_at = [TAB_FIRST_AT, TAB_MID_AT, TAB_LAST_AT]
+        tab_window = [placed("tab_window%d" % a, [P, T], U32, tab_at[a]) for a in range(PASSES)]
+        tab2_window = placed("tab2_window", [P, T2], U32, TAB2_AT)
+        w1_raw = [sbuf("w1_raw0", [P, PACK, H], F32), placed("w1_raw1", [P, PACK, H], F32, W1_MID_AT)]
+        w1_raw = w1_raw + [placed("w1_raw2", [P, PACK, H], F32, W1_LAST_AT)]
+        w1_bf16 = [sbuf("w1_bf16_%d" % a, [P, H, PACK], BF16) for a in range(PASSES)]
+        w1_codes = [sbuf("w1_codes%d" % a, [P, H], U32) for a in range(PASSES)]
+        w1_plane = [sbuf("w1_plane%d" % a, [P, H], U8) for a in range(PASSES)]
         w4_codes = sbuf("w4_codes", [P, PASSES, 2 * H], U8)
         w4_plane = sbuf("w4_plane", [P, PASSES, H], U8)
         v_plane = [sbuf("v_plane%d" % a, [P, S], U8) for a in range(PASSES)]
+        v2_rows = sbuf("v2_rows", [P, S2], U8)
         v2_plane = sbuf("v2_plane", [P, S2], U8)
-        alpha_rows = sbuf("alpha_rows", [P, P], F32)
         alpha_cols = sbuf("alpha_cols", [P, ROW_TILES], F32)
-        h_turned = [placed("h_turned0", [P, HALF, PACK], BF16, H_FIRST_AT)]
-        h_turned = h_turned + [sbuf("h_turned%d" % b, [P, PIECES[b][1], PACK], BF16) for b in (1, 2)]
-        h_plane = [sbuf("h_plane%d" % b, [P, width], U8) for b, (first, width) in enumerate(PIECES)]
-        squared = [sbuf("squared%d" % n, [P, BANK], F32) for n in range(len(BLOCKS))]
-        result = [sbuf("result%d" % n, [P, BANK], F32) for n in range(len(BLOCKS))]
+        h_codes = [sbuf("h_codes%d" % b, [P, HALF], U32) for b in range(2)]
+        h_plane = [sbuf("h_plane%d" % b, [P, HALF], U8) for b in range(2)]
         banks = [psum.tile([P, BANK], F32, name="bank%d" % b) for b in range(8)]
-        tab_window, w1_raw, w1_codes, w1_plane = {}, {}, {}, {}
-        v_codes, v2_codes, sig, h_chunk, h_codes = {}, {}, {}, {}, {}
+        v_codes, v2_codes, sig, h_chunk, h_turned = {}, {}, {}, {}, {}
 
+        nc.gpsimd.memset(tab2_scale_window[:, 0 : T2 // 2].bitcast(I32), 0)
+        nc.vector.memset(tab2_scale_window[:, T2 // 2 : T2].bitcast(I32), 0)
         nc.vector.memset(tab_scale_window[:].bitcast(I32), 0)
         nc.vector.memset(w4_plane[:].rearrange("p a c -> p (a c)").bitcast(I32), 0)
-        nc.vector.memset(tab2_scale_window[:].bitcast(I32), 0)
-        nc.vector.memset(alpha_rows[:], 0.0)
+        warm = sbuf("warm", [P, 2], F32)
+        nc.gpsimd.memset(warm[:, 0:1], 0.0)
+        nc.scalar.activation(out=warm[:, 1:2], in_=warm[:, 0:1], func=ACT.Sigmoid)
         for a in range(1, PASSES):
             nc.vector.memset(v_plane[a][:].bitcast(I32), 0)
         nc.vector.memset(v2_plane[:].bitcast(I32), 0)
@@ -103,37 +106,35 @@ def tile_list_poly_kernel_contributions_kernel(
         def load_words(words, tile):
             nc.sync.dma_start(out=tile[:].bitcast(I32), in_=words.rearrange("p t i -> p (t i)").bitcast(I32))
 
-        def load_tab(a, tile):
-            tab_window[a] = tile
-            load_words(tab_words[a], tile)
-
-        def load_w1(a, tile):
-            w1_raw[a] = tile
+        def load_w1(a):
             rows = w1[K_PASS * a : K_PASS * (a + 1), :]
-            nc.sync.dma_start(out=tile[:], in_=rows.rearrange("(p t) c -> p t c", t=PACK))
+            nc.sync.dma_start(out=w1_raw[a][:], in_=rows.rearrange("(p t) c -> p t c", t=PACK))
 
-        nc.sync.dma_start(idx[:], offs)
         nc.sync.dma_start(idx2[:], offs2)
-        load_tab(0, sbuf("tab_window0", [P, T], U32))
-        load_w1(0, sbuf("w1_raw0", [P, PACK, H], F32))
+        nc.sync.dma_start(idx[:], offs)
+        nc.sync.dma_start(out=w4_codes[:, 0, :].bitcast(I32), in_=w4_words[0].bitcast(I32))
+        nc.sync.dma_start(
+            out=tab2_scale_window[TAB2_ROWS_AT:P:TAB2_ROWS_STEP, :].bitcast(I32), in_=tab2_scales[0].bitcast(I32)
+        )
+        load_words(tab_words[0], tab_window[0])
+        nc.sync.dma_start(
+            out=w4_codes[:, 1:PASSES, :].bitcast(I32), in_=w4_words[1:PASSES].bitcast(I32).rearrange("a p c -> p a c")
+        )
         for q in range(4):
             nc.sync.dma_start(
                 out=tab_scale_window[QUADRANT * q : QUADRANT * q + 4 * PASSES, :].bitcast(I32),
                 in_=tab_scales[:, 4 * q : 4 * q + 4, :].bitcast(I32),
             )
-        load_tab(1, placed("tab_window1", [P, T], U32, TAB_MID_AT))
-        nc.sync.dma_start(out=w4_codes[:].bitcast(I32), in_=w4_words.bitcast(I32).rearrange("a p c -> p a c"))
+        load_words(tab_words[1], tab_window[1])
         for q in range(4):
             nc.sync.dma_start(
                 out=w4_plane[QUADRANT * q : QUADRANT * q + 4, :, :].bitcast(I32),
                 in_=w4_scales[:, 4 * q : 4 * q + 4, :].bitcast(I32).rearrange("a s c -> s a c"),
             )
-        nc.sync.dma_start(
-            out=tab2_scale_window[TAB2_ROWS_AT:P:TAB2_ROWS_STEP, :].bitcast(I32), in_=tab2_scales[0].bitcast(I32)
-        )
-        load_w1(1, sbuf("w1_raw1", [P, PACK, H], F32))
-        load_tab(LAST, sbuf("tab_window2", [P, T], U32))
-        nc.gpsimd.dma_start(out=alpha_rows[0:ROW_TILES, :], in_=alpha.rearrange("(n p) -> n p", p=P))
+        load_w1(0)
+        load_words(tab_words[LAST], tab_window[LAST])
+        with nc.allow_non_contiguous_dma(reason="one coefficient for each partition and tile of rows"):
+            nc.gpsimd.dma_start(out=alpha_cols[:], in_=alpha.rearrange("(n p) -> p n", p=P))
 
         def entries(offsets, first, count):
             return offsets[:, first // LIST_ROWS : (first + count) // LIST_ROWS]
@@ -153,18 +154,17 @@ def tile_list_poly_kernel_contributions_kernel(
                 )
 
         def gather_tab2_scales():
-            rows = placed("v2_scale_rows", [P, S2], U8, TAB2_ROWS_TILE_AT)
-            nc.vector.tensor_copy(out=rows[:], in_=tab2_scale_window[:].indirect(idx2[:]))
+            nc.vector.tensor_copy(out=v2_rows[:], in_=tab2_scale_window[:].indirect(idx2[:]))
             for q in range(4):
                 first = QUADRANT * q
                 nc.gpsimd.dma_start(
                     out=v2_plane[first + TAB2_PLANE : first + TAB2_PLANE + 4, :].bitcast(I32),
-                    in_=rows[first + TAB2_ROWS_AT : first + QUADRANT : TAB2_ROWS_STEP, :].bitcast(I32),
+                    in_=v2_rows[first + TAB2_ROWS_AT : first + QUADRANT : TAB2_ROWS_STEP, :].bitcast(I32),
                 )
 
-        def gather_tab2(b, offset):
-            v2_codes[b] = placed("v2_codes%d" % b, [P, HALF], U32, offset)
-            nc.vector.tensor_copy(out=v2_codes[b][:], in_=tab2_window[:].indirect(entries(idx2, b * HALF, HALF)))
+        def gather_tab2(b, tile):
+            v2_codes[b] = tile
+            nc.vector.tensor_copy(out=tile[:], in_=tab2_window[:].indirect(entries(idx2, b * HALF, HALF)))
 
         def interleave_w1(a, copy, columns=slice(0, H)):
             copy(
@@ -172,31 +172,35 @@ def tile_list_poly_kernel_contributions_kernel(
                 in_=w1_raw[a][:, :, columns].rearrange("p t (c i) -> p c t i", i=4),
             )
 
-        def quantise_w1(a, on=None):
-            w1_codes[a] = sbuf("w1_codes%d" % a, [P, H], U32, on)
-            w1_plane[a] = sbuf("w1_plane%d" % a, [P, H], U8)
+        def quantise_w1(a):
             nc.vector.quantize_mx(
                 out=w1_codes[a][:].bitcast(FP8X4),
                 scales=w1_plane[a][:],
                 in_=w1_bf16[a][:].rearrange("p c t -> p (c t)"),
             )
 
-        def project(bank, c, a, codes, plane):
+        def project(c, a, codes, plane, start, stop):
             nc.tensor.matmul_mx(
-                out=bank[:],
+                out=banks[c][:],
                 lhsT=v_codes[a, c].bitcast(FP8X4),
                 lhsT_scale=v_plane[a][:, c * P : (c + 1) * P],
                 rhs=codes,
                 rhs_scale=plane,
-                start=(a == 0),
-                stop=(a == LAST),
+                start=start,
+                stop=stop,
             )
 
         def g_pass(c, a):
-            project(banks[G_BANK[c]], c, a, w4_codes[:, a, :].bitcast(FP4X4), w4_plane[:, a, :])
+            project(c, a, w4_codes[:, a, :].bitcast(FP4X4), w4_plane[:, a, :], a == 0, a == LAST)
 
-        def a_pass(c, a):
-            project(banks[A_BANK[c]], c, a, w1_codes[a][:].bitcast(FP8X4), w1_plane[a][:])
+        def a_order(c):
+            if c < PER_HALF:
+                return [0, 1, 2]
+            return [2, 0, 1]
+
+        def a_pass(c, step):
+            a = a_order(c)[step]
+            project(c, a, w1_codes[a][:].bitcast(FP8X4), w1_plane[a][:], step == 0, step == LAST)
 
         def in_word_order(bank):
             return bank[:].rearrange("j (p u e) -> j u p e", u=2, e=2)
@@ -205,127 +209,136 @@ def tile_list_poly_kernel_contributions_kernel(
             return tile[:].rearrange("j (u p e) -> j u p e", u=2, e=2)
 
         def sig_at(c):
-            return W1_LAST_AT + (c - 1) * SIG_BYTES
+            if c < PER_HALF:
+                return W1_MID_AT + (c - 2) * SIG_BYTES
+            return W1_LAST_AT + (c - PER_HALF) * SIG_BYTES
 
         def sigmoid(c):
-            if 1 <= c < PER_HALF:
+            if c >= 2:
                 sig[c] = placed("sig%d" % c, [P, H], F32, sig_at(c))
             else:
                 sig[c] = sbuf("sig%d" % c, [P, H], F32)
-            nc.scalar.activation(out=as_stored(sig[c]), in_=in_word_order(banks[G_BANK[c]]), func=ACT.Sigmoid)
+            nc.scalar.activation(out=as_stored(sig[c]), in_=in_word_order(banks[c]), func=ACT.Sigmoid)
 
         def gate(c):
-            h_chunk[c] = sbuf("h_chunk%d" % c, [P, H], BF16)
+            if c in (PER_HALF, PER_HALF + 1):
+                h_chunk[c] = placed("h_chunk%d" % c, [P, H], BF16, TURNED_AT + (c - PER_HALF) * 2 * H)
+            else:
+                h_chunk[c] = sbuf("h_chunk%d" % c, [P, H], BF16)
             nc.vector.tensor_tensor(
-                out=as_stored(h_chunk[c]), in0=in_word_order(banks[A_BANK[c]]), in1=as_stored(sig[c]), op=MULT
+                out=as_stored(h_chunk[c]), in0=in_word_order(banks[c]), in1=as_stored(sig[c]), op=MULT
             )
 
-        def turn(pair, piece, first, copy):
+        def turn(pair):
             bank = banks[TURN_BANK[pair]]
+            if pair == 1:
+                h_turned[pair] = placed("h_turned1", [P, 2 * P, PACK], BF16, TURNED_AT)
+            else:
+                h_turned[pair] = sbuf("h_turned%d" % pair, [P, 2 * P, PACK], BF16)
             for second in (1, 0):
                 words = h_chunk[2 * pair + second][:].bitcast(F32)
                 for u in range(2):
                     o = (2 * u + second) * P
                     nc.tensor.transpose(bank[:, o : o + P], words[:, u * P : (u + 1) * P], ident[:])
-            samples = h_turned[piece][:, first : first + 2 * P, :].rearrange("p j t -> p (j t)").bitcast(F32)
-            copy(out=samples.rearrange("p (j u) -> p j u", u=2), in_=bank[:].rearrange("p (u j) -> p j u", u=2))
-
-        def quantise_h(piece):
-            h_codes[piece] = sbuf("h_codes%d" % piece, [P, PIECES[piece][1]], U32)
-            nc.vector.quantize_mx(
-                out=h_codes[piece][:].bitcast(FP8X4),
-                scales=h_plane[piece][:],
-                in_=h_turned[piece][:].rearrange("p j t -> p (j t)"),
+            samples = h_turned[pair][:].rearrange("p j t -> p (j t)").bitcast(F32)
+            nc.scalar.copy(
+                out=samples.rearrange("p (j u) -> p j u", u=2), in_=bank[:].rearrange("p (u j) -> p j u", u=2)
             )
 
-        def quarter(piece, copy):
-            pair = piece + 1
-            for c in (2 * pair, 2 * pair + 1):
-                for a in range(PASSES):
-                    a_pass(c, a)
-                gate(c)
-            turn(pair, piece, 0, copy)
-            quantise_h(piece)
+        def quantise_h(pair):
+            b, o = divmod(pair, 2)
+            columns = slice(o * 2 * P, (o + 1) * 2 * P)
+            nc.vector.quantize_mx(
+                out=h_codes[b][:, columns].bitcast(FP8X4),
+                scales=h_plane[b][:, columns],
+                in_=h_turned[pair][:].rearrange("p j t -> p (j t)"),
+            )
 
         def out_block(n):
-            piece, tiles = BLOCKS[n]
-            first, width = PIECES[piece]
-            bank = banks[Y_BANK[n]]
-            for m, i in enumerate(tiles):
-                b, o = divmod(i, PER_HALF)
+            i, halves = BLOCKS[n]
+            first = sum(len(hs) for j, hs in BLOCKS[:n])
+            width = HALF * len(halves)
+            squared = sbuf("squared%d" % n, [P, width], F32)
+            result = sbuf("result%d" % n, [P, width], F32)
+            b, o = divmod(i, PER_HALF)
+            for m, half in enumerate(halves):
+                bank = banks[Y_BANK[first + m]]
                 nc.tensor.matmul_mx(
-                    out=bank[:, m * width : (m + 1) * width],
+                    out=bank[:],
                     lhsT=v2_codes[b][:, o * P : (o + 1) * P].bitcast(FP8X4),
                     lhsT_scale=v2_plane[TAB2_PLANE:P, i * P : (i + 1) * P],
-                    rhs=h_codes[piece][:].bitcast(FP8X4),
-                    rhs_scale=h_plane[piece][:],
+                    rhs=h_codes[half][:].bitcast(FP8X4),
+                    rhs_scale=h_plane[half][:],
                     start=True,
                     stop=True,
                 )
-            nc.scalar.activation(out=squared[n][:], in_=bank[:], func=ACT.Square, bias=1.0)
-            for m, i in enumerate(tiles):
-                columns = slice(m * width, (m + 1) * width)
-                nc.vector.tensor_scalar(
-                    out=result[n][:, columns],
-                    in0=squared[n][:, columns],
-                    scalar1=alpha_cols[:, i : i + 1],
-                    scalar2=None,
-                    op0=MULT,
-                )
-            rows = out[tiles[0] * P : (tiles[-1] + 1) * P, first : first + width]
-            nc.sync.dma_start(
-                out=rows.rearrange("(m p) c -> p m c", p=P),
-                in_=result[n][:].rearrange("p (m c) -> p m c", c=width),
+                nc.scalar.activation(out=squared[:, m * HALF : (m + 1) * HALF], in_=bank[:], func=ACT.Square, bias=1.0)
+            nc.vector.tensor_scalar(
+                out=result[:], in0=squared[:], scalar1=alpha_cols[:, i : i + 1], scalar2=None, op0=MULT
             )
+            nc.sync.dma_start(out=out[i * P : (i + 1) * P, halves[0] * HALF : halves[0] * HALF + width], in_=result[:])
 
-        gather_tab(0, 0, sbuf("v_codes0", [P, S], U32))
-        ident = sbuf("ident", [P, P], F32, on="tab_window0")
-        make_identity(nc, ident[:])
-        gather_tab_scales()
-        load_w1(LAST, placed("w1_raw2", [P, PACK, H], F32, W1_LAST_AT))
-        interleave_w1(0, nc.scalar.copy)
-        nc.tensor.transpose(banks[ALPHA_BANK][:, 0:P], alpha_rows[:], ident[:])
-        nc.scalar.copy(out=alpha_cols[:], in_=banks[ALPHA_BANK][:, 0:ROW_TILES])
-        quantise_w1(0, on="alpha_rows")
-        gather_tab(1, 0, placed("v_codes1", [P, S], U32, V_MID_AT))
-        tab2_window = placed("tab2_window", [P, T2], U32, TAB2_AT)
-        load_words(tab2_words[0], tab2_window)
+        def interleave_shared(a):
+            interleave_w1(a, nc.vector.tensor_copy, slice(0, VECTOR_COLUMNS[a]))
+            interleave_w1(a, nc.scalar.copy, slice(VECTOR_COLUMNS[a], H))
+            quantise_w1(a)
+
+        def project_a(c):
+            for step in range(PASSES):
+                a_pass(c, step)
+
         gather_tab2_scales()
-        interleave_w1(1, nc.scalar.copy)
-        quantise_w1(1)
-
-        gather_tab(LAST, 0, sbuf("v_codes2_0", [P, HALF], U32))
+        ident = placed("ident", [P, P], F32, TAB2_SCALES_AT)
+        make_identity(nc, ident[:])
+        gather_tab(0, 0, placed("v_codes0_0", [P, HALF], U32, V_FIRST_AT))
+        gather_tab_scales()
+        gather_tab(0, PER_HALF, placed("v_codes0_1", [P, HALF], U32, V_MID_AT))
+        load_w1(1)
+        load_w1(LAST)
+        for b in range(2):
+            gather_tab(1, b * PER_HALF, sbuf("v_codes1_%d" % b, [P, HALF], U32))
+        load_words(tab2_words[0], tab2_window)
+        interleave_shared(0)
+        for pair in range(PAIRS):
+            gather_tab(LAST, 2 * pair, sbuf("v_codes2_%d" % pair, [P, 2 * P], U32))
         for a in range(PASSES):
-            for c in range(PER_HALF):
+            for c in range(CHUNKS):
                 g_pass(c, a)
-        for a in range(LAST):
-            for c in range(PER_HALF):
-                a_pass(c, a)
-        interleave_w1(LAST, nc.vector.tensor_copy, slice(0, VECTOR_COLUMNS))
-        interleave_w1(LAST, nc.scalar.copy, slice(VECTOR_COLUMNS, H))
-        gather_tab(LAST, PER_HALF, sbuf("v_codes2_4", [P, 2 * P], U32))
-        quantise_w1(LAST)
-        gather_tab(LAST, PER_HALF + 2, sbuf("v_codes2_6", [P, 2 * P], U32, on="w1_bf16_2"))
-        for c in range(PER_HALF):
+        for c in range(2):
             sigmoid(c)
-        for pair in range(PER_HALF // 2):
-            for c in (2 * pair, 2 * pair + 1):
-                a_pass(c, LAST)
-                gate(c)
-            turn(pair, 0, pair * 2 * P, nc.scalar.copy)
-        gather_tab2(0, sig_at(PER_HALF - 1))
-        quantise_h(0)
-        gather_tab2(1, H_FIRST_AT)
-
+        interleave_shared(1)
+        for c in range(2, PER_HALF):
+            sigmoid(c)
+        interleave_shared(LAST)
         for c in range(PER_HALF, CHUNKS):
-            for a in range(PASSES):
-                g_pass(c, a)
             sigmoid(c)
-        for n in range(0, 2):
-            out_block(n)
-        quarter(1, nc.scalar.copy)
-        for n in range(2, 6):
-            out_block(n)
-        quarter(2, nc.vector.tensor_copy)
-        for n in range(6, len(BLOCKS)):
+        for c in range(PER_HALF):
+            for step in range(LAST):
+                a_pass(c, step)
+        for c in range(PER_HALF):
+            a_pass(c, LAST)
+            gate(c)
+        turn(0)
+        turn(1)
+        quantise_h(0)
+        gather_tab2(0, sbuf("v2_codes0", [P, HALF], U32))
+        quantise_h(1)
+        project_a(4)
+        project_a(5)
+        gate(4)
+        gate(5)
+        out_block(0)
+        gather_tab2(1, placed("v2_codes1", [P, HALF], U32, sig_at(PER_HALF + 1)))
+        out_block(1)
+        turn(2)
+        out_block(2)
+        for c in (6, 7):
+            project_a(c)
+            gate(c)
+        turn(3)
+        out_block(3)
+        quantise_h(2)
+        out_block(4)
+        quantise_h(3)
+        for n in range(5, len(BLOCKS)):
             out_block(n)

@@ -32,7 +32,7 @@ QUADRANT = 32
 SHIFT_ROWS = 112
 TAB2_ROWS_AT, TAB2_ROWS_STEP = 4, 8
 TAB2_PLANE = 12
-VECTOR_COLUMNS = [128, 320, 320]
+VECTOR_COLUMNS = [128, 224, 320]
 PAIRS = CHUNKS // 2
 TURN_BANK = [0, 2, 4, 6]
 BLOCKS = [(i, [half]) for half in range(2) for i in range(ROW_TILES)]
@@ -52,6 +52,7 @@ W1_LAST_AT = TAB_FIRST_AT + WINDOW - LAP
 TAB_MID_AT = W1_LAST_AT + WINDOW
 TAB2_AT = TAB_MID_AT + WINDOW - LAP
 TURNED_AT = TAB2_AT + 4 * T2
+W1_BF16_AT = TURNED_AT + 2 * PACK * 2 * P
 
 
 def tile_list_poly_kernel_contributions_kernel(
@@ -78,7 +79,8 @@ def tile_list_poly_kernel_contributions_kernel(
         tab2_window = placed("tab2_window", [P, T2], U32, TAB2_AT)
         w1_raw = [sbuf("w1_raw0", [P, PACK, H], F32), placed("w1_raw1", [P, PACK, H], F32, W1_MID_AT)]
         w1_raw = w1_raw + [placed("w1_raw2", [P, PACK, H], F32, W1_LAST_AT)]
-        w1_bf16 = [sbuf("w1_bf16_%d" % a, [P, H, PACK], BF16) for a in range(PASSES)]
+        w1_bf16 = [sbuf("w1_bf16_%d" % a, [P, H, PACK], BF16) for a in range(LAST)]
+        w1_bf16 = w1_bf16 + [placed("w1_bf16_2", [P, H, PACK], BF16, W1_BF16_AT)]
         w1_codes = [sbuf("w1_codes%d" % a, [P, H], U32) for a in range(PASSES)]
         w1_plane = [sbuf("w1_plane%d" % a, [P, H], U8) for a in range(PASSES)]
         w4_codes = sbuf("w4_codes", [P, PASSES, 2 * H], U8)
@@ -86,6 +88,7 @@ def tile_list_poly_kernel_contributions_kernel(
         v_plane = [sbuf("v_plane%d" % a, [P, S], U8) for a in range(PASSES)]
         v2_rows = sbuf("v2_rows", [P, S2], U8)
         v2_plane = sbuf("v2_plane", [P, S2], U8)
+        alpha_rows = sbuf("alpha_rows", [P, P], F32)
         alpha_cols = sbuf("alpha_cols", [P, ROW_TILES], F32)
         h_codes = [sbuf("h_codes%d" % b, [P, HALF], U32) for b in range(2)]
         h_plane = [sbuf("h_plane%d" % b, [P, HALF], U8) for b in range(2)]
@@ -102,6 +105,7 @@ def tile_list_poly_kernel_contributions_kernel(
         for a in range(1, PASSES):
             nc.vector.memset(v_plane[a][:].bitcast(I32), 0)
         nc.vector.memset(v2_plane[:].bitcast(I32), 0)
+        nc.vector.memset(alpha_rows[:], 0.0)
 
         def load_words(words, tile):
             nc.sync.dma_start(out=tile[:].bitcast(I32), in_=words.rearrange("p t i -> p (t i)").bitcast(I32))
@@ -133,8 +137,7 @@ def tile_list_poly_kernel_contributions_kernel(
             )
         load_w1(0)
         load_words(tab_words[LAST], tab_window[LAST])
-        with nc.allow_non_contiguous_dma(reason="one coefficient for each partition and tile of rows"):
-            nc.gpsimd.dma_start(out=alpha_cols[:], in_=alpha.rearrange("(n p) -> p n", p=P))
+        nc.gpsimd.dma_start(out=alpha_rows[0:ROW_TILES, :], in_=alpha.rearrange("(n p) -> n p", p=P))
 
         def entries(offsets, first, count):
             return offsets[:, first // LIST_ROWS : (first + count) // LIST_ROWS]
@@ -209,15 +212,14 @@ def tile_list_poly_kernel_contributions_kernel(
             return tile[:].rearrange("j (u p e) -> j u p e", u=2, e=2)
 
         def sig_at(c):
-            if c < PER_HALF:
-                return W1_MID_AT + (c - 2) * SIG_BYTES
-            return W1_LAST_AT + (c - PER_HALF) * SIG_BYTES
+            if c < 2:
+                return W1_MID_AT + c * SIG_BYTES
+            if c < 6:
+                return W1_LAST_AT + (c - 2) * SIG_BYTES
+            return W1_BF16_AT + (c - 6) * SIG_BYTES
 
         def sigmoid(c):
-            if c >= 2:
-                sig[c] = placed("sig%d" % c, [P, H], F32, sig_at(c))
-            else:
-                sig[c] = sbuf("sig%d" % c, [P, H], F32)
+            sig[c] = placed("sig%d" % c, [P, H], F32, sig_at(c))
             nc.scalar.activation(out=as_stored(sig[c]), in_=in_word_order(banks[c]), func=ACT.Sigmoid)
 
         def gate(c):
@@ -304,21 +306,25 @@ def tile_list_poly_kernel_contributions_kernel(
         for a in range(PASSES):
             for c in range(CHUNKS):
                 g_pass(c, a)
+        interleave_shared(1)
         for c in range(2):
             sigmoid(c)
-        interleave_shared(1)
-        for c in range(2, PER_HALF):
-            sigmoid(c)
         interleave_shared(LAST)
-        for c in range(PER_HALF, CHUNKS):
+        for c in range(2, CHUNKS):
             sigmoid(c)
-        for c in range(PER_HALF):
+        for c in range(2):
             for step in range(LAST):
                 a_pass(c, step)
-        for c in range(PER_HALF):
+        for c in range(2):
             a_pass(c, LAST)
             gate(c)
+        for c in range(2, PER_HALF):
+            for step in range(PASSES):
+                a_pass(c, step)
+            gate(c)
         turn(0)
+        nc.tensor.transpose(banks[Y_BANK[0]][:, 0:P], alpha_rows[:], ident[:])
+        nc.scalar.copy(out=alpha_cols[:], in_=banks[Y_BANK[0]][:, 0:ROW_TILES])
         turn(1)
         quantise_h(0)
         gather_tab2(0, sbuf("v2_codes0", [P, HALF], U32))

@@ -32,7 +32,8 @@ QUADRANT = 32
 SHIFT_ROWS = 112
 TAB2_ROWS_AT, TAB2_ROWS_STEP = 4, 8
 TAB2_PLANE = 12
-VECTOR_COLUMNS = [128, 224, 320]
+VECTOR_COLUMNS = [160, 512, 320]
+SIG_FREE = 3
 PAIRS = CHUNKS // 2
 TURN_BANK = [0, 2, 4, 6]
 BLOCKS = [(i, [half]) for half in range(2) for i in range(ROW_TILES)]
@@ -42,17 +43,15 @@ LAP = 64
 WINDOW = 4 * T
 SIG_BYTES = 4 * H
 TAB2_SCALES_AT = 0
-V_FIRST_AT = TAB2_SCALES_AT + T2 - LAP
-TAB_LAST_AT = V_FIRST_AT + 4 * HALF
-TAB_SCALES_AT = TAB_LAST_AT + WINDOW
-V_MID_AT = TAB_SCALES_AT + T - LAP
-W1_MID_AT = V_MID_AT + 4 * HALF
-TAB_FIRST_AT = W1_MID_AT + WINDOW - LAP
-W1_LAST_AT = TAB_FIRST_AT + WINDOW - LAP
+W1_MID_AT = TAB2_SCALES_AT + T2
+TAB_SCALES_AT = W1_MID_AT + WINDOW - LAP
+W1_LAST_AT = TAB_SCALES_AT + T - LAP
 TAB_MID_AT = W1_LAST_AT + WINDOW
 TAB2_AT = TAB_MID_AT + WINDOW - LAP
-TURNED_AT = TAB2_AT + 4 * T2
-W1_BF16_AT = TURNED_AT + 2 * PACK * 2 * P
+TURNED_AT = TAB2_AT + 4 * T2 + 2048
+W1_BF16_AT = TURNED_AT + 4 * PACK * 2 * P + 4096
+V2_AT = TAB2_AT
+HOLD = {5: TURNED_AT - 2 * H + LAP, 6: TURNED_AT + LAP, 7: V2_AT}
 
 
 def tile_list_poly_kernel_contributions_kernel(
@@ -74,8 +73,8 @@ def tile_list_poly_kernel_contributions_kernel(
         idx2 = keep.tile([P, S2 // LIST_ROWS], U16, name="idx2")
         tab2_scale_window = placed("tab2_scale_window", [P, T2], U8, TAB2_SCALES_AT)
         tab_scale_window = placed("tab_scale_window", [P, T], U8, TAB_SCALES_AT)
-        tab_at = [TAB_FIRST_AT, TAB_MID_AT, TAB_LAST_AT]
-        tab_window = [placed("tab_window%d" % a, [P, T], U32, tab_at[a]) for a in range(PASSES)]
+        tab_window = [sbuf("tab_window0", [P, T], U32), placed("tab_window1", [P, T], U32, TAB_MID_AT)]
+        tab_window = tab_window + [sbuf("tab_window2", [P, T], U32)]
         tab2_window = placed("tab2_window", [P, T2], U32, TAB2_AT)
         w1_raw = [sbuf("w1_raw0", [P, PACK, H], F32), placed("w1_raw1", [P, PACK, H], F32, W1_MID_AT)]
         w1_raw = w1_raw + [placed("w1_raw2", [P, PACK, H], F32, W1_LAST_AT)]
@@ -93,7 +92,7 @@ def tile_list_poly_kernel_contributions_kernel(
         h_codes = [sbuf("h_codes%d" % b, [P, HALF], U32) for b in range(2)]
         h_plane = [sbuf("h_plane%d" % b, [P, HALF], U8) for b in range(2)]
         banks = [psum.tile([P, BANK], F32, name="bank%d" % b) for b in range(8)]
-        v_codes, v2_codes, sig, h_chunk, h_turned = {}, {}, {}, {}, {}
+        v_codes, v2_codes, sig, h_chunk, h_turned, finish = {}, {}, {}, {}, {}, {}
 
         nc.gpsimd.memset(tab2_scale_window[:, 0 : T2 // 2].bitcast(I32), 0)
         nc.vector.memset(tab2_scale_window[:, T2 // 2 : T2].bitcast(I32), 0)
@@ -197,7 +196,7 @@ def tile_list_poly_kernel_contributions_kernel(
             project(c, a, w4_codes[:, a, :].bitcast(FP4X4), w4_plane[:, a, :], a == 0, a == LAST)
 
         def a_order(c):
-            if c < PER_HALF:
+            if c < SIG_FREE:
                 return [0, 1, 2]
             return [2, 0, 1]
 
@@ -212,19 +211,19 @@ def tile_list_poly_kernel_contributions_kernel(
             return tile[:].rearrange("j (u p e) -> j u p e", u=2, e=2)
 
         def sig_at(c):
-            if c < 2:
-                return W1_MID_AT + c * SIG_BYTES
-            if c < 6:
-                return W1_LAST_AT + (c - 2) * SIG_BYTES
-            return W1_BF16_AT + (c - 6) * SIG_BYTES
+            if c >= SIG_FREE + 4:
+                return W1_BF16_AT + SIG_BYTES
+            if c >= SIG_FREE:
+                return W1_LAST_AT + (c - SIG_FREE) * SIG_BYTES
+            return W1_BF16_AT + 2 * PACK * H + c * SIG_BYTES
 
         def sigmoid(c):
             sig[c] = placed("sig%d" % c, [P, H], F32, sig_at(c))
             nc.scalar.activation(out=as_stored(sig[c]), in_=in_word_order(banks[c]), func=ACT.Sigmoid)
 
         def gate(c):
-            if c in (PER_HALF, PER_HALF + 1):
-                h_chunk[c] = placed("h_chunk%d" % c, [P, H], BF16, TURNED_AT + (c - PER_HALF) * 2 * H)
+            if c >= 5:
+                h_chunk[c] = placed("h_chunk%d" % c, [P, H], BF16, HOLD[c])
             else:
                 h_chunk[c] = sbuf("h_chunk%d" % c, [P, H], BF16)
             nc.vector.tensor_tensor(
@@ -275,14 +274,22 @@ def tile_list_poly_kernel_contributions_kernel(
                     stop=True,
                 )
                 nc.scalar.activation(out=squared[:, m * HALF : (m + 1) * HALF], in_=bank[:], func=ACT.Square, bias=1.0)
+            finish[n] = (squared, result)
+
+        def store_block(n):
+            i, halves = BLOCKS[n]
+            width = HALF * len(halves)
+            squared, result = finish[n]
             nc.vector.tensor_scalar(
                 out=result[:], in0=squared[:], scalar1=alpha_cols[:, i : i + 1], scalar2=None, op0=MULT
             )
             nc.sync.dma_start(out=out[i * P : (i + 1) * P, halves[0] * HALF : halves[0] * HALF + width], in_=result[:])
 
         def interleave_shared(a):
-            interleave_w1(a, nc.vector.tensor_copy, slice(0, VECTOR_COLUMNS[a]))
-            interleave_w1(a, nc.scalar.copy, slice(VECTOR_COLUMNS[a], H))
+            if VECTOR_COLUMNS[a]:
+                interleave_w1(a, nc.vector.tensor_copy, slice(0, VECTOR_COLUMNS[a]))
+            if VECTOR_COLUMNS[a] < H:
+                interleave_w1(a, nc.scalar.copy, slice(VECTOR_COLUMNS[a], H))
             quantise_w1(a)
 
         def project_a(c):
@@ -292,59 +299,75 @@ def tile_list_poly_kernel_contributions_kernel(
         gather_tab2_scales()
         ident = placed("ident", [P, P], F32, TAB2_SCALES_AT)
         make_identity(nc, ident[:])
-        gather_tab(0, 0, placed("v_codes0_0", [P, HALF], U32, V_FIRST_AT))
+        gather_tab(0, 0, sbuf("v_codes0", [P, S], U32))
         gather_tab_scales()
-        gather_tab(0, PER_HALF, placed("v_codes0_1", [P, HALF], U32, V_MID_AT))
         load_w1(1)
         load_w1(LAST)
-        for b in range(2):
-            gather_tab(1, b * PER_HALF, sbuf("v_codes1_%d" % b, [P, HALF], U32))
+        gather_tab(1, 0, sbuf("v_codes1", [P, S], U32))
         load_words(tab2_words[0], tab2_window)
         interleave_shared(0)
-        for pair in range(PAIRS):
+        for pair in range(PAIRS - 1):
             gather_tab(LAST, 2 * pair, sbuf("v_codes2_%d" % pair, [P, 2 * P], U32))
-        for a in range(PASSES):
+        for a in range(LAST):
             for c in range(CHUNKS):
                 g_pass(c, a)
+        for c in range(CHUNKS - 2):
+            g_pass(c, LAST)
+        for c in range(SIG_FREE):
+            sigmoid(c)
         interleave_shared(1)
-        for c in range(2):
-            sigmoid(c)
         interleave_shared(LAST)
-        for c in range(2, CHUNKS):
+        gather_tab(LAST, CHUNKS - 2, placed("v_codes2_3", [P, 2 * P], U32, W1_BF16_AT))
+        for c in range(SIG_FREE, CHUNKS - 2):
             sigmoid(c)
-        for c in range(2):
-            for step in range(LAST):
+        for step in range(LAST):
+            for c in range(SIG_FREE):
                 a_pass(c, step)
-        for c in range(2):
+        for c in range(SIG_FREE):
             a_pass(c, LAST)
             gate(c)
-        for c in range(2, PER_HALF):
-            for step in range(PASSES):
-                a_pass(c, step)
+        for c in range(SIG_FREE, PER_HALF):
+            project_a(c)
             gate(c)
+        project_a(4)
+        gate(4)
         turn(0)
         nc.tensor.transpose(banks[Y_BANK[0]][:, 0:P], alpha_rows[:], ident[:])
         nc.scalar.copy(out=alpha_cols[:], in_=banks[Y_BANK[0]][:, 0:ROW_TILES])
         turn(1)
+        gather_tab2(0, placed("v2_codes0", [P, HALF], U32, sig_at(PER_HALF - 1)))
         quantise_h(0)
-        gather_tab2(0, sbuf("v2_codes0", [P, HALF], U32))
         quantise_h(1)
-        project_a(4)
+        for c in range(CHUNKS - 2, CHUNKS):
+            g_pass(c, LAST)
+            sigmoid(c)
         project_a(5)
-        gate(4)
-        gate(5)
         out_block(0)
-        gather_tab2(1, placed("v2_codes1", [P, HALF], U32, sig_at(PER_HALF + 1)))
         out_block(1)
-        turn(2)
+        project_a(6)
         out_block(2)
-        for c in (6, 7):
-            project_a(c)
-            gate(c)
-        turn(3)
         out_block(3)
-        quantise_h(2)
+        project_a(7)
+        gate(5)
+        gate(6)
+        gather_tab2(1, placed("v2_codes1", [P, HALF], U32, TURNED_AT + 2048 - LAP))
+        turn(2)
+        store_block(0)
+        gate(7)
         out_block(4)
+        out_block(5)
+        turn(3)
+        store_block(1)
+        store_block(2)
+        store_block(3)
+        quantise_h(2)
+        out_block(6)
+        out_block(7)
         quantise_h(3)
-        for n in range(5, len(BLOCKS)):
+        store_block(4)
+        store_block(5)
+        store_block(6)
+        store_block(7)
+        for n in range(8, len(BLOCKS)):
             out_block(n)
+            store_block(n)

@@ -35,9 +35,10 @@ TAB2_PLANE = 12
 VECTOR_COLUMNS = [160, 512, 320]
 SIG_FREE = 3
 PAIRS = CHUNKS // 2
-TURN_BANK = [0, 2, 4, 6]
+A_BANK = [0, 1, 2, 3, 4, 3, 0, 2]
+TURN_BANK = [0, 2, 4, 0]
 BLOCKS = [(i, [half]) for half in range(2) for i in range(ROW_TILES)]
-Y_BANK = [1, 3, 0, 2, 1, 3, 5, 0, 2, 7, 4, 1, 3, 6, 5, 0]
+Y_BANK = [1, 5, 6, 7, 1, 2, 1, 0, 3, 4, 5, 6, 7, 2, 1, 0]
 
 LAP = 64
 WINDOW = 4 * T
@@ -98,9 +99,6 @@ def tile_list_poly_kernel_contributions_kernel(
         nc.vector.memset(tab2_scale_window[:, T2 // 2 : T2].bitcast(I32), 0)
         nc.vector.memset(tab_scale_window[:].bitcast(I32), 0)
         nc.vector.memset(w4_plane[:].rearrange("p a c -> p (a c)").bitcast(I32), 0)
-        warm = sbuf("warm", [P, 2], F32)
-        nc.gpsimd.memset(warm[:, 0:1], 0.0)
-        nc.scalar.activation(out=warm[:, 1:2], in_=warm[:, 0:1], func=ACT.Sigmoid)
         for a in range(1, PASSES):
             nc.vector.memset(v_plane[a][:].bitcast(I32), 0)
         nc.vector.memset(v2_plane[:].bitcast(I32), 0)
@@ -181,9 +179,9 @@ def tile_list_poly_kernel_contributions_kernel(
                 in_=w1_bf16[a][:].rearrange("p c t -> p (c t)"),
             )
 
-        def project(c, a, codes, plane, start, stop):
+        def project(bank, c, a, codes, plane, start, stop):
             nc.tensor.matmul_mx(
-                out=banks[c][:],
+                out=bank[:],
                 lhsT=v_codes[a, c].bitcast(FP8X4),
                 lhsT_scale=v_plane[a][:, c * P : (c + 1) * P],
                 rhs=codes,
@@ -193,7 +191,7 @@ def tile_list_poly_kernel_contributions_kernel(
             )
 
         def g_pass(c, a):
-            project(c, a, w4_codes[:, a, :].bitcast(FP4X4), w4_plane[:, a, :], a == 0, a == LAST)
+            project(banks[c], c, a, w4_codes[:, a, :].bitcast(FP4X4), w4_plane[:, a, :], a == 0, a == LAST)
 
         def a_order(c):
             if c < SIG_FREE:
@@ -202,7 +200,7 @@ def tile_list_poly_kernel_contributions_kernel(
 
         def a_pass(c, step):
             a = a_order(c)[step]
-            project(c, a, w1_codes[a][:].bitcast(FP8X4), w1_plane[a][:], step == 0, step == LAST)
+            project(banks[A_BANK[c]], c, a, w1_codes[a][:].bitcast(FP8X4), w1_plane[a][:], step == 0, step == LAST)
 
         def in_word_order(bank):
             return bank[:].rearrange("j (p u e) -> j u p e", u=2, e=2)
@@ -227,7 +225,7 @@ def tile_list_poly_kernel_contributions_kernel(
             else:
                 h_chunk[c] = sbuf("h_chunk%d" % c, [P, H], BF16)
             nc.vector.tensor_tensor(
-                out=as_stored(h_chunk[c]), in0=in_word_order(banks[c]), in1=as_stored(sig[c]), op=MULT
+                out=as_stored(h_chunk[c]), in0=in_word_order(banks[A_BANK[c]]), in1=as_stored(sig[c]), op=MULT
             )
 
         def turn(pair):
@@ -306,19 +304,18 @@ def tile_list_poly_kernel_contributions_kernel(
         gather_tab(1, 0, sbuf("v_codes1", [P, S], U32))
         load_words(tab2_words[0], tab2_window)
         interleave_shared(0)
-        for pair in range(PAIRS - 1):
+        for pair in range(PAIRS):
             gather_tab(LAST, 2 * pair, sbuf("v_codes2_%d" % pair, [P, 2 * P], U32))
         for a in range(LAST):
             for c in range(CHUNKS):
                 g_pass(c, a)
-        for c in range(CHUNKS - 2):
+        for c in range(CHUNKS):
             g_pass(c, LAST)
         for c in range(SIG_FREE):
             sigmoid(c)
         interleave_shared(1)
         interleave_shared(LAST)
-        gather_tab(LAST, CHUNKS - 2, placed("v_codes2_3", [P, 2 * P], U32, W1_BF16_AT))
-        for c in range(SIG_FREE, CHUNKS - 2):
+        for c in range(SIG_FREE, CHUNKS):
             sigmoid(c)
         for step in range(LAST):
             for c in range(SIG_FREE):
@@ -338,16 +335,13 @@ def tile_list_poly_kernel_contributions_kernel(
         gather_tab2(0, placed("v2_codes0", [P, HALF], U32, sig_at(PER_HALF - 1)))
         quantise_h(0)
         quantise_h(1)
-        for c in range(CHUNKS - 2, CHUNKS):
-            g_pass(c, LAST)
-            sigmoid(c)
         project_a(5)
         out_block(0)
         out_block(1)
         project_a(6)
         out_block(2)
-        out_block(3)
         project_a(7)
+        out_block(3)
         gate(5)
         gate(6)
         gather_tab2(1, placed("v2_codes1", [P, HALF], U32, TURNED_AT + 2048 - LAP))
@@ -355,16 +349,16 @@ def tile_list_poly_kernel_contributions_kernel(
         store_block(0)
         gate(7)
         out_block(4)
-        out_block(5)
         turn(3)
+        out_block(5)
         store_block(1)
         store_block(2)
         store_block(3)
         quantise_h(2)
         out_block(6)
         out_block(7)
-        quantise_h(3)
         store_block(4)
+        quantise_h(3)
         store_block(5)
         store_block(6)
         store_block(7)

@@ -95,8 +95,7 @@ def tile_list_poly_kernel_contributions_kernel(
         banks = [psum.tile([P, BANK], F32, name="bank%d" % b) for b in range(8)]
         v_codes, v2_codes, sig, h_chunk, h_turned, finish = {}, {}, {}, {}, {}, {}
 
-        nc.gpsimd.memset(tab2_scale_window[:, 0 : T2 // 2].bitcast(I32), 0)
-        nc.vector.memset(tab2_scale_window[:, T2 // 2 : T2].bitcast(I32), 0)
+        nc.vector.memset(tab2_scale_window[:].bitcast(I32), 0)
         nc.vector.memset(tab_scale_window[:].bitcast(I32), 0)
         nc.vector.memset(w4_plane[:].rearrange("p a c -> p (a c)").bitcast(I32), 0)
         for a in range(1, PASSES):
@@ -113,14 +112,14 @@ def tile_list_poly_kernel_contributions_kernel(
 
         nc.sync.dma_start(idx2[:], offs2)
         nc.sync.dma_start(idx[:], offs)
-        nc.sync.dma_start(out=w4_codes[:, 0, :].bitcast(I32), in_=w4_words[0].bitcast(I32))
+        nc.sync.dma_start(
+            out=w4_codes[:, 0:LAST, :].bitcast(I32), in_=w4_words[0:LAST].bitcast(I32).rearrange("a p c -> p a c")
+        )
         nc.sync.dma_start(
             out=tab2_scale_window[TAB2_ROWS_AT:P:TAB2_ROWS_STEP, :].bitcast(I32), in_=tab2_scales[0].bitcast(I32)
         )
         load_words(tab_words[0], tab_window[0])
-        nc.sync.dma_start(
-            out=w4_codes[:, 1:PASSES, :].bitcast(I32), in_=w4_words[1:PASSES].bitcast(I32).rearrange("a p c -> p a c")
-        )
+        nc.sync.dma_start(out=w4_codes[:, LAST, :].bitcast(I32), in_=w4_words[LAST].bitcast(I32))
         for q in range(4):
             nc.sync.dma_start(
                 out=tab_scale_window[QUADRANT * q : QUADRANT * q + 4 * PASSES, :].bitcast(I32),

@@ -25,34 +25,37 @@ LAST = PASSES - 1
 BANK = 512
 HALF = 512
 CHUNKS = S // P
+PAIRS = CHUNKS // 2
 PER_HALF = HALF // P
 ROW_TILES = S2 // P
+BLOCKS = 2 * ROW_TILES
 LIST_ROWS = 16
-QUADRANT = 32
+QUADRANTS, QUADRANT = 4, 32
 SHIFT_ROWS = 112
 TAB2_ROWS_AT, TAB2_ROWS_STEP = 4, 8
 TAB2_PLANE = 12
-VECTOR_COLUMNS = [160, 512, 320]
-SIG_FREE = 3
-PAIRS = CHUNKS // 2
+VECTOR_FIRST, VECTOR_LAST = 160, 320
+EARLY = 3
+
 A_BANK = [0, 1, 2, 3, 4, 3, 0, 2]
 TURN_BANK = [0, 2, 4, 0]
-BLOCKS = [(i, [half]) for half in range(2) for i in range(ROW_TILES)]
 Y_BANK = [1, 5, 6, 7, 1, 2, 1, 0, 3, 4, 5, 6, 7, 2, 1, 0]
 
 LAP = 64
 WINDOW = 4 * T
 SIG_BYTES = 4 * H
+CHUNK_BYTES = 2 * H
 TAB2_SCALES_AT = 0
 W1_MID_AT = TAB2_SCALES_AT + T2
 TAB_SCALES_AT = W1_MID_AT + WINDOW - LAP
 W1_LAST_AT = TAB_SCALES_AT + T - LAP
 TAB_MID_AT = W1_LAST_AT + WINDOW
 TAB2_AT = TAB_MID_AT + WINDOW - LAP
-TURNED_AT = TAB2_AT + 4 * T2 + 2048
-W1_BF16_AT = TURNED_AT + 4 * PACK * 2 * P + 4096
-V2_AT = TAB2_AT
-HOLD = {5: TURNED_AT - 2 * H + LAP, 6: TURNED_AT + LAP, 7: V2_AT}
+TURNED_AT = TAB2_AT + 4 * T2 + CHUNK_BYTES
+V2_SECOND_AT = TURNED_AT + 2 * CHUNK_BYTES - LAP
+W1_BF16_AT = V2_SECOND_AT + 4 * HALF
+SIG_EARLY_AT = W1_BF16_AT + 2 * PACK * H
+H_CHUNK_AT = {5: TURNED_AT - CHUNK_BYTES + LAP, 6: TURNED_AT + LAP, 7: TAB2_AT}
 
 
 def tile_list_poly_kernel_contributions_kernel(
@@ -74,13 +77,22 @@ def tile_list_poly_kernel_contributions_kernel(
         idx2 = keep.tile([P, S2 // LIST_ROWS], U16, name="idx2")
         tab2_scale_window = placed("tab2_scale_window", [P, T2], U8, TAB2_SCALES_AT)
         tab_scale_window = placed("tab_scale_window", [P, T], U8, TAB_SCALES_AT)
-        tab_window = [sbuf("tab_window0", [P, T], U32), placed("tab_window1", [P, T], U32, TAB_MID_AT)]
-        tab_window = tab_window + [sbuf("tab_window2", [P, T], U32)]
+        tab_window = [
+            sbuf("tab_window0", [P, T], U32),
+            placed("tab_window1", [P, T], U32, TAB_MID_AT),
+            sbuf("tab_window2", [P, T], U32),
+        ]
         tab2_window = placed("tab2_window", [P, T2], U32, TAB2_AT)
-        w1_raw = [sbuf("w1_raw0", [P, PACK, H], F32), placed("w1_raw1", [P, PACK, H], F32, W1_MID_AT)]
-        w1_raw = w1_raw + [placed("w1_raw2", [P, PACK, H], F32, W1_LAST_AT)]
-        w1_bf16 = [sbuf("w1_bf16_%d" % a, [P, H, PACK], BF16) for a in range(LAST)]
-        w1_bf16 = w1_bf16 + [placed("w1_bf16_2", [P, H, PACK], BF16, W1_BF16_AT)]
+        w1_raw = [
+            sbuf("w1_raw0", [P, PACK, H], F32),
+            placed("w1_raw1", [P, PACK, H], F32, W1_MID_AT),
+            placed("w1_raw2", [P, PACK, H], F32, W1_LAST_AT),
+        ]
+        w1_bf16 = [
+            sbuf("w1_bf16_0", [P, H, PACK], BF16),
+            sbuf("w1_bf16_1", [P, H, PACK], BF16),
+            placed("w1_bf16_2", [P, H, PACK], BF16, W1_BF16_AT),
+        ]
         w1_codes = [sbuf("w1_codes%d" % a, [P, H], U32) for a in range(PASSES)]
         w1_plane = [sbuf("w1_plane%d" % a, [P, H], U8) for a in range(PASSES)]
         w4_codes = sbuf("w4_codes", [P, PASSES, 2 * H], U8)
@@ -90,10 +102,10 @@ def tile_list_poly_kernel_contributions_kernel(
         v2_plane = sbuf("v2_plane", [P, S2], U8)
         alpha_rows = sbuf("alpha_rows", [P, P], F32)
         alpha_cols = sbuf("alpha_cols", [P, ROW_TILES], F32)
-        h_codes = [sbuf("h_codes%d" % b, [P, HALF], U32) for b in range(2)]
-        h_plane = [sbuf("h_plane%d" % b, [P, HALF], U8) for b in range(2)]
+        h_codes = [sbuf("h_codes%d" % half, [P, HALF], U32) for half in range(2)]
+        h_plane = [sbuf("h_plane%d" % half, [P, HALF], U8) for half in range(2)]
         banks = [psum.tile([P, BANK], F32, name="bank%d" % b) for b in range(8)]
-        v_codes, v2_codes, sig, h_chunk, h_turned, finish = {}, {}, {}, {}, {}, {}
+        v_codes, v2_codes, sig, h_chunk, h_turned, squared, result = {}, {}, {}, {}, {}, {}, {}
 
         nc.vector.memset(tab2_scale_window[:].bitcast(I32), 0)
         nc.vector.memset(tab_scale_window[:].bitcast(I32), 0)
@@ -120,20 +132,20 @@ def tile_list_poly_kernel_contributions_kernel(
         )
         load_words(tab_words[0], tab_window[0])
         nc.sync.dma_start(out=w4_codes[:, LAST, :].bitcast(I32), in_=w4_words[LAST].bitcast(I32))
-        for q in range(4):
+        for q in range(QUADRANTS):
             nc.sync.dma_start(
                 out=tab_scale_window[QUADRANT * q : QUADRANT * q + 4 * PASSES, :].bitcast(I32),
                 in_=tab_scales[:, 4 * q : 4 * q + 4, :].bitcast(I32),
             )
         load_words(tab_words[1], tab_window[1])
-        for q in range(4):
+        for q in range(QUADRANTS):
             nc.sync.dma_start(
                 out=w4_plane[QUADRANT * q : QUADRANT * q + 4, :, :].bitcast(I32),
                 in_=w4_scales[:, 4 * q : 4 * q + 4, :].bitcast(I32).rearrange("a s c -> s a c"),
             )
+        nc.sync.dma_start(out=alpha_rows[0:ROW_TILES, :], in_=alpha.rearrange("(n p) -> n p", p=P))
         load_w1(0)
         load_words(tab_words[LAST], tab_window[LAST])
-        nc.gpsimd.dma_start(out=alpha_rows[0:ROW_TILES, :], in_=alpha.rearrange("(n p) -> n p", p=P))
 
         def entries(offsets, first, count):
             return offsets[:, first // LIST_ROWS : (first + count) // LIST_ROWS]
@@ -152,24 +164,27 @@ def tile_list_poly_kernel_contributions_kernel(
                     in_=v_plane[0][4 * a : 4 * a + SHIFT_ROWS, :].bitcast(I32),
                 )
 
-        def gather_tab2_scales():
-            nc.vector.tensor_copy(out=v2_rows[:], in_=tab2_scale_window[:].indirect(idx2[:]))
-            for q in range(4):
+        def move_tab2_scales():
+            for q in range(QUADRANTS):
                 first = QUADRANT * q
-                nc.gpsimd.dma_start(
+                nc.sync.dma_start(
                     out=v2_plane[first + TAB2_PLANE : first + TAB2_PLANE + 4, :].bitcast(I32),
                     in_=v2_rows[first + TAB2_ROWS_AT : first + QUADRANT : TAB2_ROWS_STEP, :].bitcast(I32),
                 )
 
-        def gather_tab2(b, tile):
-            v2_codes[b] = tile
-            nc.vector.tensor_copy(out=tile[:], in_=tab2_window[:].indirect(entries(idx2, b * HALF, HALF)))
+        def gather_tab2(b, offset):
+            v2_codes[b] = placed("v2_codes%d" % b, [P, HALF], U32, offset)
+            nc.vector.tensor_copy(out=v2_codes[b][:], in_=tab2_window[:].indirect(entries(idx2, b * HALF, HALF)))
 
-        def interleave_w1(a, copy, columns=slice(0, H)):
+        def interleave_w1(a, copy, columns):
             copy(
                 out=w1_bf16[a][:, columns, :].rearrange("p (c i) t -> p c t i", i=4),
                 in_=w1_raw[a][:, :, columns].rearrange("p t (c i) -> p c t i", i=4),
             )
+
+        def interleave_shared(a, split):
+            interleave_w1(a, nc.vector.tensor_copy, slice(0, split))
+            interleave_w1(a, nc.scalar.copy, slice(split, H))
 
         def quantise_w1(a):
             nc.vector.quantize_mx(
@@ -178,28 +193,26 @@ def tile_list_poly_kernel_contributions_kernel(
                 in_=w1_bf16[a][:].rearrange("p c t -> p (c t)"),
             )
 
-        def project(bank, c, a, codes, plane, start, stop):
+        def project(bank, c, a, codes, plane, step):
             nc.tensor.matmul_mx(
                 out=bank[:],
                 lhsT=v_codes[a, c].bitcast(FP8X4),
                 lhsT_scale=v_plane[a][:, c * P : (c + 1) * P],
                 rhs=codes,
                 rhs_scale=plane,
-                start=start,
-                stop=stop,
+                start=(step == 0),
+                stop=(step == LAST),
             )
 
         def g_pass(c, a):
-            project(banks[c], c, a, w4_codes[:, a, :].bitcast(FP4X4), w4_plane[:, a, :], a == 0, a == LAST)
+            project(banks[c], c, a, w4_codes[:, a, :].bitcast(FP4X4), w4_plane[:, a, :], a)
 
-        def a_order(c):
-            if c < SIG_FREE:
-                return [0, 1, 2]
-            return [2, 0, 1]
+        def a_pass(c, a, step):
+            project(banks[A_BANK[c]], c, a, w1_codes[a][:].bitcast(FP8X4), w1_plane[a][:], step)
 
-        def a_pass(c, step):
-            a = a_order(c)[step]
-            project(banks[A_BANK[c]], c, a, w1_codes[a][:].bitcast(FP8X4), w1_plane[a][:], step == 0, step == LAST)
+        def late_a(c):
+            for step in range(PASSES):
+                a_pass(c, (LAST + step) % PASSES, step)
 
         def in_word_order(bank):
             return bank[:].rearrange("j (p u e) -> j u p e", u=2, e=2)
@@ -208,92 +221,74 @@ def tile_list_poly_kernel_contributions_kernel(
             return tile[:].rearrange("j (u p e) -> j u p e", u=2, e=2)
 
         def sig_at(c):
-            if c >= SIG_FREE + 4:
-                return W1_BF16_AT + SIG_BYTES
-            if c >= SIG_FREE:
-                return W1_LAST_AT + (c - SIG_FREE) * SIG_BYTES
-            return W1_BF16_AT + 2 * PACK * H + c * SIG_BYTES
+            if c < EARLY:
+                return SIG_EARLY_AT + c * SIG_BYTES
+            if c < CHUNKS - 1:
+                return W1_LAST_AT + (c - EARLY) * SIG_BYTES
+            return W1_BF16_AT
 
         def sigmoid(c):
             sig[c] = placed("sig%d" % c, [P, H], F32, sig_at(c))
             nc.scalar.activation(out=as_stored(sig[c]), in_=in_word_order(banks[c]), func=ACT.Sigmoid)
 
         def gate(c):
-            if c >= 5:
-                h_chunk[c] = placed("h_chunk%d" % c, [P, H], BF16, HOLD[c])
+            if c in H_CHUNK_AT:
+                h_chunk[c] = placed("h_chunk%d" % c, [P, H], BF16, H_CHUNK_AT[c])
             else:
                 h_chunk[c] = sbuf("h_chunk%d" % c, [P, H], BF16)
             nc.vector.tensor_tensor(
                 out=as_stored(h_chunk[c]), in0=in_word_order(banks[A_BANK[c]]), in1=as_stored(sig[c]), op=MULT
             )
 
-        def turn(pair):
+        def turn(pair, tile):
+            h_turned[pair] = tile
             bank = banks[TURN_BANK[pair]]
-            if pair == 1:
-                h_turned[pair] = placed("h_turned1", [P, 2 * P, PACK], BF16, TURNED_AT)
-            else:
-                h_turned[pair] = sbuf("h_turned%d" % pair, [P, 2 * P, PACK], BF16)
             for second in (1, 0):
                 words = h_chunk[2 * pair + second][:].bitcast(F32)
                 for u in range(2):
                     o = (2 * u + second) * P
                     nc.tensor.transpose(bank[:, o : o + P], words[:, u * P : (u + 1) * P], ident[:])
-            samples = h_turned[pair][:].rearrange("p j t -> p (j t)").bitcast(F32)
+            samples = tile[:].rearrange("p j t -> p (j t)").bitcast(F32)
             nc.scalar.copy(
                 out=samples.rearrange("p (j u) -> p j u", u=2), in_=bank[:].rearrange("p (u j) -> p j u", u=2)
             )
 
         def quantise_h(pair):
-            b, o = divmod(pair, 2)
+            half, o = divmod(pair, 2)
             columns = slice(o * 2 * P, (o + 1) * 2 * P)
             nc.vector.quantize_mx(
-                out=h_codes[b][:, columns].bitcast(FP8X4),
-                scales=h_plane[b][:, columns],
+                out=h_codes[half][:, columns].bitcast(FP8X4),
+                scales=h_plane[half][:, columns],
                 in_=h_turned[pair][:].rearrange("p j t -> p (j t)"),
             )
 
-        def out_block(n):
-            i, halves = BLOCKS[n]
-            first = sum(len(hs) for j, hs in BLOCKS[:n])
-            width = HALF * len(halves)
-            squared = sbuf("squared%d" % n, [P, width], F32)
-            result = sbuf("result%d" % n, [P, width], F32)
+        def square(n):
+            half, i = divmod(n, ROW_TILES)
             b, o = divmod(i, PER_HALF)
-            for m, half in enumerate(halves):
-                bank = banks[Y_BANK[first + m]]
-                nc.tensor.matmul_mx(
-                    out=bank[:],
-                    lhsT=v2_codes[b][:, o * P : (o + 1) * P].bitcast(FP8X4),
-                    lhsT_scale=v2_plane[TAB2_PLANE:P, i * P : (i + 1) * P],
-                    rhs=h_codes[half][:].bitcast(FP8X4),
-                    rhs_scale=h_plane[half][:],
-                    start=True,
-                    stop=True,
-                )
-                nc.scalar.activation(out=squared[:, m * HALF : (m + 1) * HALF], in_=bank[:], func=ACT.Square, bias=1.0)
-            finish[n] = (squared, result)
-
-        def store_block(n):
-            i, halves = BLOCKS[n]
-            width = HALF * len(halves)
-            squared, result = finish[n]
-            nc.vector.tensor_scalar(
-                out=result[:], in0=squared[:], scalar1=alpha_cols[:, i : i + 1], scalar2=None, op0=MULT
+            bank = banks[Y_BANK[n]]
+            squared[n] = sbuf("squared%d" % n, [P, HALF], F32)
+            result[n] = sbuf("result%d" % n, [P, HALF], F32)
+            nc.tensor.matmul_mx(
+                out=bank[:],
+                lhsT=v2_codes[b][:, o * P : (o + 1) * P].bitcast(FP8X4),
+                lhsT_scale=v2_plane[TAB2_PLANE:P, i * P : (i + 1) * P],
+                rhs=h_codes[half][:].bitcast(FP8X4),
+                rhs_scale=h_plane[half][:],
+                start=True,
+                stop=True,
             )
-            nc.sync.dma_start(out=out[i * P : (i + 1) * P, halves[0] * HALF : halves[0] * HALF + width], in_=result[:])
+            nc.scalar.activation(out=squared[n][:], in_=bank[:], func=ACT.Square, bias=1.0)
 
-        def interleave_shared(a):
-            if VECTOR_COLUMNS[a]:
-                interleave_w1(a, nc.vector.tensor_copy, slice(0, VECTOR_COLUMNS[a]))
-            if VECTOR_COLUMNS[a] < H:
-                interleave_w1(a, nc.scalar.copy, slice(VECTOR_COLUMNS[a], H))
-            quantise_w1(a)
+        def store(n):
+            half, i = divmod(n, ROW_TILES)
+            nc.vector.tensor_scalar(
+                out=result[n][:], in0=squared[n][:], scalar1=alpha_cols[:, i : i + 1], scalar2=None, op0=MULT
+            )
+            nc.sync.dma_start(out=out[i * P : (i + 1) * P, half * HALF : (half + 1) * HALF], in_=result[n][:])
 
-        def project_a(c):
-            for step in range(PASSES):
-                a_pass(c, step)
+        turned_shape = [P, 2 * P, PACK]
 
-        gather_tab2_scales()
+        nc.vector.tensor_copy(out=v2_rows[:], in_=tab2_scale_window[:].indirect(idx2[:]))
         ident = placed("ident", [P, P], F32, TAB2_SCALES_AT)
         make_identity(nc, ident[:])
         gather_tab(0, 0, sbuf("v_codes0", [P, S], U32))
@@ -302,65 +297,66 @@ def tile_list_poly_kernel_contributions_kernel(
         load_w1(LAST)
         gather_tab(1, 0, sbuf("v_codes1", [P, S], U32))
         load_words(tab2_words[0], tab2_window)
-        interleave_shared(0)
+        move_tab2_scales()
+        interleave_shared(0, VECTOR_FIRST)
+        quantise_w1(0)
         for pair in range(PAIRS):
             gather_tab(LAST, 2 * pair, sbuf("v_codes2_%d" % pair, [P, 2 * P], U32))
-        for a in range(LAST):
+
+        for a in range(PASSES):
             for c in range(CHUNKS):
                 g_pass(c, a)
-        for c in range(CHUNKS):
-            g_pass(c, LAST)
-        for c in range(SIG_FREE):
+        for c in range(EARLY):
             sigmoid(c)
-        interleave_shared(1)
-        interleave_shared(LAST)
-        for c in range(SIG_FREE, CHUNKS):
+        interleave_w1(1, nc.vector.tensor_copy, slice(0, H))
+        quantise_w1(1)
+        interleave_shared(LAST, VECTOR_LAST)
+        quantise_w1(LAST)
+        for c in range(EARLY, CHUNKS):
             sigmoid(c)
-        for step in range(LAST):
-            for c in range(SIG_FREE):
-                a_pass(c, step)
-        for c in range(SIG_FREE):
-            a_pass(c, LAST)
+
+        for a in range(LAST):
+            for c in range(EARLY):
+                a_pass(c, a, a)
+        for c in range(EARLY):
+            a_pass(c, LAST, LAST)
             gate(c)
-        for c in range(SIG_FREE, PER_HALF):
-            project_a(c)
+        for c in range(EARLY, PER_HALF + 1):
+            late_a(c)
             gate(c)
-        project_a(4)
-        gate(4)
-        turn(0)
+        turn(0, sbuf("h_turned0", turned_shape, BF16))
         nc.tensor.transpose(banks[Y_BANK[0]][:, 0:P], alpha_rows[:], ident[:])
         nc.scalar.copy(out=alpha_cols[:], in_=banks[Y_BANK[0]][:, 0:ROW_TILES])
-        turn(1)
-        gather_tab2(0, placed("v2_codes0", [P, HALF], U32, sig_at(PER_HALF - 1)))
+        turn(1, placed("h_turned1", turned_shape, BF16, TURNED_AT))
+        gather_tab2(0, sig_at(PER_HALF - 1))
         quantise_h(0)
         quantise_h(1)
-        project_a(5)
-        out_block(0)
-        out_block(1)
-        project_a(6)
-        out_block(2)
-        project_a(7)
-        out_block(3)
+
+        late_a(5)
+        square(0)
+        square(1)
+        late_a(6)
+        square(2)
+        late_a(7)
+        square(3)
         gate(5)
         gate(6)
-        gather_tab2(1, placed("v2_codes1", [P, HALF], U32, TURNED_AT + 2048 - LAP))
-        turn(2)
-        store_block(0)
+        gather_tab2(1, V2_SECOND_AT)
+        turn(2, sbuf("h_turned2", turned_shape, BF16))
+        store(0)
         gate(7)
-        out_block(4)
-        turn(3)
-        out_block(5)
-        store_block(1)
-        store_block(2)
-        store_block(3)
+        square(4)
+        turn(3, sbuf("h_turned3", turned_shape, BF16))
+        square(5)
+        for n in range(1, PER_HALF):
+            store(n)
         quantise_h(2)
-        out_block(6)
-        out_block(7)
-        store_block(4)
+        square(6)
+        square(7)
+        store(4)
         quantise_h(3)
-        store_block(5)
-        store_block(6)
-        store_block(7)
-        for n in range(8, len(BLOCKS)):
-            out_block(n)
-            store_block(n)
+        for n in range(5, ROW_TILES):
+            store(n)
+        for n in range(ROW_TILES, BLOCKS):
+            square(n)
+            store(n)

@@ -38,8 +38,8 @@ VECTOR_FIRST, VECTOR_LAST = 160, 320
 EARLY = 3
 
 A_BANK = [0, 1, 2, 3, 4, 3, 0, 2]
-TURN_BANK = [0, 2, 4, 0]
-Y_BANK = [1, 5, 6, 7, 1, 2, 1, 0, 3, 4, 5, 6, 7, 2, 1, 0]
+Y_FIRST = [1, 5, 6, 7, 1, 2, 1, 0]
+Y_BANK = Y_FIRST + [3, 4, 5, 6, 7] + Y_FIRST[5:]
 
 LAP = 64
 WINDOW = 4 * T
@@ -107,9 +107,9 @@ def tile_list_poly_kernel_contributions_kernel(
         banks = [psum.tile([P, BANK], F32, name="bank%d" % b) for b in range(8)]
         v_codes, v2_codes, sig, h_chunk, h_turned, squared, result = {}, {}, {}, {}, {}, {}, {}
 
-        nc.vector.memset(tab2_scale_window[:].bitcast(I32), 0)
         nc.vector.memset(tab_scale_window[:].bitcast(I32), 0)
         nc.vector.memset(w4_plane[:].rearrange("p a c -> p (a c)").bitcast(I32), 0)
+        nc.vector.memset(tab2_scale_window[:].bitcast(I32), 0)
         for a in range(1, PASSES):
             nc.vector.memset(v_plane[a][:].bitcast(I32), 0)
         nc.vector.memset(v2_plane[:].bitcast(I32), 0)
@@ -122,16 +122,10 @@ def tile_list_poly_kernel_contributions_kernel(
             rows = w1[K_PASS * a : K_PASS * (a + 1), :]
             nc.sync.dma_start(out=w1_raw[a][:], in_=rows.rearrange("(p t) c -> p t c", t=PACK))
 
-        nc.sync.dma_start(idx2[:], offs2)
         nc.sync.dma_start(idx[:], offs)
-        nc.sync.dma_start(
-            out=w4_codes[:, 0:LAST, :].bitcast(I32), in_=w4_words[0:LAST].bitcast(I32).rearrange("a p c -> p a c")
-        )
-        nc.sync.dma_start(
-            out=tab2_scale_window[TAB2_ROWS_AT:P:TAB2_ROWS_STEP, :].bitcast(I32), in_=tab2_scales[0].bitcast(I32)
-        )
+        nc.sync.dma_start(idx2[:], offs2)
         load_words(tab_words[0], tab_window[0])
-        nc.sync.dma_start(out=w4_codes[:, LAST, :].bitcast(I32), in_=w4_words[LAST].bitcast(I32))
+        nc.sync.dma_start(out=w4_codes[:].bitcast(I32), in_=w4_words.bitcast(I32).rearrange("a p c -> p a c"))
         for q in range(QUADRANTS):
             nc.sync.dma_start(
                 out=tab_scale_window[QUADRANT * q : QUADRANT * q + 4 * PASSES, :].bitcast(I32),
@@ -144,6 +138,9 @@ def tile_list_poly_kernel_contributions_kernel(
                 in_=w4_scales[:, 4 * q : 4 * q + 4, :].bitcast(I32).rearrange("a s c -> s a c"),
             )
         nc.sync.dma_start(out=alpha_rows[0:ROW_TILES, :], in_=alpha.rearrange("(n p) -> n p", p=P))
+        nc.sync.dma_start(
+            out=tab2_scale_window[TAB2_ROWS_AT:P:TAB2_ROWS_STEP, :].bitcast(I32), in_=tab2_scales[0].bitcast(I32)
+        )
         load_w1(0)
         load_words(tab_words[LAST], tab_window[LAST])
 
@@ -242,7 +239,7 @@ def tile_list_poly_kernel_contributions_kernel(
 
         def turn(pair, tile):
             h_turned[pair] = tile
-            bank = banks[TURN_BANK[pair]]
+            bank = banks[A_BANK[2 * pair]]
             for second in (1, 0):
                 words = h_chunk[2 * pair + second][:].bitcast(F32)
                 for u in range(2):
@@ -288,15 +285,15 @@ def tile_list_poly_kernel_contributions_kernel(
 
         turned_shape = [P, 2 * P, PACK]
 
-        nc.vector.tensor_copy(out=v2_rows[:], in_=tab2_scale_window[:].indirect(idx2[:]))
-        ident = placed("ident", [P, P], F32, TAB2_SCALES_AT)
-        make_identity(nc, ident[:])
         gather_tab(0, 0, sbuf("v_codes0", [P, S], U32))
         gather_tab_scales()
         load_w1(1)
         load_w1(LAST)
         gather_tab(1, 0, sbuf("v_codes1", [P, S], U32))
         load_words(tab2_words[0], tab2_window)
+        nc.vector.tensor_copy(out=v2_rows[:], in_=tab2_scale_window[:].indirect(idx2[:]))
+        ident = placed("ident", [P, P], F32, TAB2_SCALES_AT)
+        make_identity(nc, ident[:])
         move_tab2_scales()
         interleave_shared(0, VECTOR_FIRST)
         quantise_w1(0)
@@ -332,12 +329,9 @@ def tile_list_poly_kernel_contributions_kernel(
         quantise_h(0)
         quantise_h(1)
 
-        late_a(5)
-        square(0)
-        square(1)
-        late_a(6)
-        square(2)
-        late_a(7)
+        for n in range(PER_HALF - 1):
+            late_a(PER_HALF + 1 + n)
+            square(n)
         square(3)
         gate(5)
         gate(6)
@@ -347,15 +341,11 @@ def tile_list_poly_kernel_contributions_kernel(
         gate(7)
         square(4)
         turn(3, sbuf("h_turned3", turned_shape, BF16))
-        square(5)
-        for n in range(1, PER_HALF):
-            store(n)
         quantise_h(2)
-        square(6)
-        square(7)
-        store(4)
         quantise_h(3)
         for n in range(5, ROW_TILES):
+            square(n)
+        for n in range(1, ROW_TILES):
             store(n)
         for n in range(ROW_TILES, BLOCKS):
             square(n)

@@ -31,10 +31,11 @@ ROW_TILES = S2 // P
 BLOCKS = 2 * ROW_TILES
 LIST_ROWS = 16
 QUADRANTS, QUADRANT = 4, 32
-SHIFT_ROWS = 112
-TAB2_ROWS_AT, TAB2_ROWS_STEP = 4, 8
+ROWS_STEP = 8
+TAB_ROWS_AT = [0, 4, 2]
+TAB2_ROWS_AT = 4
 TAB2_PLANE = 12
-VECTOR_FIRST, VECTOR_LAST = 160, 320
+VECTOR_LAST = 320
 EARLY = 3
 
 A_BANK = [0, 1, 2, 3, 4, 3, 0, 2]
@@ -97,7 +98,8 @@ def tile_list_poly_kernel_contributions_kernel(
         w1_plane = [sbuf("w1_plane%d" % a, [P, H], U8) for a in range(PASSES)]
         w4_codes = sbuf("w4_codes", [P, PASSES, 2 * H], U8)
         w4_plane = sbuf("w4_plane", [P, PASSES, H], U8)
-        v_plane = [sbuf("v_plane%d" % a, [P, S], U8) for a in range(PASSES)]
+        v_rows = sbuf("v_rows", [P, S], U8)
+        v_plane = sbuf("v_plane", [P, PASSES, S], U8)
         v2_rows = sbuf("v2_rows", [P, S2], U8)
         v2_plane = sbuf("v2_plane", [P, S2], U8)
         alpha_rows = sbuf("alpha_rows", [P, P], F32)
@@ -108,10 +110,9 @@ def tile_list_poly_kernel_contributions_kernel(
         v_codes, v2_codes, sig, h_chunk, h_turned, squared, result = {}, {}, {}, {}, {}, {}, {}
 
         nc.vector.memset(tab_scale_window[:].bitcast(I32), 0)
-        nc.vector.memset(w4_plane[:].rearrange("p a c -> p (a c)").bitcast(I32), 0)
         nc.vector.memset(tab2_scale_window[:].bitcast(I32), 0)
-        for a in range(1, PASSES):
-            nc.vector.memset(v_plane[a][:].bitcast(I32), 0)
+        nc.vector.memset(w4_plane[:].rearrange("p a c -> p (a c)").bitcast(I32), 0)
+        nc.vector.memset(v_plane[:].rearrange("p a c -> p (a c)").bitcast(I32), 0)
         nc.vector.memset(v2_plane[:].bitcast(I32), 0)
         nc.vector.memset(alpha_rows[:], 0.0)
 
@@ -124,25 +125,24 @@ def tile_list_poly_kernel_contributions_kernel(
 
         nc.sync.dma_start(idx[:], offs)
         nc.sync.dma_start(idx2[:], offs2)
-        load_words(tab_words[0], tab_window[0])
-        nc.sync.dma_start(out=w4_codes[:].bitcast(I32), in_=w4_words.bitcast(I32).rearrange("a p c -> p a c"))
-        for q in range(QUADRANTS):
-            nc.sync.dma_start(
-                out=tab_scale_window[QUADRANT * q : QUADRANT * q + 4 * PASSES, :].bitcast(I32),
-                in_=tab_scales[:, 4 * q : 4 * q + 4, :].bitcast(I32),
-            )
-        load_words(tab_words[1], tab_window[1])
-        for q in range(QUADRANTS):
-            nc.sync.dma_start(
-                out=w4_plane[QUADRANT * q : QUADRANT * q + 4, :, :].bitcast(I32),
-                in_=w4_scales[:, 4 * q : 4 * q + 4, :].bitcast(I32).rearrange("a s c -> s a c"),
-            )
-        nc.sync.dma_start(out=alpha_rows[0:ROW_TILES, :], in_=alpha.rearrange("(n p) -> n p", p=P))
+        w4_in = w4_words.bitcast(I32).rearrange("a p c -> p a c")
+        nc.sync.dma_start(out=w4_codes[:, 0, :].bitcast(I32), in_=w4_in[:, 0, :])
         nc.sync.dma_start(
-            out=tab2_scale_window[TAB2_ROWS_AT:P:TAB2_ROWS_STEP, :].bitcast(I32), in_=tab2_scales[0].bitcast(I32)
+            out=tab_scale_window[0 : P : ROWS_STEP // 2, :].bitcast(I32),
+            in_=tab_scales[0:LAST].bitcast(I32).rearrange("a q t -> q a t"),
         )
-        load_w1(0)
-        load_words(tab_words[LAST], tab_window[LAST])
+        nc.sync.dma_start(
+            out=tab_scale_window[TAB_ROWS_AT[LAST] : P : ROWS_STEP, :].bitcast(I32), in_=tab_scales[LAST].bitcast(I32)
+        )
+        load_words(tab_words[0], tab_window[0])
+        nc.sync.dma_start(
+            out=tab2_scale_window[TAB2_ROWS_AT:P:ROWS_STEP, :].bitcast(I32), in_=tab2_scales[0].bitcast(I32)
+        )
+        nc.sync.dma_start(out=w4_codes[:, 1:PASSES, :].bitcast(I32), in_=w4_in[:, 1:PASSES, :])
+        w4_rows = w4_scales.bitcast(I32).rearrange("a (q s) c -> s q a c", s=4)
+        for s in range(4):
+            nc.sync.dma_start(out=w4_plane[s:P:QUADRANT, :, :].bitcast(I32), in_=w4_rows[s])
+        load_words(tab_words[1], tab_window[1])
 
         def entries(offsets, first, count):
             return offsets[:, first // LIST_ROWS : (first + count) // LIST_ROWS]
@@ -153,20 +153,11 @@ def tile_list_poly_kernel_contributions_kernel(
             for o in range(count // P):
                 v_codes[a, first + o] = tile[:, o * P : (o + 1) * P]
 
-        def gather_tab_scales():
-            nc.vector.tensor_copy(out=v_plane[0][:], in_=tab_scale_window[:].indirect(idx[:]))
-            for a in range(1, PASSES):
+        def move_rows(plane, plane_first, rows, rows_first):
+            for s in range(4):
                 nc.sync.dma_start(
-                    out=v_plane[a][0:SHIFT_ROWS, :].bitcast(I32),
-                    in_=v_plane[0][4 * a : 4 * a + SHIFT_ROWS, :].bitcast(I32),
-                )
-
-        def move_tab2_scales():
-            for q in range(QUADRANTS):
-                first = QUADRANT * q
-                nc.sync.dma_start(
-                    out=v2_plane[first + TAB2_PLANE : first + TAB2_PLANE + 4, :].bitcast(I32),
-                    in_=v2_rows[first + TAB2_ROWS_AT : first + QUADRANT : TAB2_ROWS_STEP, :].bitcast(I32),
+                    out=plane[plane_first + s : P : QUADRANT, :].bitcast(I32),
+                    in_=rows[rows_first + ROWS_STEP * s : P : QUADRANT, :].bitcast(I32),
                 )
 
         def gather_tab2(b, offset):
@@ -194,7 +185,7 @@ def tile_list_poly_kernel_contributions_kernel(
             nc.tensor.matmul_mx(
                 out=bank[:],
                 lhsT=v_codes[a, c].bitcast(FP8X4),
-                lhsT_scale=v_plane[a][:, c * P : (c + 1) * P],
+                lhsT_scale=v_plane[:, a, c * P : (c + 1) * P],
                 rhs=codes,
                 rhs_scale=plane,
                 start=(step == 0),
@@ -285,17 +276,23 @@ def tile_list_poly_kernel_contributions_kernel(
 
         turned_shape = [P, 2 * P, PACK]
 
-        gather_tab(0, 0, sbuf("v_codes0", [P, S], U32))
-        gather_tab_scales()
+        nc.vector.tensor_copy(out=v_rows[:], in_=tab_scale_window[:].indirect(idx[:]))
+        move_rows(v_plane[:, 0, :], 0, v_rows, TAB_ROWS_AT[0])
+        nc.sync.dma_start(out=alpha_rows[0:ROW_TILES, :], in_=alpha.rearrange("(n p) -> n p", p=P))
+        load_w1(0)
+        move_rows(v_plane[:, 1, :], 0, v_rows, TAB_ROWS_AT[1])
+        load_words(tab_words[LAST], tab_window[LAST])
+        move_rows(v_plane[:, LAST, :], 0, v_rows, TAB_ROWS_AT[LAST])
         load_w1(1)
         load_w1(LAST)
+        gather_tab(0, 0, sbuf("v_codes0", [P, S], U32))
+        nc.vector.tensor_copy(out=v2_rows[:], in_=tab2_scale_window[:].indirect(idx2[:]))
         gather_tab(1, 0, sbuf("v_codes1", [P, S], U32))
         load_words(tab2_words[0], tab2_window)
-        nc.vector.tensor_copy(out=v2_rows[:], in_=tab2_scale_window[:].indirect(idx2[:]))
         ident = placed("ident", [P, P], F32, TAB2_SCALES_AT)
         make_identity(nc, ident[:])
-        move_tab2_scales()
-        interleave_shared(0, VECTOR_FIRST)
+        move_rows(v2_plane[:], TAB2_PLANE, v2_rows, TAB2_ROWS_AT)
+        interleave_w1(0, nc.scalar.copy, slice(0, H))
         quantise_w1(0)
         for pair in range(PAIRS):
             gather_tab(LAST, 2 * pair, sbuf("v_codes2_%d" % pair, [P, 2 * P], U32))

@@ -32,7 +32,7 @@ BLOCKS = 2 * ROW_TILES
 LIST_ROWS = 16
 QUADRANTS, QUADRANT = 4, 32
 ROWS_STEP = 8
-TAB_ROWS_AT = [0, 4, 2]
+TAB_ROWS_AT = [2, 0, 4]
 TAB2_ROWS_AT = 4
 TAB2_PLANE = 12
 VECTOR_LAST = 320
@@ -56,7 +56,9 @@ TURNED_AT = TAB2_AT + 4 * T2 + CHUNK_BYTES
 V2_SECOND_AT = TURNED_AT + 2 * CHUNK_BYTES - LAP
 W1_BF16_AT = V2_SECOND_AT + 4 * HALF
 SIG_EARLY_AT = W1_BF16_AT + 2 * PACK * H
-H_CHUNK_AT = {5: TURNED_AT - CHUNK_BYTES + LAP, 6: TURNED_AT + LAP, 7: TAB2_AT}
+SQUARED_AT = SIG_EARLY_AT + EARLY * SIG_BYTES
+H_CHUNK_AT = {5: TURNED_AT - CHUNK_BYTES + LAP, 6: SQUARED_AT, 7: SQUARED_AT + 4 * HALF}
+TURN_BANK = [0, 2, 5, 0]
 
 
 def tile_list_poly_kernel_contributions_kernel(
@@ -129,10 +131,10 @@ def tile_list_poly_kernel_contributions_kernel(
         nc.sync.dma_start(out=w4_codes[:, 0, :].bitcast(I32), in_=w4_in[:, 0, :])
         nc.sync.dma_start(
             out=tab_scale_window[0 : P : ROWS_STEP // 2, :].bitcast(I32),
-            in_=tab_scales[0:LAST].bitcast(I32).rearrange("a q t -> q a t"),
+            in_=tab_scales[1:PASSES].bitcast(I32).rearrange("a q t -> q a t"),
         )
         nc.sync.dma_start(
-            out=tab_scale_window[TAB_ROWS_AT[LAST] : P : ROWS_STEP, :].bitcast(I32), in_=tab_scales[LAST].bitcast(I32)
+            out=tab_scale_window[TAB_ROWS_AT[0] : P : ROWS_STEP, :].bitcast(I32), in_=tab_scales[0].bitcast(I32)
         )
         load_words(tab_words[0], tab_window[0])
         nc.sync.dma_start(
@@ -230,7 +232,7 @@ def tile_list_poly_kernel_contributions_kernel(
 
         def turn(pair, tile):
             h_turned[pair] = tile
-            bank = banks[A_BANK[2 * pair]]
+            bank = banks[TURN_BANK[pair]]
             for second in (1, 0):
                 words = h_chunk[2 * pair + second][:].bitcast(F32)
                 for u in range(2):
@@ -254,7 +256,10 @@ def tile_list_poly_kernel_contributions_kernel(
             half, i = divmod(n, ROW_TILES)
             b, o = divmod(i, PER_HALF)
             bank = banks[Y_BANK[n]]
-            squared[n] = sbuf("squared%d" % n, [P, HALF], F32)
+            if n < 2:
+                squared[n] = placed("squared%d" % n, [P, HALF], F32, SQUARED_AT + n * 4 * HALF)
+            else:
+                squared[n] = sbuf("squared%d" % n, [P, HALF], F32)
             result[n] = sbuf("result%d" % n, [P, HALF], F32)
             nc.tensor.matmul_mx(
                 out=bank[:],
@@ -280,9 +285,13 @@ def tile_list_poly_kernel_contributions_kernel(
         move_rows(v_plane[:, 0, :], 0, v_rows, TAB_ROWS_AT[0])
         nc.sync.dma_start(out=alpha_rows[0:ROW_TILES, :], in_=alpha.rearrange("(n p) -> n p", p=P))
         load_w1(0)
-        move_rows(v_plane[:, 1, :], 0, v_rows, TAB_ROWS_AT[1])
+        for q in (0, 2, 1, 3):
+            first = QUADRANT * q
+            nc.sync.dma_start(
+                out=v_plane[first : first + 4, 1:PASSES, :].bitcast(I32),
+                in_=v_rows[first : first + QUADRANT : ROWS_STEP // 2, :].bitcast(I32),
+            )
         load_words(tab_words[LAST], tab_window[LAST])
-        move_rows(v_plane[:, LAST, :], 0, v_rows, TAB_ROWS_AT[LAST])
         load_w1(1)
         load_w1(LAST)
         gather_tab(0, 0, sbuf("v_codes0", [P, S], U32))
@@ -330,19 +339,23 @@ def tile_list_poly_kernel_contributions_kernel(
             late_a(PER_HALF + 1 + n)
             square(n)
         square(3)
-        gate(5)
-        gate(6)
         gather_tab2(1, V2_SECOND_AT)
+        gate(5)
         turn(2, sbuf("h_turned2", turned_shape, BF16))
         store(0)
+        gate(6)
+        store(1)
         gate(7)
         square(4)
         turn(3, sbuf("h_turned3", turned_shape, BF16))
-        quantise_h(2)
-        quantise_h(3)
         for n in range(5, ROW_TILES):
             square(n)
-        for n in range(1, ROW_TILES):
+        store(2)
+        store(3)
+        quantise_h(2)
+        store(4)
+        quantise_h(3)
+        for n in range(5, ROW_TILES):
             store(n)
         for n in range(ROW_TILES, BLOCKS):
             square(n)

@@ -48,8 +48,8 @@ SIG_BYTES = 4 * H
 CHUNK_BYTES = 2 * H
 TAB2_SCALES_AT = 0
 W1_MID_AT = TAB2_SCALES_AT + T2
-TAB_SCALES_AT = W1_MID_AT + WINDOW - LAP
-W1_LAST_AT = TAB_SCALES_AT + T - LAP
+TAB_SCALES_AT = W1_MID_AT + WINDOW
+W1_LAST_AT = TAB_SCALES_AT + T
 TAB_MID_AT = W1_LAST_AT + WINDOW
 TAB2_AT = TAB_MID_AT + WINDOW - LAP
 TURNED_AT = TAB2_AT + 4 * T2 + CHUNK_BYTES
@@ -89,21 +89,23 @@ def tile_list_poly_kernel_contributions_kernel(
         w1_raw = [
             sbuf("w1_raw0", [P, PACK, H], F32),
             placed("w1_raw1", [P, PACK, H], F32, W1_MID_AT),
-            placed("w1_raw2", [P, PACK, H], F32, W1_LAST_AT),
         ]
         w1_bf16 = [
             sbuf("w1_bf16_0", [P, H, PACK], BF16),
             sbuf("w1_bf16_1", [P, H, PACK], BF16),
-            placed("w1_bf16_2", [P, H, PACK], BF16, W1_BF16_AT),
         ]
+        last_raw = [placed("last_raw%d" % b, [P, PACK, H // 2], F32, W1_LAST_AT + b * WINDOW // 2) for b in range(2)]
+        last_bf16 = [placed("last_bf16_%d" % b, [P, H // 2, PACK], BF16, W1_BF16_AT + b * PACK * H) for b in range(2)]
         w1_codes = [sbuf("w1_codes%d" % a, [P, H], U32) for a in range(PASSES)]
         w1_plane = [sbuf("w1_plane%d" % a, [P, H], U8) for a in range(PASSES)]
         w4_codes = sbuf("w4_codes", [P, PASSES, 2 * H], U8)
         w4_plane = sbuf("w4_plane", [P, PASSES, H], U8)
         v_rows = sbuf("v_rows", [P, S], U8)
-        v_plane = sbuf("v_plane", [P, PASSES, S], U8)
+        v_plane_first = sbuf("v_plane_first", [P, S], U8)
+        v_plane_rest = placed("v_plane_rest", [P, LAST, S], U8, TAB_SCALES_AT)
+        v_plane = [v_plane_first[:], v_plane_rest[:, 0, :], v_plane_rest[:, 1, :]]
         v2_rows = sbuf("v2_rows", [P, S2], U8)
-        v2_plane = sbuf("v2_plane", [P, S2], U8)
+        v2_plane = placed("v2_plane", [P, S2], U8, TAB2_SCALES_AT + S2)
         alpha_rows = sbuf("alpha_rows", [P, P], F32)
         alpha_cols = sbuf("alpha_cols", [P, ROW_TILES], F32)
         h_codes = [sbuf("h_codes%d" % half, [P, HALF], U32) for half in range(2)]
@@ -114,8 +116,7 @@ def tile_list_poly_kernel_contributions_kernel(
         nc.vector.memset(tab_scale_window[:].bitcast(I32), 0)
         nc.vector.memset(tab2_scale_window[:].bitcast(I32), 0)
         nc.vector.memset(w4_plane[:].rearrange("p a c -> p (a c)").bitcast(I32), 0)
-        nc.vector.memset(v_plane[:].rearrange("p a c -> p (a c)").bitcast(I32), 0)
-        nc.vector.memset(v2_plane[:].bitcast(I32), 0)
+        nc.vector.memset(v_plane_first[:].bitcast(I32), 0)
         nc.vector.memset(alpha_rows[:], 0.0)
 
         def load_words(words, tile):
@@ -125,10 +126,8 @@ def tile_list_poly_kernel_contributions_kernel(
             rows = w1[K_PASS * a : K_PASS * (a + 1), :]
             nc.sync.dma_start(out=w1_raw[a][:], in_=rows.rearrange("(p t) c -> p t c", t=PACK))
 
+        nc.sync.dma_start(out=w4_codes[:].bitcast(I32), in_=w4_words.bitcast(I32).rearrange("a p c -> p a c"))
         nc.sync.dma_start(idx[:], offs)
-        nc.sync.dma_start(idx2[:], offs2)
-        w4_in = w4_words.bitcast(I32).rearrange("a p c -> p a c")
-        nc.sync.dma_start(out=w4_codes[:, 0, :].bitcast(I32), in_=w4_in[:, 0, :])
         nc.sync.dma_start(
             out=tab_scale_window[0 : P : ROWS_STEP // 2, :].bitcast(I32),
             in_=tab_scales[1:PASSES].bitcast(I32).rearrange("a q t -> q a t"),
@@ -137,10 +136,10 @@ def tile_list_poly_kernel_contributions_kernel(
             out=tab_scale_window[TAB_ROWS_AT[0] : P : ROWS_STEP, :].bitcast(I32), in_=tab_scales[0].bitcast(I32)
         )
         load_words(tab_words[0], tab_window[0])
+        nc.sync.dma_start(idx2[:], offs2)
         nc.sync.dma_start(
             out=tab2_scale_window[TAB2_ROWS_AT:P:ROWS_STEP, :].bitcast(I32), in_=tab2_scales[0].bitcast(I32)
         )
-        nc.sync.dma_start(out=w4_codes[:, 1:PASSES, :].bitcast(I32), in_=w4_in[:, 1:PASSES, :])
         w4_rows = w4_scales.bitcast(I32).rearrange("a (q s) c -> s q a c", s=4)
         for s in range(4):
             nc.sync.dma_start(out=w4_plane[s:P:QUADRANT, :, :].bitcast(I32), in_=w4_rows[s])
@@ -187,7 +186,7 @@ def tile_list_poly_kernel_contributions_kernel(
             nc.tensor.matmul_mx(
                 out=bank[:],
                 lhsT=v_codes[a, c].bitcast(FP8X4),
-                lhsT_scale=v_plane[:, a, c * P : (c + 1) * P],
+                lhsT_scale=v_plane[a][:, c * P : (c + 1) * P],
                 rhs=codes,
                 rhs_scale=plane,
                 start=(step == 0),
@@ -215,7 +214,7 @@ def tile_list_poly_kernel_contributions_kernel(
                 return SIG_EARLY_AT + c * SIG_BYTES
             if c < CHUNKS - 1:
                 return W1_LAST_AT + (c - EARLY) * SIG_BYTES
-            return W1_BF16_AT
+            return W1_BF16_AT + PACK * H
 
         def sigmoid(c):
             sig[c] = placed("sig%d" % c, [P, H], F32, sig_at(c))
@@ -282,18 +281,20 @@ def tile_list_poly_kernel_contributions_kernel(
         turned_shape = [P, 2 * P, PACK]
 
         nc.vector.tensor_copy(out=v_rows[:], in_=tab_scale_window[:].indirect(idx[:]))
-        move_rows(v_plane[:, 0, :], 0, v_rows, TAB_ROWS_AT[0])
+        move_rows(v_plane_first, 0, v_rows, TAB_ROWS_AT[0])
         nc.sync.dma_start(out=alpha_rows[0:ROW_TILES, :], in_=alpha.rearrange("(n p) -> n p", p=P))
         load_w1(0)
         for q in (0, 2, 1, 3):
             first = QUADRANT * q
             nc.sync.dma_start(
-                out=v_plane[first : first + 4, 1:PASSES, :].bitcast(I32),
+                out=v_plane_rest[first : first + 4, :, :].bitcast(I32),
                 in_=v_rows[first : first + QUADRANT : ROWS_STEP // 2, :].bitcast(I32),
             )
         load_words(tab_words[LAST], tab_window[LAST])
         load_w1(1)
-        load_w1(LAST)
+        last_rows = w1[K_PASS * LAST : K, :].rearrange("(p t) c -> p t c", t=PACK)
+        for b in range(2):
+            nc.sync.dma_start(out=last_raw[b][:], in_=last_rows[:, :, b * H // 2 : (b + 1) * H // 2])
         gather_tab(0, 0, sbuf("v_codes0", [P, S], U32))
         nc.vector.tensor_copy(out=v2_rows[:], in_=tab2_scale_window[:].indirect(idx2[:]))
         gather_tab(1, 0, sbuf("v_codes1", [P, S], U32))
@@ -313,8 +314,18 @@ def tile_list_poly_kernel_contributions_kernel(
             sigmoid(c)
         interleave_w1(1, nc.vector.tensor_copy, slice(0, H))
         quantise_w1(1)
-        interleave_shared(LAST, VECTOR_LAST)
-        quantise_w1(LAST)
+        for b, copy in enumerate((nc.scalar.copy, nc.vector.tensor_copy)):
+            copy(
+                out=last_bf16[b][:].rearrange("p (c i) t -> p c t i", i=4),
+                in_=last_raw[b][:].rearrange("p t (c i) -> p c t i", i=4),
+            )
+        for b in range(2):
+            columns = slice(b * H // 2, (b + 1) * H // 2)
+            nc.vector.quantize_mx(
+                out=w1_codes[LAST][:, columns].bitcast(FP8X4),
+                scales=w1_plane[LAST][:, columns],
+                in_=last_bf16[b][:].rearrange("p c t -> p (c t)"),
+            )
         for c in range(EARLY, CHUNKS):
             sigmoid(c)
 

@@ -30,23 +30,26 @@ PER_HALF = HALF // P
 ROW_TILES = S2 // P
 BLOCKS = 2 * ROW_TILES
 LIST_ROWS = 16
-QUADRANTS, QUADRANT = 4, 32
+QUADRANT = 32
 ROWS_STEP = 8
-TAB_ROWS_AT = [2, 0, 4]
+TAB_LAST_ROWS_AT = 2
 TAB2_ROWS_AT = 4
 TAB2_PLANE = 12
-VECTOR_LAST = 320
+W1_HALF = H // 2
 EARLY = 3
 
 A_BANK = [0, 1, 2, 3, 4, 3, 0, 2]
 Y_FIRST = [1, 5, 6, 7, 1, 2, 1, 0]
 Y_BANK = Y_FIRST + [3, 4, 5, 6, 7] + Y_FIRST[5:]
+TURN_BANK = [A_BANK[0], A_BANK[2], Y_BANK[1], A_BANK[6]]
 
 LAP = 64
 WINDOW = 4 * T
 SIG_BYTES = 4 * H
 CHUNK_BYTES = 2 * H
+BLOCK_BYTES = 4 * HALF
 TAB2_SCALES_AT = 0
+TAB2_PLANE_AT = TAB2_SCALES_AT + S2
 W1_MID_AT = TAB2_SCALES_AT + T2
 TAB_SCALES_AT = W1_MID_AT + WINDOW
 W1_LAST_AT = TAB_SCALES_AT + T
@@ -54,11 +57,12 @@ TAB_MID_AT = W1_LAST_AT + WINDOW
 TAB2_AT = TAB_MID_AT + WINDOW - LAP
 TURNED_AT = TAB2_AT + 4 * T2 + CHUNK_BYTES
 V2_SECOND_AT = TURNED_AT + 2 * CHUNK_BYTES - LAP
-W1_BF16_AT = V2_SECOND_AT + 4 * HALF
-SIG_EARLY_AT = W1_BF16_AT + 2 * PACK * H
+W1_BF16_AT = V2_SECOND_AT + BLOCK_BYTES
+HALF_BF16 = 2 * PACK * W1_HALF
+SIG_EARLY_AT = W1_BF16_AT + 2 * HALF_BF16
 SQUARED_AT = SIG_EARLY_AT + EARLY * SIG_BYTES
-H_CHUNK_AT = {5: TURNED_AT - CHUNK_BYTES + LAP, 6: SQUARED_AT, 7: SQUARED_AT + 4 * HALF}
-TURN_BANK = [0, 2, 5, 0]
+HELD = 2
+H_CHUNK_AT = {5: TURNED_AT - CHUNK_BYTES + LAP, 6: SQUARED_AT, 7: SQUARED_AT + BLOCK_BYTES}
 
 
 def tile_list_poly_kernel_contributions_kernel(
@@ -86,26 +90,20 @@ def tile_list_poly_kernel_contributions_kernel(
             sbuf("tab_window2", [P, T], U32),
         ]
         tab2_window = placed("tab2_window", [P, T2], U32, TAB2_AT)
-        w1_raw = [
-            sbuf("w1_raw0", [P, PACK, H], F32),
-            placed("w1_raw1", [P, PACK, H], F32, W1_MID_AT),
-        ]
-        w1_bf16 = [
-            sbuf("w1_bf16_0", [P, H, PACK], BF16),
-            sbuf("w1_bf16_1", [P, H, PACK], BF16),
-        ]
-        last_raw = [placed("last_raw%d" % b, [P, PACK, H // 2], F32, W1_LAST_AT + b * WINDOW // 2) for b in range(2)]
-        last_bf16 = [placed("last_bf16_%d" % b, [P, H // 2, PACK], BF16, W1_BF16_AT + b * PACK * H) for b in range(2)]
+        w1_raw = [sbuf("w1_raw0", [P, PACK, H], F32), placed("w1_raw1", [P, PACK, H], F32, W1_MID_AT)]
+        w1_bf16 = [sbuf("w1_bf16_%d" % a, [P, H, PACK], BF16) for a in range(LAST)]
+        last_raw = [placed("last_raw%d" % b, [P, PACK, W1_HALF], F32, W1_LAST_AT + b * WINDOW // 2) for b in range(2)]
+        last_bf16 = [placed("last_bf16_%d" % b, [P, W1_HALF, PACK], BF16, W1_BF16_AT + b * HALF_BF16) for b in range(2)]
         w1_codes = [sbuf("w1_codes%d" % a, [P, H], U32) for a in range(PASSES)]
         w1_plane = [sbuf("w1_plane%d" % a, [P, H], U8) for a in range(PASSES)]
         w4_codes = sbuf("w4_codes", [P, PASSES, 2 * H], U8)
         w4_plane = sbuf("w4_plane", [P, PASSES, H], U8)
         v_rows = sbuf("v_rows", [P, S], U8)
-        v_plane_first = sbuf("v_plane_first", [P, S], U8)
-        v_plane_rest = placed("v_plane_rest", [P, LAST, S], U8, TAB_SCALES_AT)
-        v_plane = [v_plane_first[:], v_plane_rest[:, 0, :], v_plane_rest[:, 1, :]]
+        v_plane_last = sbuf("v_plane_last", [P, S], U8)
+        v_plane_pair = placed("v_plane_pair", [P, LAST, S], U8, TAB_SCALES_AT)
+        v_plane = [v_plane_pair[:, 0, :], v_plane_pair[:, 1, :], v_plane_last[:]]
         v2_rows = sbuf("v2_rows", [P, S2], U8)
-        v2_plane = placed("v2_plane", [P, S2], U8, TAB2_SCALES_AT + S2)
+        v2_plane = placed("v2_plane", [P, S2], U8, TAB2_PLANE_AT)
         alpha_rows = sbuf("alpha_rows", [P, P], F32)
         alpha_cols = sbuf("alpha_cols", [P, ROW_TILES], F32)
         h_codes = [sbuf("h_codes%d" % half, [P, HALF], U32) for half in range(2)]
@@ -116,24 +114,24 @@ def tile_list_poly_kernel_contributions_kernel(
         nc.vector.memset(tab_scale_window[:].bitcast(I32), 0)
         nc.vector.memset(tab2_scale_window[:].bitcast(I32), 0)
         nc.vector.memset(w4_plane[:].rearrange("p a c -> p (a c)").bitcast(I32), 0)
-        nc.vector.memset(v_plane_first[:].bitcast(I32), 0)
+        nc.vector.memset(v_plane_last[:].bitcast(I32), 0)
         nc.vector.memset(alpha_rows[:], 0.0)
 
         def load_words(words, tile):
             nc.sync.dma_start(out=tile[:].bitcast(I32), in_=words.rearrange("p t i -> p (t i)").bitcast(I32))
 
-        def load_w1(a):
-            rows = w1[K_PASS * a : K_PASS * (a + 1), :]
-            nc.sync.dma_start(out=w1_raw[a][:], in_=rows.rearrange("(p t) c -> p t c", t=PACK))
+        def load_w1(a, tile, columns):
+            rows = w1[K_PASS * a : K_PASS * (a + 1), :].rearrange("(p t) c -> p t c", t=PACK)
+            nc.sync.dma_start(out=tile[:], in_=rows[:, :, columns])
 
         nc.sync.dma_start(out=w4_codes[:].bitcast(I32), in_=w4_words.bitcast(I32).rearrange("a p c -> p a c"))
         nc.sync.dma_start(idx[:], offs)
         nc.sync.dma_start(
             out=tab_scale_window[0 : P : ROWS_STEP // 2, :].bitcast(I32),
-            in_=tab_scales[1:PASSES].bitcast(I32).rearrange("a q t -> q a t"),
+            in_=tab_scales[0:LAST].bitcast(I32).rearrange("a q t -> q a t"),
         )
         nc.sync.dma_start(
-            out=tab_scale_window[TAB_ROWS_AT[0] : P : ROWS_STEP, :].bitcast(I32), in_=tab_scales[0].bitcast(I32)
+            out=tab_scale_window[TAB_LAST_ROWS_AT:P:ROWS_STEP, :].bitcast(I32), in_=tab_scales[LAST].bitcast(I32)
         )
         load_words(tab_words[0], tab_window[0])
         nc.sync.dma_start(idx2[:], offs2)
@@ -161,25 +159,29 @@ def tile_list_poly_kernel_contributions_kernel(
                     in_=rows[rows_first + ROWS_STEP * s : P : QUADRANT, :].bitcast(I32),
                 )
 
+        def move_pair_rows():
+            for q in (0, 2, 1, 3):
+                first = QUADRANT * q
+                nc.sync.dma_start(
+                    out=v_plane_pair[first : first + 4, :, :].bitcast(I32),
+                    in_=v_rows[first : first + QUADRANT : ROWS_STEP // 2, :].bitcast(I32),
+                )
+
         def gather_tab2(b, offset):
             v2_codes[b] = placed("v2_codes%d" % b, [P, HALF], U32, offset)
             nc.vector.tensor_copy(out=v2_codes[b][:], in_=tab2_window[:].indirect(entries(idx2, b * HALF, HALF)))
 
-        def interleave_w1(a, copy, columns):
+        def interleave(copy, raw, grouped):
             copy(
-                out=w1_bf16[a][:, columns, :].rearrange("p (c i) t -> p c t i", i=4),
-                in_=w1_raw[a][:, :, columns].rearrange("p t (c i) -> p c t i", i=4),
+                out=grouped[:].rearrange("p (c i) t -> p c t i", i=4),
+                in_=raw[:].rearrange("p t (c i) -> p c t i", i=4),
             )
 
-        def interleave_shared(a, split):
-            interleave_w1(a, nc.vector.tensor_copy, slice(0, split))
-            interleave_w1(a, nc.scalar.copy, slice(split, H))
-
-        def quantise_w1(a):
+        def quantise_w1(a, grouped, columns):
             nc.vector.quantize_mx(
-                out=w1_codes[a][:].bitcast(FP8X4),
-                scales=w1_plane[a][:],
-                in_=w1_bf16[a][:].rearrange("p c t -> p (c t)"),
+                out=w1_codes[a][:, columns].bitcast(FP8X4),
+                scales=w1_plane[a][:, columns],
+                in_=grouped[:].rearrange("p c t -> p (c t)"),
             )
 
         def project(bank, c, a, codes, plane, step):
@@ -214,7 +216,7 @@ def tile_list_poly_kernel_contributions_kernel(
                 return SIG_EARLY_AT + c * SIG_BYTES
             if c < CHUNKS - 1:
                 return W1_LAST_AT + (c - EARLY) * SIG_BYTES
-            return W1_BF16_AT + PACK * H
+            return W1_BF16_AT + HALF_BF16
 
         def sigmoid(c):
             sig[c] = placed("sig%d" % c, [P, H], F32, sig_at(c))
@@ -255,8 +257,8 @@ def tile_list_poly_kernel_contributions_kernel(
             half, i = divmod(n, ROW_TILES)
             b, o = divmod(i, PER_HALF)
             bank = banks[Y_BANK[n]]
-            if n < 2:
-                squared[n] = placed("squared%d" % n, [P, HALF], F32, SQUARED_AT + n * 4 * HALF)
+            if n < HELD:
+                squared[n] = placed("squared%d" % n, [P, HALF], F32, SQUARED_AT + n * BLOCK_BYTES)
             else:
                 squared[n] = sbuf("squared%d" % n, [P, HALF], F32)
             result[n] = sbuf("result%d" % n, [P, HALF], F32)
@@ -280,30 +282,28 @@ def tile_list_poly_kernel_contributions_kernel(
 
         turned_shape = [P, 2 * P, PACK]
 
+        whole = slice(0, H)
+        halves = [slice(0, W1_HALF), slice(W1_HALF, H)]
+
         nc.vector.tensor_copy(out=v_rows[:], in_=tab_scale_window[:].indirect(idx[:]))
-        move_rows(v_plane_first, 0, v_rows, TAB_ROWS_AT[0])
-        nc.sync.dma_start(out=alpha_rows[0:ROW_TILES, :], in_=alpha.rearrange("(n p) -> n p", p=P))
-        load_w1(0)
-        for q in (0, 2, 1, 3):
-            first = QUADRANT * q
-            nc.sync.dma_start(
-                out=v_plane_rest[first : first + 4, :, :].bitcast(I32),
-                in_=v_rows[first : first + QUADRANT : ROWS_STEP // 2, :].bitcast(I32),
-            )
+        move_pair_rows()
+        load_w1(0, w1_raw[0], whole)
         load_words(tab_words[LAST], tab_window[LAST])
-        load_w1(1)
-        last_rows = w1[K_PASS * LAST : K, :].rearrange("(p t) c -> p t c", t=PACK)
+        nc.sync.dma_start(out=alpha_rows[0:ROW_TILES, :], in_=alpha.rearrange("(n p) -> n p", p=P))
+        move_rows(v_plane_last, 0, v_rows, TAB_LAST_ROWS_AT)
+        load_w1(1, w1_raw[1], whole)
         for b in range(2):
-            nc.sync.dma_start(out=last_raw[b][:], in_=last_rows[:, :, b * H // 2 : (b + 1) * H // 2])
+            load_w1(LAST, last_raw[b], halves[b])
         gather_tab(0, 0, sbuf("v_codes0", [P, S], U32))
         nc.vector.tensor_copy(out=v2_rows[:], in_=tab2_scale_window[:].indirect(idx2[:]))
-        gather_tab(1, 0, sbuf("v_codes1", [P, S], U32))
+        for half in range(2):
+            gather_tab(1, half * PER_HALF, sbuf("v_codes1_%d" % half, [P, HALF], U32))
         load_words(tab2_words[0], tab2_window)
         ident = placed("ident", [P, P], F32, TAB2_SCALES_AT)
         make_identity(nc, ident[:])
-        move_rows(v2_plane[:], TAB2_PLANE, v2_rows, TAB2_ROWS_AT)
-        interleave_w1(0, nc.scalar.copy, slice(0, H))
-        quantise_w1(0)
+        move_rows(v2_plane, TAB2_PLANE, v2_rows, TAB2_ROWS_AT)
+        interleave(nc.scalar.copy, w1_raw[0], w1_bf16[0])
+        quantise_w1(0, w1_bf16[0], whole)
         for pair in range(PAIRS):
             gather_tab(LAST, 2 * pair, sbuf("v_codes2_%d" % pair, [P, 2 * P], U32))
 
@@ -312,20 +312,12 @@ def tile_list_poly_kernel_contributions_kernel(
                 g_pass(c, a)
         for c in range(EARLY):
             sigmoid(c)
-        interleave_w1(1, nc.vector.tensor_copy, slice(0, H))
-        quantise_w1(1)
-        for b, copy in enumerate((nc.scalar.copy, nc.vector.tensor_copy)):
-            copy(
-                out=last_bf16[b][:].rearrange("p (c i) t -> p c t i", i=4),
-                in_=last_raw[b][:].rearrange("p t (c i) -> p c t i", i=4),
-            )
+        interleave(nc.vector.tensor_copy, w1_raw[1], w1_bf16[1])
+        quantise_w1(1, w1_bf16[1], whole)
+        interleave(nc.scalar.copy, last_raw[0], last_bf16[0])
+        interleave(nc.vector.tensor_copy, last_raw[1], last_bf16[1])
         for b in range(2):
-            columns = slice(b * H // 2, (b + 1) * H // 2)
-            nc.vector.quantize_mx(
-                out=w1_codes[LAST][:, columns].bitcast(FP8X4),
-                scales=w1_plane[LAST][:, columns],
-                in_=last_bf16[b][:].rearrange("p c t -> p (c t)"),
-            )
+            quantise_w1(LAST, last_bf16[b], halves[b])
         for c in range(EARLY, CHUNKS):
             sigmoid(c)
 

@@ -16,6 +16,7 @@ FP8X4 = mybir.dt.float8_e4m3fn_x4
 FP4X4 = mybir.dt.float4_e2m1fn_x4
 ACT = mybir.ActivationFunctionType
 MULT = mybir.AluOpType.mult
+ADD = mybir.AluOpType.add
 
 P = 128
 PACK = 4
@@ -39,9 +40,9 @@ W1_HALF = H // 2
 EARLY = 3
 
 A_BANK = [0, 1, 2, 3, 4, 3, 0, 2]
-Y_FIRST = [1, 5, 6, 7, 1, 2, 1, 0]
-Y_BANK = Y_FIRST + [3, 4, 5, 6, 7] + Y_FIRST[5:]
-TURN_BANK = [A_BANK[0], A_BANK[2], Y_BANK[1], A_BANK[6]]
+Y_FIRST = [1, 5, 6, 7]
+Y_BANK = Y_FIRST + Y_FIRST + [0, 2, 4, 3] + Y_FIRST
+TURN_BANK = [A_BANK[0], A_BANK[2], A_BANK[4], A_BANK[5]]
 
 LAP = 64
 WINDOW = 4 * T
@@ -60,9 +61,13 @@ V2_SECOND_AT = TURNED_AT + 2 * CHUNK_BYTES - LAP
 W1_BF16_AT = V2_SECOND_AT + BLOCK_BYTES
 HALF_BF16 = 2 * PACK * W1_HALF
 SIG_EARLY_AT = W1_BF16_AT + 2 * HALF_BF16
-SQUARED_AT = SIG_EARLY_AT + EARLY * SIG_BYTES
-HELD = 2
-H_CHUNK_AT = {5: TURNED_AT - CHUNK_BYTES + LAP, 6: SQUARED_AT, 7: SQUARED_AT + BLOCK_BYTES}
+H_CHUNK_AT = {
+    4: TURNED_AT - CHUNK_BYTES + LAP,
+    5: TURNED_AT + LAP,
+    6: W1_LAST_AT + (4 - EARLY) * SIG_BYTES,
+    7: W1_LAST_AT + (5 - EARLY) * SIG_BYTES,
+}
+ON_GPSIMD = (0, 1, 2, 4)
 
 
 def tile_list_poly_kernel_contributions_kernel(
@@ -116,6 +121,9 @@ def tile_list_poly_kernel_contributions_kernel(
         nc.vector.memset(w4_plane[:].rearrange("p a c -> p (a c)").bitcast(I32), 0)
         nc.vector.memset(v_plane_last[:].bitcast(I32), 0)
         nc.vector.memset(alpha_rows[:], 0.0)
+        ident = sbuf("ident", [P, P], F32)
+        nc.vector.memset(ident[:], 0.0)
+        make_identity(nc, ident[:], nomemset=True)
 
         def load_words(words, tile):
             nc.sync.dma_start(out=tile[:].bitcast(I32), in_=words.rearrange("p t i -> p (t i)").bitcast(I32))
@@ -231,7 +239,7 @@ def tile_list_poly_kernel_contributions_kernel(
                 out=as_stored(h_chunk[c]), in0=in_word_order(banks[A_BANK[c]]), in1=as_stored(sig[c]), op=MULT
             )
 
-        def turn(pair, tile):
+        def turn(pair, tile, copy):
             h_turned[pair] = tile
             bank = banks[TURN_BANK[pair]]
             for second in (1, 0):
@@ -240,9 +248,7 @@ def tile_list_poly_kernel_contributions_kernel(
                     o = (2 * u + second) * P
                     nc.tensor.transpose(bank[:, o : o + P], words[:, u * P : (u + 1) * P], ident[:])
             samples = tile[:].rearrange("p j t -> p (j t)").bitcast(F32)
-            nc.scalar.copy(
-                out=samples.rearrange("p (j u) -> p j u", u=2), in_=bank[:].rearrange("p (u j) -> p j u", u=2)
-            )
+            copy(out=samples.rearrange("p (j u) -> p j u", u=2), in_=bank[:].rearrange("p (u j) -> p j u", u=2))
 
         def quantise_h(pair):
             half, o = divmod(pair, 2)
@@ -257,10 +263,7 @@ def tile_list_poly_kernel_contributions_kernel(
             half, i = divmod(n, ROW_TILES)
             b, o = divmod(i, PER_HALF)
             bank = banks[Y_BANK[n]]
-            if n < HELD:
-                squared[n] = placed("squared%d" % n, [P, HALF], F32, SQUARED_AT + n * BLOCK_BYTES)
-            else:
-                squared[n] = sbuf("squared%d" % n, [P, HALF], F32)
+            squared[n] = sbuf("squared%d" % n, [P, HALF], F32)
             result[n] = sbuf("result%d" % n, [P, HALF], F32)
             nc.tensor.matmul_mx(
                 out=bank[:],
@@ -275,9 +278,14 @@ def tile_list_poly_kernel_contributions_kernel(
 
         def store(n):
             half, i = divmod(n, ROW_TILES)
-            nc.vector.tensor_scalar(
-                out=result[n][:], in0=squared[n][:], scalar1=alpha_cols[:, i : i + 1], scalar2=None, op0=MULT
-            )
+            if n in ON_GPSIMD:
+                nc.gpsimd.tensor_scalar(
+                    out=result[n][:], in0=squared[n][:], scalar1=alpha_cols[:, i : i + 1], scalar2=0.0, op0=MULT, op1=ADD
+                )
+            else:
+                nc.vector.tensor_scalar(
+                    out=result[n][:], in0=squared[n][:], scalar1=alpha_cols[:, i : i + 1], scalar2=None, op0=MULT
+                )
             nc.sync.dma_start(out=out[i * P : (i + 1) * P, half * HALF : (half + 1) * HALF], in_=result[n][:])
 
         turned_shape = [P, 2 * P, PACK]
@@ -299,8 +307,6 @@ def tile_list_poly_kernel_contributions_kernel(
         for half in range(2):
             gather_tab(1, half * PER_HALF, sbuf("v_codes1_%d" % half, [P, HALF], U32))
         load_words(tab2_words[0], tab2_window)
-        ident = placed("ident", [P, P], F32, TAB2_SCALES_AT)
-        make_identity(nc, ident[:])
         move_rows(v2_plane, TAB2_PLANE, v2_rows, TAB2_ROWS_AT)
         interleave(nc.scalar.copy, w1_raw[0], w1_bf16[0])
         quantise_w1(0, w1_bf16[0], whole)
@@ -327,13 +333,13 @@ def tile_list_poly_kernel_contributions_kernel(
         for c in range(EARLY):
             a_pass(c, LAST, LAST)
             gate(c)
-        for c in range(EARLY, PER_HALF + 1):
-            late_a(c)
-            gate(c)
-        turn(0, sbuf("h_turned0", turned_shape, BF16))
+        late_a(EARLY)
+        gate(EARLY)
+        late_a(PER_HALF)
+        turn(0, sbuf("h_turned0", turned_shape, BF16), nc.scalar.copy)
         nc.tensor.transpose(banks[Y_BANK[0]][:, 0:P], alpha_rows[:], ident[:])
         nc.scalar.copy(out=alpha_cols[:], in_=banks[Y_BANK[0]][:, 0:ROW_TILES])
-        turn(1, placed("h_turned1", turned_shape, BF16, TURNED_AT))
+        turn(1, placed("h_turned1", turned_shape, BF16, TURNED_AT), nc.scalar.copy)
         gather_tab2(0, sig_at(PER_HALF - 1))
         quantise_h(0)
         quantise_h(1)
@@ -343,22 +349,17 @@ def tile_list_poly_kernel_contributions_kernel(
             square(n)
         square(3)
         gather_tab2(1, V2_SECOND_AT)
-        gate(5)
-        turn(2, sbuf("h_turned2", turned_shape, BF16))
-        store(0)
-        gate(6)
-        store(1)
-        gate(7)
-        square(4)
-        turn(3, sbuf("h_turned3", turned_shape, BF16))
-        for n in range(5, ROW_TILES):
+        for c in range(PER_HALF, CHUNKS):
+            gate(c)
+        turn(2, sbuf("h_turned2", turned_shape, BF16), nc.scalar.copy)
+        for n in range(PER_HALF, ROW_TILES):
             square(n)
-        store(2)
-        store(3)
+        for n in range(PER_HALF):
+            store(n)
+        turn(3, sbuf("h_turned3", turned_shape, BF16), nc.vector.tensor_copy)
         quantise_h(2)
-        store(4)
         quantise_h(3)
-        for n in range(5, ROW_TILES):
+        for n in range(PER_HALF, ROW_TILES):
             store(n)
         for n in range(ROW_TILES, BLOCKS):
             square(n)

@@ -39,10 +39,10 @@ TAB2_PLANE = 12
 W1_HALF = H // 2
 EARLY = 3
 
-A_BANK = [0, 1, 2, 3, 4, 3, 0, 2]
-Y_FIRST = [1, 5, 6, 7]
-Y_BANK = Y_FIRST + Y_FIRST + [0, 2, 4, 3] + Y_FIRST
-TURN_BANK = [A_BANK[0], A_BANK[2], A_BANK[4], A_BANK[5]]
+A_BANK = [0, 1, 2, 3, 4, 1, 3, 4]
+Y_FIRST = [5, 6, 7, 0]
+Y_BANK = Y_FIRST + [7, 0, 3, 4] + [1, 2, 5, 7, 0, 6, 3, 4]
+TURN_BANK = [A_BANK[0], A_BANK[2], Y_BANK[0], Y_BANK[1]]
 
 LAP = 64
 WINDOW = 4 * T
@@ -64,10 +64,16 @@ SIG_EARLY_AT = W1_BF16_AT + 2 * HALF_BF16
 H_CHUNK_AT = {
     4: TURNED_AT - CHUNK_BYTES + LAP,
     5: TURNED_AT + LAP,
-    6: W1_LAST_AT + (4 - EARLY) * SIG_BYTES,
-    7: W1_LAST_AT + (5 - EARLY) * SIG_BYTES,
+    6: TAB2_AT + LAP,
+    7: TAB2_AT + LAP + BLOCK_BYTES,
 }
-ON_GPSIMD = (0, 1, 2, 4)
+ON_GPSIMD = (0, 1, 2, 3, 4, 5)
+LAST_TURNED_AT = SIG_EARLY_AT + EARLY * SIG_BYTES + BLOCK_BYTES
+V2_ROWS_AT = LAST_TURNED_AT + 2 * BLOCK_BYTES
+RESULT_AT = {
+    6: LAST_TURNED_AT - BLOCK_BYTES + LAP,
+    7: LAST_TURNED_AT + 2 * CHUNK_BYTES - LAP,
+}
 
 
 def tile_list_poly_kernel_contributions_kernel(
@@ -107,12 +113,12 @@ def tile_list_poly_kernel_contributions_kernel(
         v_plane_last = sbuf("v_plane_last", [P, S], U8)
         v_plane_pair = placed("v_plane_pair", [P, LAST, S], U8, TAB_SCALES_AT)
         v_plane = [v_plane_pair[:, 0, :], v_plane_pair[:, 1, :], v_plane_last[:]]
-        v2_rows = sbuf("v2_rows", [P, S2], U8)
+        v2_rows = placed("v2_rows", [P, S2], U8, V2_ROWS_AT)
         v2_plane = placed("v2_plane", [P, S2], U8, TAB2_PLANE_AT)
         alpha_rows = sbuf("alpha_rows", [P, P], F32)
         alpha_cols = sbuf("alpha_cols", [P, ROW_TILES], F32)
         h_codes = [sbuf("h_codes%d" % half, [P, HALF], U32) for half in range(2)]
-        h_plane = [sbuf("h_plane%d" % half, [P, HALF], U8) for half in range(2)]
+        h_plane = [placed("h_plane0", [P, HALF], U8, V2_ROWS_AT), sbuf("h_plane1", [P, HALF], U8)]
         banks = [psum.tile([P, BANK], F32, name="bank%d" % b) for b in range(8)]
         v_codes, v2_codes, sig, h_chunk, h_turned, squared, result = {}, {}, {}, {}, {}, {}, {}
 
@@ -264,7 +270,10 @@ def tile_list_poly_kernel_contributions_kernel(
             b, o = divmod(i, PER_HALF)
             bank = banks[Y_BANK[n]]
             squared[n] = sbuf("squared%d" % n, [P, HALF], F32)
-            result[n] = sbuf("result%d" % n, [P, HALF], F32)
+            if n in RESULT_AT:
+                result[n] = placed("result%d" % n, [P, HALF], F32, RESULT_AT[n])
+            else:
+                result[n] = sbuf("result%d" % n, [P, HALF], F32)
             nc.tensor.matmul_mx(
                 out=bank[:],
                 lhsT=v2_codes[b][:, o * P : (o + 1) * P].bitcast(FP8X4),
@@ -330,36 +339,41 @@ def tile_list_poly_kernel_contributions_kernel(
         for a in range(LAST):
             for c in range(EARLY):
                 a_pass(c, a, a)
-        for c in range(EARLY):
+        for a in range(LAST):
+            a_pass(EARLY, a, a)
+        for c in range(PER_HALF):
             a_pass(c, LAST, LAST)
             gate(c)
-        late_a(EARLY)
-        gate(EARLY)
-        late_a(PER_HALF)
-        turn(0, sbuf("h_turned0", turned_shape, BF16), nc.scalar.copy)
+        late_a(4)
         nc.tensor.transpose(banks[Y_BANK[0]][:, 0:P], alpha_rows[:], ident[:])
         nc.scalar.copy(out=alpha_cols[:], in_=banks[Y_BANK[0]][:, 0:ROW_TILES])
+        turn(0, sbuf("h_turned0", turned_shape, BF16), nc.scalar.copy)
+        a_pass(5, LAST, 0)
         turn(1, placed("h_turned1", turned_shape, BF16, TURNED_AT), nc.scalar.copy)
+        a_pass(5, 0, 1)
+        a_pass(5, 1, 2)
+        late_a(6)
         gather_tab2(0, sig_at(PER_HALF - 1))
         quantise_h(0)
         quantise_h(1)
 
-        for n in range(PER_HALF - 1):
-            late_a(PER_HALF + 1 + n)
-            square(n)
-        square(3)
+        gate(4)
+        gate(5)
         gather_tab2(1, V2_SECOND_AT)
-        for c in range(PER_HALF, CHUNKS):
-            gate(c)
-        turn(2, sbuf("h_turned2", turned_shape, BF16), nc.scalar.copy)
-        for n in range(PER_HALF, ROW_TILES):
-            square(n)
         for n in range(PER_HALF):
-            store(n)
-        turn(3, sbuf("h_turned3", turned_shape, BF16), nc.vector.tensor_copy)
+            square(n)
+        late_a(7)
+        gate(6)
+        gate(7)
+        turn(2, sbuf("h_turned2", turned_shape, BF16), nc.scalar.copy)
+        square(4)
+        square(5)
+        turn(3, placed("h_turned3", turned_shape, BF16, LAST_TURNED_AT), nc.vector.tensor_copy)
+        square(6)
+        square(7)
         quantise_h(2)
         quantise_h(3)
-        for n in range(PER_HALF, ROW_TILES):
+        for n in range(ROW_TILES):
             store(n)
         for n in range(ROW_TILES, BLOCKS):
             square(n)

@@ -44,7 +44,8 @@ Y_FIRST = [5, 6, 7, 0]
 Y_BANK = Y_FIRST + [7, 0, 3, 4] + [1, 2, 5, 7, 0, 6, 3, 4]
 TURN_BANK = [A_BANK[0], A_BANK[2], Y_BANK[0], Y_BANK[1]]
 
-LAP = 64
+ALIGN = 256
+LAP = ALIGN
 WINDOW = 4 * T
 SIG_BYTES = 4 * H
 CHUNK_BYTES = 2 * H
@@ -86,10 +87,10 @@ def tile_list_poly_kernel_contributions_kernel(
         psum = ctx.enter_context(tc.psum_pool(name="psum", bufs=1))
 
         def sbuf(name, shape, dtype):
-            return keep.tile(shape, dtype, name=name, align_bytes=64)
+            return keep.tile(shape, dtype, name=name, align_bytes=ALIGN)
 
         def placed(name, shape, dtype, offset):
-            return shared.tile(shape, dtype, name=name, align_bytes=64, offset=offset)
+            return shared.tile(shape, dtype, name=name, align_bytes=ALIGN, offset=offset)
 
         idx = keep.tile([P, S // LIST_ROWS], U16, name="idx")
         idx2 = keep.tile([P, S2 // LIST_ROWS], U16, name="idx2")

from contextlib import ExitStack

import concourse.mybir as mybir
from concourse.masks import make_identity

K, H, T, S, T2, S2 = 1536, 512, 2048, 1024, 4096, 1024
FLOPS = 2 * (2 * K * H * S + H * S * S2)

F32 = mybir.dt.float32
BF16 = mybir.dt.bfloat16
I32 = mybir.dt.int32
U32 = mybir.dt.uint32
U16 = mybir.dt.uint16
U8 = mybir.dt.uint8
FP8X4 = mybir.dt.float8_e4m3fn_x4
FP4X4 = mybir.dt.float4_e2m1fn_x4
ACT = mybir.ActivationFunctionType
MULT = mybir.AluOpType.mult
ADD = mybir.AluOpType.add

P = 128
PACK = 4
K_PASS = P * PACK
PASSES = K // K_PASS
LAST = PASSES - 1
BANK = 512
HALF = 512
CHUNKS = S // P
PAIRS = CHUNKS // 2
PER_HALF = HALF // P
ROW_TILES = S2 // P
BLOCKS = 2 * ROW_TILES
LIST_ROWS = 16
QUADRANT = 32
ROWS_STEP = 8
TAB_LAST_ROWS_AT = 2
TAB2_ROWS_AT = 4
TAB2_PLANE = 12
W1_HALF = H // 2
EARLY = 3

A_BANK = [0, 1, 2, 3, 4, 1, 3, 4]
Y_FIRST = [5, 6, 7, 0]
Y_BANK = Y_FIRST + [7, 0, 3, 4] + [1, 2, 5, 7, 0, 6, 3, 4]
TURN_BANK = [A_BANK[0], A_BANK[2], Y_BANK[0], Y_BANK[1]]

ALIGN = 256
LAP = ALIGN
WINDOW = 4 * T
SIG_BYTES = 4 * H
CHUNK_BYTES = 2 * H
BLOCK_BYTES = 4 * HALF
TAB2_SCALES_AT = 0
TAB2_PLANE_AT = TAB2_SCALES_AT + S2
W1_MID_AT = TAB2_SCALES_AT + T2
TAB_SCALES_AT = W1_MID_AT + WINDOW
W1_LAST_AT = TAB_SCALES_AT + T
TAB_MID_AT = W1_LAST_AT + WINDOW
TAB2_AT = TAB_MID_AT + WINDOW - LAP
TURNED_AT = TAB2_AT + 4 * T2 + CHUNK_BYTES
V2_SECOND_AT = TURNED_AT + 2 * CHUNK_BYTES - LAP
W1_BF16_AT = V2_SECOND_AT + BLOCK_BYTES
HALF_BF16 = 2 * PACK * W1_HALF
SIG_EARLY_AT = W1_BF16_AT + 2 * HALF_BF16
H_CHUNK_AT = {
    4: TURNED_AT - CHUNK_BYTES + LAP,
    5: TURNED_AT + LAP,
    6: TAB2_AT + LAP,
    7: TAB2_AT + LAP + BLOCK_BYTES,
}
ON_GPSIMD = (0, 1, 2, 3, 4, 5)
LAST_TURNED_AT = SIG_EARLY_AT + EARLY * SIG_BYTES + BLOCK_BYTES
V2_ROWS_AT = LAST_TURNED_AT + 2 * BLOCK_BYTES
RESULT_AT = {
    6: LAST_TURNED_AT - BLOCK_BYTES + LAP,
    7: LAST_TURNED_AT + 2 * CHUNK_BYTES - LAP,
}


def tile_list_poly_kernel_contributions_kernel(
    tc, tab_words, tab_scales, offs, tab2_words, tab2_scales, offs2, w1, w4_words, w4_scales, alpha, out
):
    nc = tc.nc
    with ExitStack() as ctx:
        keep = ctx.enter_context(tc.tile_pool(name="keep", bufs=1))
        shared = ctx.enter_context(tc.tile_pool(name="shared", bufs=1))
        psum = ctx.enter_context(tc.psum_pool(name="psum", bufs=1))

        def sbuf(name, shape, dtype):
            return keep.tile(shape, dtype, name=name, align_bytes=ALIGN)

        def placed(name, shape, dtype, offset):
            return shared.tile(shape, dtype, name=name, align_bytes=ALIGN, offset=offset)

        idx = keep.tile([P, S // LIST_ROWS], U16, name="idx")
        idx2 = keep.tile([P, S2 // LIST_ROWS], U16, name="idx2")
        tab2_scale_window = placed("tab2_scale_window", [P, T2], U8, TAB2_SCALES_AT)
        tab_scale_window = placed("tab_scale_window", [P, T], U8, TAB_SCALES_AT)
        tab_window = [
            sbuf("tab_window0", [P, T], U32),
            placed("tab_window1", [P, T], U32, TAB_MID_AT),
            sbuf("tab_window2", [P, T], U32),
        ]
        tab2_window = placed("tab2_window", [P, T2], U32, TAB2_AT)
        w1_raw = [sbuf("w1_raw0", [P, PACK, H], F32), placed("w1_raw1", [P, PACK, H], F32, W1_MID_AT)]
        w1_bf16 = [sbuf("w1_bf16_%d" % a, [P, H, PACK], BF16) for a in range(LAST)]
        last_raw = [placed("last_raw%d" % b, [P, PACK, W1_HALF], F32, W1_LAST_AT + b * WINDOW // 2) for b in range(2)]
        last_bf16 = [placed("last_bf16_%d" % b, [P, W1_HALF, PACK], BF16, W1_BF16_AT + b * HALF_BF16) for b in range(2)]
        w1_codes = [sbuf("w1_codes%d" % a, [P, H], U32) for a in range(PASSES)]
        w1_plane = [sbuf("w1_plane%d" % a, [P, H], U8) for a in range(PASSES)]
        w4_codes = sbuf("w4_codes", [P, PASSES, 2 * H], U8)
        w4_plane = sbuf("w4_plane", [P, PASSES, H], U8)
        v_rows = sbuf("v_rows", [P, S], U8)
        v_plane_last = sbuf("v_plane_last", [P, S], U8)
        v_plane_pair = placed("v_plane_pair", [P, LAST, S], U8, TAB_SCALES_AT)
        v_plane = [v_plane_pair[:, 0, :], v_plane_pair[:, 1, :], v_plane_last[:]]
        v2_rows = placed("v2_rows", [P, S2], U8, V2_ROWS_AT)
        v2_plane = placed("v2_plane", [P, S2], U8, TAB2_PLANE_AT)
        alpha_rows = sbuf("alpha_rows", [P, P], F32)
        alpha_cols = sbuf("alpha_cols", [P, ROW_TILES], F32)
        h_codes = [sbuf("h_codes%d" % half, [P, HALF], U32) for half in range(2)]
        h_plane = [placed("h_plane0", [P, HALF], U8, V2_ROWS_AT), sbuf("h_plane1", [P, HALF], U8)]
        banks = [psum.tile([P, BANK], F32, name="bank%d" % b) for b in range(8)]
        v_codes, v2_codes, sig, h_chunk, h_turned, squared, result = {}, {}, {}, {}, {}, {}, {}

        nc.vector.memset(tab_scale_window[:].bitcast(I32), 0)
        nc.vector.memset(tab2_scale_window[:].bitcast(I32), 0)
        nc.vector.memset(w4_plane[:].rearrange("p a c -> p (a c)").bitcast(I32), 0)
        nc.vector.memset(v_plane_last[:].bitcast(I32), 0)
        nc.vector.memset(alpha_rows[:], 0.0)
        ident = sbuf("ident", [P, P], F32)
        nc.vector.memset(ident[:], 0.0)
        make_identity(nc, ident[:], nomemset=True)

        def load_words(words, tile):
            nc.sync.dma_start(out=tile[:].bitcast(I32), in_=words.rearrange("p t i -> p (t i)").bitcast(I32))

        def load_w1(a, tile, columns):
            rows = w1[K_PASS * a : K_PASS * (a + 1), :].rearrange("(p t) c -> p t c", t=PACK)
            nc.sync.dma_start(out=tile[:], in_=rows[:, :, columns])

        nc.sync.dma_start(out=w4_codes[:].bitcast(I32), in_=w4_words.bitcast(I32).rearrange("a p c -> p a c"))
        nc.sync.dma_start(idx[:], offs)
        nc.sync.dma_start(
            out=tab_scale_window[0 : P : ROWS_STEP // 2, :].bitcast(I32),
            in_=tab_scales[0:LAST].bitcast(I32).rearrange("a q t -> q a t"),
        )
        nc.sync.dma_start(
            out=tab_scale_window[TAB_LAST_ROWS_AT:P:ROWS_STEP, :].bitcast(I32), in_=tab_scales[LAST].bitcast(I32)
        )
        load_words(tab_words[0], tab_window[0])
        nc.sync.dma_start(idx2[:], offs2)
        nc.sync.dma_start(
            out=tab2_scale_window[TAB2_ROWS_AT:P:ROWS_STEP, :].bitcast(I32), in_=tab2_scales[0].bitcast(I32)
        )
        w4_rows = w4_scales.bitcast(I32).rearrange("a (q s) c -> s q a c", s=4)
        for s in range(4):
            nc.sync.dma_start(out=w4_plane[s:P:QUADRANT, :, :].bitcast(I32), in_=w4_rows[s])
        load_words(tab_words[1], tab_window[1])

        def entries(offsets, first, count):
            return offsets[:, first // LIST_ROWS : (first + count) // LIST_ROWS]

        def gather_tab(a, first, tile):
            count = tile[:].shape[1]
            nc.vector.tensor_copy(out=tile[:], in_=tab_window[a][:].indirect(entries(idx, first * P, count)))
            for o in range(count // P):
                v_codes[a, first + o] = tile[:, o * P : (o + 1) * P]

        def move_rows(plane, plane_first, rows, rows_first):
            for s in range(4):
                nc.sync.dma_start(
                    out=plane[plane_first + s : P : QUADRANT, :].bitcast(I32),
                    in_=rows[rows_first + ROWS_STEP * s : P : QUADRANT, :].bitcast(I32),
                )

        def move_pair_rows():
            for q in (0, 2, 1, 3):
                first = QUADRANT * q
                nc.sync.dma_start(
                    out=v_plane_pair[first : first + 4, :, :].bitcast(I32),
                    in_=v_rows[first : first + QUADRANT : ROWS_STEP // 2, :].bitcast(I32),
                )

        def gather_tab2(b, offset):
            v2_codes[b] = placed("v2_codes%d" % b, [P, HALF], U32, offset)
            nc.vector.tensor_copy(out=v2_codes[b][:], in_=tab2_window[:].indirect(entries(idx2, b * HALF, HALF)))

        def interleave(copy, raw, grouped):
            copy(
                out=grouped[:].rearrange("p (c i) t -> p c t i", i=4),
                in_=raw[:].rearrange("p t (c i) -> p c t i", i=4),
            )

        def quantise_w1(a, grouped, columns):
            nc.vector.quantize_mx(
                out=w1_codes[a][:, columns].bitcast(FP8X4),
                scales=w1_plane[a][:, columns],
                in_=grouped[:].rearrange("p c t -> p (c t)"),
            )

        def project(bank, c, a, codes, plane, step):
            nc.tensor.matmul_mx(
                out=bank[:],
                lhsT=v_codes[a, c].bitcast(FP8X4),
                lhsT_scale=v_plane[a][:, c * P : (c + 1) * P],
                rhs=codes,
                rhs_scale=plane,
                start=(step == 0),
                stop=(step == LAST),
            )

        def g_pass(c, a):
            project(banks[c], c, a, w4_codes[:, a, :].bitcast(FP4X4), w4_plane[:, a, :], a)

        def a_pass(c, a, step):
            project(banks[A_BANK[c]], c, a, w1_codes[a][:].bitcast(FP8X4), w1_plane[a][:], step)

        def late_a(c):
            for step in range(PASSES):
                a_pass(c, (LAST + step) % PASSES, step)

        def in_word_order(bank):
            return bank[:].rearrange("j (p u e) -> j u p e", u=2, e=2)

        def as_stored(tile):
            return tile[:].rearrange("j (u p e) -> j u p e", u=2, e=2)

        def sig_at(c):
            if c < EARLY:
                return SIG_EARLY_AT + c * SIG_BYTES
            if c < CHUNKS - 1:
                return W1_LAST_AT + (c - EARLY) * SIG_BYTES
            return W1_BF16_AT + HALF_BF16

        def sigmoid(c):
            sig[c] = placed("sig%d" % c, [P, H], F32, sig_at(c))
            nc.scalar.activation(out=as_stored(sig[c]), in_=in_word_order(banks[c]), func=ACT.Sigmoid)

        def gate(c):
            if c in H_CHUNK_AT:
                h_chunk[c] = placed("h_chunk%d" % c, [P, H], BF16, H_CHUNK_AT[c])
            else:
                h_chunk[c] = sbuf("h_chunk%d" % c, [P, H], BF16)
            nc.vector.tensor_tensor(
                out=as_stored(h_chunk[c]), in0=in_word_order(banks[A_BANK[c]]), in1=as_stored(sig[c]), op=MULT
            )

        def turn(pair, tile, copy):
            h_turned[pair] = tile
            bank = banks[TURN_BANK[pair]]
            for second in (1, 0):
                words = h_chunk[2 * pair + second][:].bitcast(F32)
                for u in range(2):
                    o = (2 * u + second) * P
                    nc.tensor.transpose(bank[:, o : o + P], words[:, u * P : (u + 1) * P], ident[:])
            samples = tile[:].rearrange("p j t -> p (j t)").bitcast(F32)
            copy(out=samples.rearrange("p (j u) -> p j u", u=2), in_=bank[:].rearrange("p (u j) -> p j u", u=2))

        def quantise_h(pair):
            half, o = divmod(pair, 2)
            columns = slice(o * 2 * P, (o + 1) * 2 * P)
            nc.vector.quantize_mx(
                out=h_codes[half][:, columns].bitcast(FP8X4),
                scales=h_plane[half][:, columns],
                in_=h_turned[pair][:].rearrange("p j t -> p (j t)"),
            )

        def square(n):
            half, i = divmod(n, ROW_TILES)
            b, o = divmod(i, PER_HALF)
            bank = banks[Y_BANK[n]]
            squared[n] = sbuf("squared%d" % n, [P, HALF], F32)
            if n in RESULT_AT:
                result[n] = placed("result%d" % n, [P, HALF], F32, RESULT_AT[n])
            else:
                result[n] = sbuf("result%d" % n, [P, HALF], F32)
            nc.tensor.matmul_mx(
                out=bank[:],
                lhsT=v2_codes[b][:, o * P : (o + 1) * P].bitcast(FP8X4),
                lhsT_scale=v2_plane[TAB2_PLANE:P, i * P : (i + 1) * P],
                rhs=h_codes[half][:].bitcast(FP8X4),
                rhs_scale=h_plane[half][:],
                start=True,
                stop=True,
            )
            nc.scalar.activation(out=squared[n][:], in_=bank[:], func=ACT.Square, bias=1.0)

        def store(n):
            half, i = divmod(n, ROW_TILES)
            if n in ON_GPSIMD:
                nc.gpsimd.tensor_scalar(
                    out=result[n][:], in0=squared[n][:], scalar1=alpha_cols[:, i : i + 1], scalar2=0.0, op0=MULT, op1=ADD
                )
            else:
                nc.vector.tensor_scalar(
                    out=result[n][:], in0=squared[n][:], scalar1=alpha_cols[:, i : i + 1], scalar2=None, op0=MULT
                )
            nc.sync.dma_start(out=out[i * P : (i + 1) * P, half * HALF : (half + 1) * HALF], in_=result[n][:])

        turned_shape = [P, 2 * P, PACK]

        whole = slice(0, H)
        halves = [slice(0, W1_HALF), slice(W1_HALF, H)]

        nc.vector.tensor_copy(out=v_rows[:], in_=tab_scale_window[:].indirect(idx[:]))
        move_pair_rows()
        load_w1(0, w1_raw[0], whole)
        load_words(tab_words[LAST], tab_window[LAST])
        nc.sync.dma_start(out=alpha_rows[0:ROW_TILES, :], in_=alpha.rearrange("(n p) -> n p", p=P))
        move_rows(v_plane_last, 0, v_rows, TAB_LAST_ROWS_AT)
        load_w1(1, w1_raw[1], whole)
        for b in range(2):
            load_w1(LAST, last_raw[b], halves[b])
        gather_tab(0, 0, sbuf("v_codes0", [P, S], U32))
        nc.vector.tensor_copy(out=v2_rows[:], in_=tab2_scale_window[:].indirect(idx2[:]))
        for half in range(2):
            gather_tab(1, half * PER_HALF, sbuf("v_codes1_%d" % half, [P, HALF], U32))
        load_words(tab2_words[0], tab2_window)
        move_rows(v2_plane, TAB2_PLANE, v2_rows, TAB2_ROWS_AT)
        interleave(nc.scalar.copy, w1_raw[0], w1_bf16[0])
        quantise_w1(0, w1_bf16[0], whole)
        for pair in range(PAIRS):
            gather_tab(LAST, 2 * pair, sbuf("v_codes2_%d" % pair, [P, 2 * P], U32))

        for a in range(PASSES):
            for c in range(CHUNKS):
                g_pass(c, a)
        for c in range(EARLY):
            sigmoid(c)
        interleave(nc.vector.tensor_copy, w1_raw[1], w1_bf16[1])
        quantise_w1(1, w1_bf16[1], whole)
        interleave(nc.scalar.copy, last_raw[0], last_bf16[0])
        interleave(nc.vector.tensor_copy, last_raw[1], last_bf16[1])
        for b in range(2):
            quantise_w1(LAST, last_bf16[b], halves[b])
        for c in range(EARLY, CHUNKS):
            sigmoid(c)

        for a in range(LAST):
            for c in range(EARLY):
                a_pass(c, a, a)
        for a in range(LAST):
            a_pass(EARLY, a, a)
        for c in range(PER_HALF):
            a_pass(c, LAST, LAST)
            gate(c)
        late_a(4)
        nc.tensor.transpose(banks[Y_BANK[0]][:, 0:P], alpha_rows[:], ident[:])
        nc.scalar.copy(out=alpha_cols[:], in_=banks[Y_BANK[0]][:, 0:ROW_TILES])
        turn(0, sbuf("h_turned0", turned_shape, BF16), nc.scalar.copy)
        a_pass(5, LAST, 0)
        turn(1, placed("h_turned1", turned_shape, BF16, TURNED_AT), nc.scalar.copy)
        a_pass(5, 0, 1)
        a_pass(5, 1, 2)
        late_a(6)
        gather_tab2(0, sig_at(PER_HALF - 1))
        quantise_h(0)
        quantise_h(1)

        gate(4)
        gate(5)
        gather_tab2(1, V2_SECOND_AT)
        for n in range(PER_HALF):
            square(n)
        late_a(7)
        gate(6)
        gate(7)
        turn(2, sbuf("h_turned2", turned_shape, BF16), nc.scalar.copy)
        square(4)
        square(5)
        turn(3, placed("h_turned3", turned_shape, BF16, LAST_TURNED_AT), nc.vector.tensor_copy)
        square(6)
        square(7)
        quantise_h(2)
        quantise_h(3)
        for n in range(ROW_TILES):
            store(n)
        for n in range(ROW_TILES, BLOCKS):
            square(n)
            store(n)
